import numpy as np
import ml_dtypes


def mxq(x, axis, fmt="e4m3"):
    dtype, down = {"e4m3": (ml_dtypes.float8_e4m3fn, 7), "e5m2": (ml_dtypes.float8_e5m2, 14)}[fmt]
    v = np.moveaxis(np.asarray(x, np.float32).astype(ml_dtypes.bfloat16).astype(np.float64), axis, -1)
    blocks = v.reshape(v.shape[:-1] + (-1, 32))
    amax = np.abs(blocks).max(-1, keepdims=True)
    byte = np.maximum(np.where(amax > 0, np.frexp(amax)[1] - 1 + 127, 0) - down, 1)
    scale = np.exp2(byte - 127.0)
    codes = (blocks / scale).astype(np.float32).astype(dtype).astype(np.float64)
    return np.moveaxis((codes * scale).reshape(v.shape), -1, axis)


WIDE = False


def mx_kscale(k):
    if not WIDE:
        return np.ones(k)
    levels = np.array([10, -10, 5, -5, 0])
    if k % 512:
        return np.exp2(np.random.permutation(np.resize(levels, k // 32))).repeat(32)
    a = np.empty((k // 512, 16))
    for p in range(k // 512):
        a[p, :8] = np.random.permutation(np.resize(levels, 8))
        for g in range(8):
            far = levels[np.abs(levels - a[p, g]) >= 10]
            a[p, g + 8] = far[np.random.randint(len(far))]
    return np.exp2(a.ravel()).repeat(32)


def f64(x):
    return np.asarray(x).astype(np.float64)


def striped(idx):
    return np.tile(idx.reshape(-1, 16).T, (8, 1)).astype(np.uint16)


def unstriped(offs):
    return offs[:16].T.reshape(-1).astype(np.int64)


def pack_weight(w):
    k, n = w.shape
    w = f64(np.asarray(w, np.float32).astype(ml_dtypes.bfloat16)).reshape(k // 32, 32, n)
    amax = np.abs(w).max(1)
    byte = np.clip(np.where(amax > 0, np.frexp(amax)[1] - 1 + 127 - 7, 1), 1, 254)
    scaled = (w * np.exp2(127.0 - byte)[:, None, :]).reshape(k, n).astype(np.float32)
    words = np.ascontiguousarray(scaled.reshape(k // 512, 128, 4, n).transpose(0, 1, 3, 2)).astype(ml_dtypes.float8_e4m3fn).view(np.uint8)
    return words, np.ascontiguousarray(byte.astype(np.uint8).reshape(k // 512, 16, n))


def unpack_weight(words, scales):
    g, p, n, _ = words.shape
    vals = np.ascontiguousarray(words).view(ml_dtypes.float8_e4m3fn).astype(np.float64) * np.repeat(np.exp2(scales.astype(np.float64) - 127.0), 8, axis=1)[..., None]
    return vals.transpose(0, 1, 3, 2).reshape(g * 512, n)


def silu(v):
    return v / (1.0 + np.exp(-np.maximum(v, -700.0)))


K, T, S, H, N = 1536, 1024, 512, 1024, 128


def setup_inputs():
    n = np.random.standard_normal
    s = mx_kscale(K)[:, None]
    u = mx_kscale(H)
    packed = pack_weight(n((K, T)) * s)
    return {
        "x_words": packed[0],
        "x_scales": packed[1],
        "w1": (n((K, H)) / np.sqrt(K) / s).astype(np.float32),
        "w3": (n((K, H)) / np.sqrt(K) / s * u).astype(np.float32),
        "w2": (n((H, N)) / np.sqrt(H) / u[:, None]).astype(np.float32),
        "gate": np.tile(np.random.uniform(0.2, 1.0, S), (N, 1)).astype(np.float32),
        "offs": striped(np.random.permutation(T)[:S]),
    }


def reference(x_words, x_scales, w1, w3, w2, gate, offs):
    idx = unstriped(offs)
    xq = unpack_weight(x_words, x_scales)[:, idx]
    h = silu(mxq(f64(w1), 0, "e4m3").T @ xq) * (mxq(f64(w3), 0, "e4m3").T @ xq)
    y = mxq(f64(w2), 0, "e4m3").T @ mxq(h, 0, "e4m3")
    out = np.zeros((N, T))
    out[:, idx] = f64(gate) * y
    return out

@@ -1,0 +1,203 @@
+from contextlib import ExitStack
+
+import concourse.mybir as mybir
+
+K, T, S, H, N = 1536, 1024, 512, 1024, 128
+FLOPS = 2 * K * H * S * 2 + 2 * H * N * S
+
+F32 = mybir.dt.float32
+BF16 = mybir.dt.bfloat16
+I32 = mybir.dt.int32
+U32 = mybir.dt.uint32
+U16 = mybir.dt.uint16
+U8 = mybir.dt.uint8
+FP8X4 = mybir.dt.float8_e4m3fn_x4
+MULT = mybir.AluOpType.mult
+SILU = mybir.ActivationFunctionType.Silu
+
+P = 128
+PACK = 4
+KP = P * PACK
+PASSES = K // KP
+CHUNKS = H // KP
+QUART = 4
+NQ = S // QUART
+SCALAR_ONLY = (0, 1, 2, 6)
+VECTOR_ONLY = (10,)
+
+
+def tile_picked_depth_glu_silu_sub_p_kernel(tc, x_words, x_scales, w1, w3, w2, gate, offs, out):
+    nc = tc.nc
+    with ExitStack() as ctx:
+        keep = ctx.enter_context(tc.tile_pool(name="keep", bufs=1))
+        stage = ctx.enter_context(tc.tile_pool(name="stage", bufs=4))
+        psum = ctx.enter_context(tc.psum_pool(name="psum", bufs=1))
+
+        offsets = keep.tile([P, S // 16], U16, name="offsets")
+        nc.sync.dma_start(offsets[:], offs)
+
+        warm = keep.tile([P, 8], F32, name="warm")
+        warm_out = keep.tile([P, 8], F32, name="warm_out")
+        xs = keep.tile([P, T], U8, name="xs", align_bytes=64)
+        nc.vector.memset(xs[:].bitcast(I32), 0)
+        nc.vector.memset(warm[:], 0.0)
+        nc.scalar.activation(warm_out[:], warm[:], SILU)
+
+        weights = (w1, w3)
+        pieces = [(c, mat, g) for c in range(CHUNKS) for mat in range(2) for g in range(PASSES)]
+        xw = [keep.tile([P, T], I32, name="xw%d" % g, align_bytes=64) for g in range(PASSES)]
+        raw = {}
+        for i, (c, mat, g) in enumerate(pieces):
+            if i < PASSES:
+                nc.sync.dma_start(out=xw[i][:], in_=x_words[i].rearrange("p n t -> p (n t)").bitcast(I32))
+            rows = weights[mat][g * KP : (g + 1) * KP, :].rearrange("(p j) h -> p j h", j=PACK)
+            parts = 2 if i == len(pieces) - 1 else 1
+            width = KP // parts
+            raw[i] = []
+            for a in range(parts):
+                tl = keep.tile([P, PACK, width], F32, name="raw%d_%d" % (i, a), align_bytes=64)
+                nc.sync.dma_start(out=tl[:], in_=rows[:, :, c * KP + a * width : c * KP + (a + 1) * width])
+                raw[i].append(tl)
+            if i == 0:
+                for q in range(4):
+                    nc.sync.dma_start(out=xs[:].bitcast(I32)[32 * q : 32 * q + 4 * PASSES, :], in_=x_scales[:, 4 * q : 4 * q + 4, :].bitcast(I32))
+        w2_raw = keep.tile([P, CHUNKS, PACK, N], F32, name="w2_raw", align_bytes=64)
+        nc.sync.dma_start(out=w2_raw[:], in_=w2.rearrange("(g p j) n -> p g j n", p=P, j=PACK))
+        gate_sb = keep.tile([P, S], F32, name="gate_sb", align_bytes=64)
+        nc.sync.dma_start(out=gate_sb[:], in_=gate)
+
+        result = keep.tile([P, T], F32, name="result", align_bytes=64)
+        nc.vector.memset(result[:], 0.0)
+
+        xg = [keep.tile([P, S], U32, name="xg%d" % g, align_bytes=64) for g in range(PASSES)]
+        xsg = keep.tile([P, S], U8, name="xsg", align_bytes=64)
+
+        grouped = {}
+        codes = {}
+        scales = {}
+
+        def cast(i):
+            grouped[i] = stage.tile([P, PACK, P, PACK], BF16, name="grouped", align_bytes=64)
+            parts = len(raw[i])
+            mw = P // parts
+            for a, tl in enumerate(raw[i]):
+                src = tl[:].rearrange("p j (m t) -> p m j t", t=PACK)
+                dst = grouped[i][:].rearrange("p t m j -> p m j t")[:, a * mw : (a + 1) * mw]
+                first = nc.vector.tensor_copy if i in VECTOR_ONLY else nc.scalar.copy
+                second = nc.scalar.copy if i in SCALAR_ONLY else nc.vector.tensor_copy
+                first(dst[:, :, :, 0:2], src[:, :, :, 0:2])
+                second(dst[:, :, :, 2:4], src[:, :, :, 2:4])
+
+        def quant(i):
+            codes[i] = keep.tile([P, KP], U32, name="codes%d" % i, align_bytes=64)
+            scales[i] = keep.tile([P, KP], U8, name="scales%d" % i, align_bytes=64)
+            nc.vector.quantize_mx(out=codes[i][:].bitcast(FP8X4), scales=scales[i][:], in_=grouped[i][:].rearrange("p t m j -> p (t m j)"))
+
+        banks = {}
+
+        def multiply(i):
+            c, mat, g = pieces[i]
+            if g == 0:
+                for q in range(QUART):
+                    banks[(c, mat, q)] = psum.tile([P, PACK, NQ], F32, name="acc", tag="bank%d" % (mat * QUART + q))
+            for q in range(QUART):
+                cols = slice(q * NQ, (q + 1) * NQ)
+                for t in range(PACK):
+                    mc = slice(t * P, (t + 1) * P)
+                    nc.tensor.matmul_mx(
+                        out=banks[(c, mat, q)][:, t, :],
+                        lhsT=codes[i][:, mc].bitcast(FP8X4),
+                        lhsT_scale=scales[i][:, mc],
+                        rhs=xg[g][:, cols].bitcast(FP8X4),
+                        rhs_scale=xsg[4 * g : P, cols],
+                        start=(g == 0 and t == 0),
+                        stop=(g == PASSES - 1 and t == PACK - 1),
+                    )
+
+        act = [keep.tile([P, QUART, NQ, PACK], F32, name="act%d" % c, align_bytes=64) for c in range(CHUNKS)]
+        hb = [keep.tile([P, QUART, NQ, PACK], BF16, name="hb%d" % c, align_bytes=64) for c in range(CHUNKS)]
+        hc = [keep.tile([P, S], U32, name="hc%d" % c, align_bytes=64) for c in range(CHUNKS)]
+        hs = [keep.tile([P, S], U8, name="hs%d" % c, align_bytes=64) for c in range(CHUNKS)]
+
+        def silu(c, q):
+            nc.scalar.activation(act[c][:, q], banks[(c, 0, q)][:].rearrange("p t n -> p n t"), SILU)
+
+        def gated(c, q):
+            nc.vector.tensor_tensor(hb[c][:, q], banks[(c, 1, q)][:].rearrange("p t n -> p n t"), act[c][:, q], MULT)
+
+        def quant_h(c, q0, q1):
+            cols = slice(q0 * NQ, q1 * NQ)
+            nc.vector.quantize_mx(out=hc[c][:, cols].bitcast(FP8X4), scales=hs[c][:, cols], in_=hb[c][:, q0:q1].rearrange("p q n t -> p (q n t)"))
+
+        def gather_words(g):
+            nc.vector.tensor_copy(xg[g][:], xw[g][:].bitcast(U32).indirect(offsets[:]))
+
+        gather_words(0)
+        cast(0)
+        nc.vector.tensor_copy(xsg[:], xs[:].indirect(offsets[:]))
+        last = len(pieces) - 1
+        for i in range(len(pieces)):
+            c, mat, g = pieces[i]
+            if i + 1 < PASSES:
+                gather_words(i + 1)
+            quant(i)
+            multiply(i)
+            if i < last:
+                cast(i + 1)
+            if g == PASSES - 1 and mat == 0:
+                for q in range(QUART):
+                    silu(c, q)
+            if g == PASSES - 1 and mat == 1 and i < last:
+                for q in range(QUART):
+                    gated(c, q)
+                quant_h(c, 0, QUART)
+
+        w2_grouped = keep.tile([P, CHUNKS, N, PACK], BF16, name="w2_grouped", align_bytes=64)
+        for g in range(CHUNKS):
+            nc.scalar.copy(
+                w2_grouped[:, g].rearrange("p (c i) j -> p c j i", i=4),
+                w2_raw[:, g].rearrange("p j (c i) -> p c j i", i=4),
+            )
+        w2_codes = keep.tile([P, CHUNKS * N], U32, name="w2_codes", align_bytes=64)
+        w2_scales = keep.tile([P, CHUNKS * N], U8, name="w2_scales", align_bytes=64)
+        y_sb = keep.tile([P, S], F32, name="y_sb", align_bytes=64)
+
+        def down(q):
+            cols = slice(q * NQ, (q + 1) * NQ)
+            y = psum.tile([P, NQ], F32, name="y", tag="bank%d" % q)
+            for g in range(CHUNKS):
+                nc.tensor.matmul_mx(
+                    out=y[:],
+                    lhsT=w2_codes[:, g * N : (g + 1) * N].bitcast(FP8X4),
+                    lhsT_scale=w2_scales[:, g * N : (g + 1) * N],
+                    rhs=hc[g][:, cols].bitcast(FP8X4),
+                    rhs_scale=hs[g][:, cols],
+                    start=(g == 0),
+                    stop=(g == CHUNKS - 1),
+                )
+            nc.scalar.copy(y_sb[:, cols], y[:])
+
+        def scatter(q):
+            cols = slice(q * NQ, (q + 1) * NQ)
+            w = NQ // 16
+            nc.vector.tensor_tensor(result[:].indirect(offsets[:, q * w : (q + 1) * w]), y_sb[:, cols], gate_sb[:, cols], MULT)
+
+        c = CHUNKS - 1
+        gated(c, 0)
+        gated(c, 1)
+        quant_h(c, 0, 1)
+        gated(c, 2)
+        quant_h(c, 1, 2)
+        nc.vector.quantize_mx(out=w2_codes[:].bitcast(FP8X4), scales=w2_scales[:], in_=w2_grouped[:].rearrange("p g n j -> p (g n j)"))
+        down(0)
+        down(1)
+        gated(c, 3)
+        quant_h(c, 2, 3)
+        down(2)
+        scatter(0)
+        quant_h(c, 3, 4)
+        down(3)
+        scatter(1)
+        scatter(2)
+        scatter(3)
+        nc.sync.dma_start(out=out, in_=result[:])

@@ -22,8 +22,7 @@ PASSES = K // KP
 CHUNKS = H // KP
 QUART = 4
 NQ = S // QUART
-SCALAR_ONLY = (0, 1, 2, 6)
-VECTOR_ONLY = (10,)
+HALF = S // 2
 
 
 def tile_picked_depth_glu_silu_sub_p_kernel(tc, x_words, x_scales, w1, w3, w2, gate, offs, out):
@@ -44,23 +43,31 @@ def tile_picked_depth_glu_silu_sub_p_kernel(tc, x_words, x_scales, w1, w3, w2, g
         nc.scalar.activation(warm_out[:], warm[:], SILU)
 
         weights = (w1, w3)
-        pieces = [(c, mat, g) for c in range(CHUNKS) for mat in range(2) for g in range(PASSES)]
         xw = [keep.tile([P, T], I32, name="xw%d" % g, align_bytes=64) for g in range(PASSES)]
         raw = {}
-        for i, (c, mat, g) in enumerate(pieces):
-            if i < PASSES:
-                nc.sync.dma_start(out=xw[i][:], in_=x_words[i].rearrange("p n t -> p (n t)").bitcast(I32))
+
+        def load_x(g):
+            nc.sync.dma_start(out=xw[g][:], in_=x_words[g].rearrange("p n t -> p (n t)").bitcast(I32))
+
+        def load_w(mat, g, c0, c1):
             rows = weights[mat][g * KP : (g + 1) * KP, :].rearrange("(p j) h -> p j h", j=PACK)
-            parts = 2 if i == len(pieces) - 1 else 1
-            width = KP // parts
-            raw[i] = []
-            for a in range(parts):
-                tl = keep.tile([P, PACK, width], F32, name="raw%d_%d" % (i, a), align_bytes=64)
-                nc.sync.dma_start(out=tl[:], in_=rows[:, :, c * KP + a * width : c * KP + (a + 1) * width])
-                raw[i].append(tl)
-            if i == 0:
-                for q in range(4):
-                    nc.sync.dma_start(out=xs[:].bitcast(I32)[32 * q : 32 * q + 4 * PASSES, :], in_=x_scales[:, 4 * q : 4 * q + 4, :].bitcast(I32))
+            tl = keep.tile([P, PACK, (c1 - c0) * KP], F32, name="raw%d%d%d" % (mat, g, c0), align_bytes=64)
+            nc.sync.dma_start(out=tl[:], in_=rows[:, :, c0 * KP : c1 * KP])
+            for c in range(c0, c1):
+                raw[(mat, g, c)] = tl[:, :, (c - c0) * KP : (c - c0 + 1) * KP]
+
+        load_x(0)
+        load_w(0, 0, 0, 2)
+        for q in range(4):
+            nc.sync.dma_start(out=xs[:].bitcast(I32)[32 * q : 32 * q + 4 * PASSES, :], in_=x_scales[:, 4 * q : 4 * q + 4, :].bitcast(I32))
+        load_x(1)
+        load_x(2)
+        load_w(0, 1, 0, 2)
+        load_w(0, 2, 0, 2)
+        load_w(1, 0, 0, 2)
+        for c in range(CHUNKS):
+            load_w(1, 1, c, c + 1)
+            load_w(1, 2, c, c + 1)
         w2_raw = keep.tile([P, CHUNKS, PACK, N], F32, name="w2_raw", align_bytes=64)
         nc.sync.dma_start(out=w2_raw[:], in_=w2.rearrange("(g p j) n -> p g j n", p=P, j=PACK))
         gate_sb = keep.tile([P, S], F32, name="gate_sb", align_bytes=64)
@@ -76,54 +83,61 @@ def tile_picked_depth_glu_silu_sub_p_kernel(tc, x_words, x_scales, w1, w3, w2, g
         codes = {}
         scales = {}
 
-        def cast(i):
-            grouped[i] = stage.tile([P, PACK, P, PACK], BF16, name="grouped", align_bytes=64)
-            parts = len(raw[i])
-            mw = P // parts
-            for a, tl in enumerate(raw[i]):
-                src = tl[:].rearrange("p j (m t) -> p m j t", t=PACK)
-                dst = grouped[i][:].rearrange("p t m j -> p m j t")[:, a * mw : (a + 1) * mw]
-                first = nc.vector.tensor_copy if i in VECTOR_ONLY else nc.scalar.copy
-                second = nc.scalar.copy if i in SCALAR_ONLY else nc.vector.tensor_copy
-                first(dst[:, :, :, 0:2], src[:, :, :, 0:2])
-                second(dst[:, :, :, 2:4], src[:, :, :, 2:4])
+        def cast(key, who):
+            grouped[key] = stage.tile([P, PACK, P, PACK], BF16, name="grouped", align_bytes=64)
+            src = raw[key].rearrange("p j (m t) -> p m j t", t=PACK)
+            dst = grouped[key][:].rearrange("p t m j -> p m j t")
+            first = nc.vector.tensor_copy if who == "V" else nc.scalar.copy
+            second = nc.scalar.copy if who == "S" else nc.vector.tensor_copy
+            first(dst[:, :, :, 0:2], src[:, :, :, 0:2])
+            second(dst[:, :, :, 2:4], src[:, :, :, 2:4])
+            codes[key] = keep.tile([P, KP], U32, name="codes%d%d%d" % key, align_bytes=64)
+            scales[key] = keep.tile([P, KP], U8, name="scales%d%d%d" % key, align_bytes=64)
 
-        def quant(i):
-            codes[i] = keep.tile([P, KP], U32, name="codes%d" % i, align_bytes=64)
-            scales[i] = keep.tile([P, KP], U8, name="scales%d" % i, align_bytes=64)
-            nc.vector.quantize_mx(out=codes[i][:].bitcast(FP8X4), scales=scales[i][:], in_=grouped[i][:].rearrange("p t m j -> p (t m j)"))
+        def quant(key, t0, t1):
+            cols = slice(t0 * P, t1 * P)
+            nc.vector.quantize_mx(
+                out=codes[key][:, cols].bitcast(FP8X4),
+                scales=scales[key][:, cols],
+                in_=grouped[key][:, t0:t1].rearrange("p t m j -> p (t m j)"),
+            )
 
         banks = {}
 
-        def multiply(i):
-            c, mat, g = pieces[i]
+        def multiply(key, ts, closes):
+            mat, g, c = key
             if g == 0:
                 for q in range(QUART):
-                    banks[(c, mat, q)] = psum.tile([P, PACK, NQ], F32, name="acc", tag="bank%d" % (mat * QUART + q))
+                    banks[(mat, c, q)] = psum.tile([P, PACK, NQ], F32, name="acc", tag="bank%d" % (c * QUART + q))
             for q in range(QUART):
                 cols = slice(q * NQ, (q + 1) * NQ)
-                for t in range(PACK):
+                for t in ts:
                     mc = slice(t * P, (t + 1) * P)
                     nc.tensor.matmul_mx(
-                        out=banks[(c, mat, q)][:, t, :],
-                        lhsT=codes[i][:, mc].bitcast(FP8X4),
-                        lhsT_scale=scales[i][:, mc],
+                        out=banks[(mat, c, q)][:, t, :],
+                        lhsT=codes[key][:, mc].bitcast(FP8X4),
+                        lhsT_scale=scales[key][:, mc],
                         rhs=xg[g][:, cols].bitcast(FP8X4),
                         rhs_scale=xsg[4 * g : P, cols],
                         start=(g == 0 and t == 0),
-                        stop=(g == PASSES - 1 and t == PACK - 1),
+                        stop=(closes and t == ts[-1]),
                     )
+
+        def whole(key):
+            quant(key, 0, PACK)
+            multiply(key, range(PACK), key[1] == PASSES - 1)
 
         act = [keep.tile([P, QUART, NQ, PACK], F32, name="act%d" % c, align_bytes=64) for c in range(CHUNKS)]
         hb = [keep.tile([P, QUART, NQ, PACK], BF16, name="hb%d" % c, align_bytes=64) for c in range(CHUNKS)]
         hc = [keep.tile([P, S], U32, name="hc%d" % c, align_bytes=64) for c in range(CHUNKS)]
         hs = [keep.tile([P, S], U8, name="hs%d" % c, align_bytes=64) for c in range(CHUNKS)]
 
-        def silu(c, q):
-            nc.scalar.activation(act[c][:, q], banks[(c, 0, q)][:].rearrange("p t n -> p n t"), SILU)
+        def silu(c):
+            for q in range(QUART):
+                nc.scalar.activation(act[c][:, q], banks[(0, c, q)][:].rearrange("p t n -> p n t"), SILU)
 
         def gated(c, q):
-            nc.vector.tensor_tensor(hb[c][:, q], banks[(c, 1, q)][:].rearrange("p t n -> p n t"), act[c][:, q], MULT)
+            nc.vector.tensor_tensor(hb[c][:, q], banks[(1, c, q)][:].rearrange("p t n -> p n t"), act[c][:, q], MULT)
 
         def quant_h(c, q0, q1):
             cols = slice(q0 * NQ, q1 * NQ)
@@ -133,24 +147,39 @@ def tile_picked_depth_glu_silu_sub_p_kernel(tc, x_words, x_scales, w1, w3, w2, g
             nc.vector.tensor_copy(xg[g][:], xw[g][:].bitcast(U32).indirect(offsets[:]))
 
         gather_words(0)
-        cast(0)
+        cast((0, 0, 0), "S")
+        cast((0, 0, 1), "S")
         nc.vector.tensor_copy(xsg[:], xs[:].indirect(offsets[:]))
-        last = len(pieces) - 1
-        for i in range(len(pieces)):
-            c, mat, g = pieces[i]
-            if i + 1 < PASSES:
-                gather_words(i + 1)
-            quant(i)
-            multiply(i)
-            if i < last:
-                cast(i + 1)
-            if g == PASSES - 1 and mat == 0:
-                for q in range(QUART):
-                    silu(c, q)
-            if g == PASSES - 1 and mat == 1 and i < last:
-                for q in range(QUART):
-                    gated(c, q)
-                quant_h(c, 0, QUART)
+        gather_words(1)
+        whole((0, 0, 0))
+        gather_words(2)
+        whole((0, 0, 1))
+        for g in (1, 2):
+            cast((0, g, 0), "both")
+            cast((0, g, 1), "both")
+            whole((0, g, 0))
+            whole((0, g, 1))
+        silu(0)
+        silu(1)
+        cast((1, 0, 0), "V")
+        cast((1, 0, 1), "V")
+        whole((1, 0, 0))
+        cast((1, 1, 0), "both")
+        whole((1, 0, 1))
+        whole((1, 1, 0))
+        cast((1, 2, 0), "both")
+        whole((1, 2, 0))
+        cast((1, 1, 1), "S")
+        for q in range(QUART):
+            gated(0, q)
+        whole((1, 1, 1))
+        last = (1, 2, 1)
+        cast(last, "both")
+        quant(last, 2, 4)
+        multiply(last, (2, 3), False)
+        quant(last, 0, 2)
+        multiply(last, (0, 1), True)
+        quant_h(0, 0, QUART)
 
         w2_grouped = keep.tile([P, CHUNKS, N, PACK], BF16, name="w2_grouped", align_bytes=64)
         for g in range(CHUNKS):
@@ -162,9 +191,9 @@ def tile_picked_depth_glu_silu_sub_p_kernel(tc, x_words, x_scales, w1, w3, w2, g
         w2_scales = keep.tile([P, CHUNKS * N], U8, name="w2_scales", align_bytes=64)
         y_sb = keep.tile([P, S], F32, name="y_sb", align_bytes=64)
 
-        def down(q):
-            cols = slice(q * NQ, (q + 1) * NQ)
-            y = psum.tile([P, NQ], F32, name="y", tag="bank%d" % q)
+        def down(u):
+            cols = slice(u * HALF, (u + 1) * HALF)
+            y = psum.tile([P, HALF], F32, name="y", tag="bank%d" % u)
             for g in range(CHUNKS):
                 nc.tensor.matmul_mx(
                     out=y[:],
@@ -177,27 +206,21 @@ def tile_picked_depth_glu_silu_sub_p_kernel(tc, x_words, x_scales, w1, w3, w2, g
                 )
             nc.scalar.copy(y_sb[:, cols], y[:])
 
-        def scatter(q):
-            cols = slice(q * NQ, (q + 1) * NQ)
-            w = NQ // 16
-            nc.vector.tensor_tensor(result[:].indirect(offsets[:, q * w : (q + 1) * w]), y_sb[:, cols], gate_sb[:, cols], MULT)
+        def scatter(u):
+            cols = slice(u * HALF, (u + 1) * HALF)
+            w = HALF // 16
+            nc.vector.tensor_tensor(result[:].indirect(offsets[:, u * w : (u + 1) * w]), y_sb[:, cols], gate_sb[:, cols], MULT)
 
         c = CHUNKS - 1
         gated(c, 0)
         gated(c, 1)
-        quant_h(c, 0, 1)
-        gated(c, 2)
-        quant_h(c, 1, 2)
         nc.vector.quantize_mx(out=w2_codes[:].bitcast(FP8X4), scales=w2_scales[:], in_=w2_grouped[:].rearrange("p g n j -> p (g n j)"))
+        quant_h(c, 0, 2)
         down(0)
-        down(1)
+        gated(c, 2)
         gated(c, 3)
-        quant_h(c, 2, 3)
-        down(2)
+        quant_h(c, 2, 4)
+        down(1)
         scatter(0)
-        quant_h(c, 3, 4)
-        down(3)
         scatter(1)
-        scatter(2)
-        scatter(3)
         nc.sync.dma_start(out=out, in_=result[:])

@@ -23,13 +23,14 @@ CHUNKS = H // KP
 QUART = 4
 NQ = S // QUART
 HALF = S // 2
+CASTERS = ("S", "S", "both", "V", "both", "both", "S", "S", "both", "V", "V", "both")
 
 
 def tile_picked_depth_glu_silu_sub_p_kernel(tc, x_words, x_scales, w1, w3, w2, gate, offs, out):
     nc = tc.nc
     with ExitStack() as ctx:
         keep = ctx.enter_context(tc.tile_pool(name="keep", bufs=1))
-        stage = ctx.enter_context(tc.tile_pool(name="stage", bufs=4))
+        stage = ctx.enter_context(tc.tile_pool(name="stage", bufs=8))
         psum = ctx.enter_context(tc.psum_pool(name="psum", bufs=1))
 
         offsets = keep.tile([P, S // 16], U16, name="offsets")
@@ -38,7 +39,7 @@ def tile_picked_depth_glu_silu_sub_p_kernel(tc, x_words, x_scales, w1, w3, w2, g
         warm = keep.tile([P, 8], F32, name="warm")
         warm_out = keep.tile([P, 8], F32, name="warm_out")
         xs = keep.tile([P, T], U8, name="xs", align_bytes=64)
-        nc.vector.memset(xs[:].bitcast(I32), 0)
+        nc.gpsimd.memset(xs[:].bitcast(I32), 0)
         nc.vector.memset(warm[:], 0.0)
         nc.scalar.activation(warm_out[:], warm[:], SILU)
 
@@ -49,25 +50,25 @@ def tile_picked_depth_glu_silu_sub_p_kernel(tc, x_words, x_scales, w1, w3, w2, g
         def load_x(g):
             nc.sync.dma_start(out=xw[g][:], in_=x_words[g].rearrange("p n t -> p (n t)").bitcast(I32))
 
-        def load_w(mat, g, c0, c1):
+        def load_w(key, parts):
+            mat, g, c = key
             rows = weights[mat][g * KP : (g + 1) * KP, :].rearrange("(p j) h -> p j h", j=PACK)
-            tl = keep.tile([P, PACK, (c1 - c0) * KP], F32, name="raw%d%d%d" % (mat, g, c0), align_bytes=64)
-            nc.sync.dma_start(out=tl[:], in_=rows[:, :, c0 * KP : c1 * KP])
-            for c in range(c0, c1):
-                raw[(mat, g, c)] = tl[:, :, (c - c0) * KP : (c - c0 + 1) * KP]
+            width = KP // parts
+            raw[key] = []
+            for a in range(parts):
+                tl = keep.tile([P, PACK, width], F32, name="raw%d%d%d%d" % (mat, g, c, a), align_bytes=64)
+                nc.sync.dma_start(out=tl[:], in_=rows[:, :, c * KP + a * width : c * KP + (a + 1) * width])
+                raw[key].append(tl)
 
-        load_x(0)
-        load_w(0, 0, 0, 2)
-        for q in range(4):
-            nc.sync.dma_start(out=xs[:].bitcast(I32)[32 * q : 32 * q + 4 * PASSES, :], in_=x_scales[:, 4 * q : 4 * q + 4, :].bitcast(I32))
-        load_x(1)
-        load_x(2)
-        load_w(0, 1, 0, 2)
-        load_w(0, 2, 0, 2)
-        load_w(1, 0, 0, 2)
-        for c in range(CHUNKS):
-            load_w(1, 1, c, c + 1)
-            load_w(1, 2, c, c + 1)
+        pieces = [(mat, g, c) for c in range(CHUNKS) for mat in range(2) for g in range(PASSES)]
+        last = pieces[-1]
+        for i, key in enumerate(pieces):
+            if i < PASSES:
+                load_x(i)
+            load_w(key, 2 if key == last else 1)
+            if i == 0:
+                for q in range(4):
+                    nc.sync.dma_start(out=xs[:].bitcast(I32)[32 * q : 32 * q + 4 * PASSES, :], in_=x_scales[:, 4 * q : 4 * q + 4, :].bitcast(I32))
         w2_raw = keep.tile([P, CHUNKS, PACK, N], F32, name="w2_raw", align_bytes=64)
         nc.sync.dma_start(out=w2_raw[:], in_=w2.rearrange("(g p j) n -> p g j n", p=P, j=PACK))
         gate_sb = keep.tile([P, S], F32, name="gate_sb", align_bytes=64)
@@ -85,12 +86,14 @@ def tile_picked_depth_glu_silu_sub_p_kernel(tc, x_words, x_scales, w1, w3, w2, g
 
         def cast(key, who):
             grouped[key] = stage.tile([P, PACK, P, PACK], BF16, name="grouped", align_bytes=64)
-            src = raw[key].rearrange("p j (m t) -> p m j t", t=PACK)
-            dst = grouped[key][:].rearrange("p t m j -> p m j t")
             first = nc.vector.tensor_copy if who == "V" else nc.scalar.copy
             second = nc.scalar.copy if who == "S" else nc.vector.tensor_copy
-            first(dst[:, :, :, 0:2], src[:, :, :, 0:2])
-            second(dst[:, :, :, 2:4], src[:, :, :, 2:4])
+            mw = P // len(raw[key])
+            for a, tl in enumerate(raw[key]):
+                src = tl[:].rearrange("p j (m t) -> p m j t", t=PACK)
+                dst = grouped[key][:].rearrange("p t m j -> p m j t")[:, a * mw : (a + 1) * mw]
+                first(dst[:, :, :, 0:2], src[:, :, :, 0:2])
+                second(dst[:, :, :, 2:4], src[:, :, :, 2:4])
             codes[key] = keep.tile([P, KP], U32, name="codes%d%d%d" % key, align_bytes=64)
             scales[key] = keep.tile([P, KP], U8, name="scales%d%d%d" % key, align_bytes=64)
 
@@ -108,7 +111,7 @@ def tile_picked_depth_glu_silu_sub_p_kernel(tc, x_words, x_scales, w1, w3, w2, g
             mat, g, c = key
             if g == 0:
                 for q in range(QUART):
-                    banks[(mat, c, q)] = psum.tile([P, PACK, NQ], F32, name="acc", tag="bank%d" % (c * QUART + q))
+                    banks[(mat, c, q)] = psum.tile([P, PACK, NQ], F32, name="acc", tag="bank%d" % (mat * QUART + q))
             for q in range(QUART):
                 cols = slice(q * NQ, (q + 1) * NQ)
                 for t in ts:
@@ -147,39 +150,25 @@ def tile_picked_depth_glu_silu_sub_p_kernel(tc, x_words, x_scales, w1, w3, w2, g
             nc.vector.tensor_copy(xg[g][:], xw[g][:].bitcast(U32).indirect(offsets[:]))
 
         gather_words(0)
-        cast((0, 0, 0), "S")
-        cast((0, 0, 1), "S")
-        nc.vector.tensor_copy(xsg[:], xs[:].indirect(offsets[:]))
-        gather_words(1)
-        whole((0, 0, 0))
-        gather_words(2)
-        whole((0, 0, 1))
-        for g in (1, 2):
-            cast((0, g, 0), "both")
-            cast((0, g, 1), "both")
-            whole((0, g, 0))
-            whole((0, g, 1))
-        silu(0)
-        silu(1)
-        cast((1, 0, 0), "V")
-        cast((1, 0, 1), "V")
-        whole((1, 0, 0))
-        cast((1, 1, 0), "both")
-        whole((1, 0, 1))
-        whole((1, 1, 0))
-        cast((1, 2, 0), "both")
-        whole((1, 2, 0))
-        cast((1, 1, 1), "S")
-        for q in range(QUART):
-            gated(0, q)
-        whole((1, 1, 1))
-        last = (1, 2, 1)
-        cast(last, "both")
-        quant(last, 2, 4)
-        multiply(last, (2, 3), False)
-        quant(last, 0, 2)
-        multiply(last, (0, 1), True)
-        quant_h(0, 0, QUART)
+        for i, key in enumerate(pieces):
+            mat, g, c = key
+            cast(key, CASTERS[i])
+            if i == 0:
+                nc.vector.tensor_copy(xsg[:], xs[:].indirect(offsets[:]))
+            elif i < PASSES:
+                gather_words(i)
+            if key == last:
+                quant(key, 2, 4)
+                quant(key, 0, 2)
+                multiply(key, (2, 3, 0, 1), True)
+                quant_h(0, 0, QUART)
+            else:
+                whole(key)
+                if g == PASSES - 1 and mat == 0:
+                    silu(c)
+                if g == PASSES - 1 and mat == 1:
+                    for q in range(QUART):
+                        gated(c, q)
 
         w2_grouped = keep.tile([P, CHUNKS, N, PACK], BF16, name="w2_grouped", align_bytes=64)
         for g in range(CHUNKS):
@@ -191,9 +180,9 @@ def tile_picked_depth_glu_silu_sub_p_kernel(tc, x_words, x_scales, w1, w3, w2, g
         w2_scales = keep.tile([P, CHUNKS * N], U8, name="w2_scales", align_bytes=64)
         y_sb = keep.tile([P, S], F32, name="y_sb", align_bytes=64)
 
-        def down(u):
-            cols = slice(u * HALF, (u + 1) * HALF)
-            y = psum.tile([P, HALF], F32, name="y", tag="bank%d" % u)
+        def down(q0, q1):
+            cols = slice(q0 * NQ, q1 * NQ)
+            y = psum.tile([P, (q1 - q0) * NQ], F32, name="y", tag="bank%d" % q0)
             for g in range(CHUNKS):
                 nc.tensor.matmul_mx(
                     out=y[:],
@@ -216,11 +205,13 @@ def tile_picked_depth_glu_silu_sub_p_kernel(tc, x_words, x_scales, w1, w3, w2, g
         gated(c, 1)
         nc.vector.quantize_mx(out=w2_codes[:].bitcast(FP8X4), scales=w2_scales[:], in_=w2_grouped[:].rearrange("p g n j -> p (g n j)"))
         quant_h(c, 0, 2)
-        down(0)
+        down(0, 2)
         gated(c, 2)
         gated(c, 3)
-        quant_h(c, 2, 4)
-        down(1)
+        quant_h(c, 2, 3)
+        down(2, 3)
+        quant_h(c, 3, 4)
+        down(3, 4)
         scatter(0)
         scatter(1)
         nc.sync.dma_start(out=out, in_=result[:])

@@ -50,25 +50,26 @@ def tile_picked_depth_glu_silu_sub_p_kernel(tc, x_words, x_scales, w1, w3, w2, g
         def load_x(g):
             nc.sync.dma_start(out=xw[g][:], in_=x_words[g].rearrange("p n t -> p (n t)").bitcast(I32))
 
-        def load_w(key, parts):
+        def load_w(key, widths):
             mat, g, c = key
             rows = weights[mat][g * KP : (g + 1) * KP, :].rearrange("(p j) h -> p j h", j=PACK)
-            width = KP // parts
             raw[key] = []
-            for a in range(parts):
-                tl = keep.tile([P, PACK, width], F32, name="raw%d%d%d%d" % (mat, g, c, a), align_bytes=64)
-                nc.sync.dma_start(out=tl[:], in_=rows[:, :, c * KP + a * width : c * KP + (a + 1) * width])
-                raw[key].append(tl)
+            col = 0
+            for width in widths:
+                tl = keep.tile([P, PACK, width], F32, name="raw%d%d%d_%d" % (mat, g, c, col), align_bytes=64)
+                nc.sync.dma_start(out=tl[:], in_=rows[:, :, c * KP + col : c * KP + col + width])
+                raw[key].append((tl, col // PACK, (col + width) // PACK))
+                col += width
 
         pieces = [(mat, g, c) for c in range(CHUNKS) for mat in range(2) for g in range(PASSES)]
         last = pieces[-1]
         for i, key in enumerate(pieces):
             if i < PASSES:
                 load_x(i)
-            load_w(key, 2 if key == last else 1)
-            if i == 0:
+            if i == 1:
                 for q in range(4):
                     nc.sync.dma_start(out=xs[:].bitcast(I32)[32 * q : 32 * q + 4 * PASSES, :], in_=x_scales[:, 4 * q : 4 * q + 4, :].bitcast(I32))
+            load_w(key, (256, 128, 128) if key == last else (KP,))
         w2_raw = keep.tile([P, CHUNKS, PACK, N], F32, name="w2_raw", align_bytes=64)
         nc.sync.dma_start(out=w2_raw[:], in_=w2.rearrange("(g p j) n -> p g j n", p=P, j=PACK))
         gate_sb = keep.tile([P, S], F32, name="gate_sb", align_bytes=64)
@@ -88,10 +89,9 @@ def tile_picked_depth_glu_silu_sub_p_kernel(tc, x_words, x_scales, w1, w3, w2, g
             grouped[key] = stage.tile([P, PACK, P, PACK], BF16, name="grouped", align_bytes=64)
             first = nc.vector.tensor_copy if who == "V" else nc.scalar.copy
             second = nc.scalar.copy if who == "S" else nc.vector.tensor_copy
-            mw = P // len(raw[key])
-            for a, tl in enumerate(raw[key]):
+            for tl, m0, m1 in raw[key]:
                 src = tl[:].rearrange("p j (m t) -> p m j t", t=PACK)
-                dst = grouped[key][:].rearrange("p t m j -> p m j t")[:, a * mw : (a + 1) * mw]
+                dst = grouped[key][:].rearrange("p t m j -> p m j t")[:, m0:m1]
                 first(dst[:, :, :, 0:2], src[:, :, :, 0:2])
                 second(dst[:, :, :, 2:4], src[:, :, :, 2:4])
             codes[key] = keep.tile([P, KP], U32, name="codes%d%d%d" % key, align_bytes=64)
@@ -154,9 +154,10 @@ def tile_picked_depth_glu_silu_sub_p_kernel(tc, x_words, x_scales, w1, w3, w2, g
             mat, g, c = key
             cast(key, CASTERS[i])
             if i == 0:
+                gather_words(1)
                 nc.vector.tensor_copy(xsg[:], xs[:].indirect(offsets[:]))
-            elif i < PASSES:
-                gather_words(i)
+            elif i == 1:
+                gather_words(2)
             if key == last:
                 quant(key, 2, 4)
                 quant(key, 0, 2)

@@ -71,7 +71,10 @@ def tile_picked_depth_glu_silu_sub_p_kernel(tc, x_words, x_scales, w1, w3, w2, g
                     nc.sync.dma_start(out=xs[:].bitcast(I32)[32 * q : 32 * q + 4 * PASSES, :], in_=x_scales[:, 4 * q : 4 * q + 4, :].bitcast(I32))
             load_w(key, (256, 128, 128) if key == last else (KP,))
         w2_raw = keep.tile([P, CHUNKS, PACK, N], F32, name="w2_raw", align_bytes=64)
-        nc.sync.dma_start(out=w2_raw[:], in_=w2.rearrange("(g p j) n -> p g j n", p=P, j=PACK))
+        w2_rows = w2.rearrange("(g a t e) n -> g e a t n", g=CHUNKS, t=PACK, e=2)
+        for g in range(CHUNKS):
+            for e in range(2):
+                nc.sync.dma_start(out=w2_raw[e:P:2, g], in_=w2_rows[g, e])
         gate_sb = keep.tile([P, S], F32, name="gate_sb", align_bytes=64)
         nc.sync.dma_start(out=gate_sb[:], in_=gate)
 
@@ -90,10 +93,10 @@ def tile_picked_depth_glu_silu_sub_p_kernel(tc, x_words, x_scales, w1, w3, w2, g
             first = nc.vector.tensor_copy if who == "V" else nc.scalar.copy
             second = nc.scalar.copy if who == "S" else nc.vector.tensor_copy
             for tl, m0, m1 in raw[key]:
-                src = tl[:].rearrange("p j (m t) -> p m j t", t=PACK)
-                dst = grouped[key][:].rearrange("p t m j -> p m j t")[:, m0:m1]
-                first(dst[:, :, :, 0:2], src[:, :, :, 0:2])
-                second(dst[:, :, :, 2:4], src[:, :, :, 2:4])
+                src = tl[:].rearrange("p j (a t e) -> p a t j e", t=PACK, e=2)
+                dst = grouped[key][:].rearrange("p t (a e) j -> p a t j e", e=2)[:, m0 // 2 : m1 // 2]
+                first(dst[:, :, 0:2], src[:, :, 0:2])
+                second(dst[:, :, 2:4], src[:, :, 2:4])
             codes[key] = keep.tile([P, KP], U32, name="codes%d%d%d" % key, align_bytes=64)
             scales[key] = keep.tile([P, KP], U8, name="scales%d%d%d" % key, align_bytes=64)
 

@@ -23,7 +23,12 @@ CHUNKS = H // KP
 QUART = 4
 NQ = S // QUART
 HALF = S // 2
-CASTERS = ("S", "S", "both", "V", "both", "both", "S", "S", "both", "V", "V", "both")
+SHARES = (32, 32, 32, 32, 48, 32, 64, 40, 64, 32, 40, 16)
+LOADS = "x0 00 x1 s 01 x2 10 020 110 120 021 111 121"
+GLAG = 3
+SLAG = (0, 2)
+TAIL = "g0 g1 w q02 d02 g2 g3 q23 d23 q34 d34 s02 s24"
+LAST = (256, 128, 128)
 
 
 def tile_picked_depth_glu_silu_sub_p_kernel(tc, x_words, x_scales, w1, w3, w2, gate, offs, out):
@@ -58,18 +63,31 @@ def tile_picked_depth_glu_silu_sub_p_kernel(tc, x_words, x_scales, w1, w3, w2, g
             for width in widths:
                 tl = keep.tile([P, PACK, width], F32, name="raw%d%d%d_%d" % (mat, g, c, col), align_bytes=64)
                 nc.sync.dma_start(out=tl[:], in_=rows[:, :, c * KP + col : c * KP + col + width])
-                raw[key].append((tl, col // PACK, (col + width) // PACK))
+                raw[key].append((tl[:], col // PACK, (col + width) // PACK))
                 col += width
 
-        pieces = [(mat, g, c) for c in range(CHUNKS) for mat in range(2) for g in range(PASSES)]
-        last = pieces[-1]
-        for i, key in enumerate(pieces):
-            if i < PASSES:
-                load_x(i)
-            if i == 1:
+        def load_full(mat, g):
+            rows = weights[mat][g * KP : (g + 1) * KP, :].rearrange("(p j) h -> p j h", j=PACK)
+            tl = keep.tile([P, PACK, H], F32, name="full%d%d" % (mat, g), align_bytes=64)
+            nc.sync.dma_start(out=tl[:], in_=rows)
+            for c in range(CHUNKS):
+                raw[(mat, g, c)] = [(tl[:, :, c * KP : (c + 1) * KP], 0, P)]
+
+        pieces = []
+        for it in LOADS.split():
+            if it[0] == "x":
+                load_x(int(it[1]))
+            elif it == "s":
                 for q in range(4):
                     nc.sync.dma_start(out=xs[:].bitcast(I32)[32 * q : 32 * q + 4 * PASSES, :], in_=x_scales[:, 4 * q : 4 * q + 4, :].bitcast(I32))
-            load_w(key, (256, 128, 128) if key == last else (KP,))
+            elif len(it) == 2:
+                load_full(int(it[0]), int(it[1]))
+                pieces += [(int(it[0]), int(it[1]), c) for c in range(2)]
+            else:
+                key = tuple(int(v) for v in it)
+                load_w(key, LAST if it == LOADS.split()[-1] else (KP,))
+                pieces.append(key)
+        last = pieces[-1]
         w2_raw = keep.tile([P, CHUNKS, PACK, N], F32, name="w2_raw", align_bytes=64)
         w2_rows = w2.rearrange("(g a t e) n -> g e a t n", g=CHUNKS, t=PACK, e=2)
         for g in range(CHUNKS):
@@ -88,15 +106,17 @@ def tile_picked_depth_glu_silu_sub_p_kernel(tc, x_words, x_scales, w1, w3, w2, g
         codes = {}
         scales = {}
 
-        def cast(key, who):
+        def cast(key, share):
             grouped[key] = stage.tile([P, PACK, P, PACK], BF16, name="grouped", align_bytes=64)
-            first = nc.vector.tensor_copy if who == "V" else nc.scalar.copy
-            second = nc.scalar.copy if who == "S" else nc.vector.tensor_copy
             for tl, m0, m1 in raw[key]:
-                src = tl[:].rearrange("p j (a t e) -> p a t j e", t=PACK, e=2)
+                src = tl.rearrange("p j (a t e) -> p a t j e", t=PACK, e=2)
                 dst = grouped[key][:].rearrange("p t (a e) j -> p a t j e", e=2)[:, m0 // 2 : m1 // 2]
-                first(dst[:, :, 0:2], src[:, :, 0:2])
-                second(dst[:, :, 2:4], src[:, :, 2:4])
+                n = (m1 - m0) // 2
+                cut = 2 * ((share * n + 64) // 128)
+                if cut > 0:
+                    nc.vector.tensor_copy(dst[:, 0:cut], src[:, 0:cut])
+                if cut < n:
+                    nc.scalar.copy(dst[:, cut:n], src[:, cut:n])
             codes[key] = keep.tile([P, KP], U32, name="codes%d%d%d" % key, align_bytes=64)
             scales[key] = keep.tile([P, KP], U8, name="scales%d%d%d" % key, align_bytes=64)
 
@@ -110,11 +130,11 @@ def tile_picked_depth_glu_silu_sub_p_kernel(tc, x_words, x_scales, w1, w3, w2, g
 
         banks = {}
 
-        def multiply(key, ts, closes):
+        def multiply(key, ts, opens, closes, half):
             mat, g, c = key
-            if g == 0:
+            if opens:
                 for q in range(QUART):
-                    banks[(mat, c, q)] = psum.tile([P, PACK, NQ], F32, name="acc", tag="bank%d" % (mat * QUART + q))
+                    banks[(mat, c, q)] = psum.tile([P, PACK, NQ], F32, name="acc", tag="bank%d" % (half * QUART + q))
             for q in range(QUART):
                 cols = slice(q * NQ, (q + 1) * NQ)
                 for t in ts:
@@ -125,13 +145,9 @@ def tile_picked_depth_glu_silu_sub_p_kernel(tc, x_words, x_scales, w1, w3, w2, g
                         lhsT_scale=scales[key][:, mc],
                         rhs=xg[g][:, cols].bitcast(FP8X4),
                         rhs_scale=xsg[4 * g : P, cols],
-                        start=(g == 0 and t == 0),
+                        start=(opens and t == ts[0]),
                         stop=(closes and t == ts[-1]),
                     )
-
-        def whole(key):
-            quant(key, 0, PACK)
-            multiply(key, range(PACK), key[1] == PASSES - 1)
 
         act = [keep.tile([P, QUART, NQ, PACK], F32, name="act%d" % c, align_bytes=64) for c in range(CHUNKS)]
         hb = [keep.tile([P, QUART, NQ, PACK], BF16, name="hb%d" % c, align_bytes=64) for c in range(CHUNKS)]
@@ -152,27 +168,60 @@ def tile_picked_depth_glu_silu_sub_p_kernel(tc, x_words, x_scales, w1, w3, w2, g
         def gather_words(g):
             nc.vector.tensor_copy(xg[g][:], xw[g][:].bitcast(U32).indirect(offsets[:]))
 
-        gather_words(0)
+        for g in range(PASSES):
+            gather_words(g)
+        nc.vector.tensor_copy(xsg[:], xs[:].indirect(offsets[:]))
+        TAGS = {}
+        free = [0, 1]
+        pend = []
+        ndone = {}
+        later = []
+
+        def pump():
+            again = True
+            while again:
+                again = False
+                for key in list(pend):
+                    mat, g, c = key
+                    if (mat, c) not in TAGS:
+                        if not free or (mat == 1 and (0, c) not in TAGS) or (c == 1 and (mat, 0) not in TAGS):
+                            continue
+                        TAGS[(mat, c)] = free.pop(0)
+                    n = ndone.get((mat, c), 0)
+                    pend.remove(key)
+                    multiply(key, range(PACK) if key != last else (2, 3, 0, 1), n == 0, n == PASSES - 1, TAGS[(mat, c)])
+                    ndone[(mat, c)] = n + 1
+                    if n == PASSES - 1 and key != last:
+                        later.append([SLAG[c] if mat == 0 else GLAG, mat, c])
+                for ent in list(later):
+                    if ent[0] <= 0 and (ent[1] == 0 or ent[2] in silued):
+                        later.remove(ent)
+                        if ent[1] == 0:
+                            silu(ent[2])
+                            silued.append(ent[2])
+                        else:
+                            for q in range(QUART):
+                                gated(ent[2], q)
+                        free.append(TAGS[(ent[1], ent[2])])
+                        again = True
+
+        silued = []
         for i, key in enumerate(pieces):
-            mat, g, c = key
-            cast(key, CASTERS[i])
-            if i == 0:
-                gather_words(1)
-                nc.vector.tensor_copy(xsg[:], xs[:].indirect(offsets[:]))
-            elif i == 1:
-                gather_words(2)
+            cast(key, SHARES[i])
             if key == last:
+                for ent in later:
+                    ent[0] = 0
+                pump()
                 quant(key, 2, 4)
                 quant(key, 0, 2)
-                multiply(key, (2, 3, 0, 1), True)
-                quant_h(0, 0, QUART)
             else:
-                whole(key)
-                if g == PASSES - 1 and mat == 0:
-                    silu(c)
-                if g == PASSES - 1 and mat == 1:
-                    for q in range(QUART):
-                        gated(c, q)
+                quant(key, 0, PACK)
+            for ent in later:
+                ent[0] -= 1
+            pend.append(key)
+            pump()
+        assert not pend and not later
+        quant_h(0, 0, QUART)
 
         w2_grouped = keep.tile([P, CHUNKS, N, PACK], BF16, name="w2_grouped", align_bytes=64)
         for g in range(CHUNKS):
@@ -186,7 +235,7 @@ def tile_picked_depth_glu_silu_sub_p_kernel(tc, x_words, x_scales, w1, w3, w2, g
 
         def down(q0, q1):
             cols = slice(q0 * NQ, q1 * NQ)
-            y = psum.tile([P, (q1 - q0) * NQ], F32, name="y", tag="bank%d" % q0)
+            y = psum.tile([P, (q1 - q0) * NQ], F32, name="y", tag="bank%d" % (4 * (1 - TAGS[(1, 1)]) + q0))
             for g in range(CHUNKS):
                 nc.tensor.matmul_mx(
                     out=y[:],
@@ -199,23 +248,21 @@ def tile_picked_depth_glu_silu_sub_p_kernel(tc, x_words, x_scales, w1, w3, w2, g
                 )
             nc.scalar.copy(y_sb[:, cols], y[:])
 
-        def scatter(u):
-            cols = slice(u * HALF, (u + 1) * HALF)
-            w = HALF // 16
-            nc.vector.tensor_tensor(result[:].indirect(offsets[:, u * w : (u + 1) * w]), y_sb[:, cols], gate_sb[:, cols], MULT)
+        def scatter(q0, q1):
+            cols = slice(q0 * NQ, q1 * NQ)
+            w = NQ // 16
+            nc.vector.tensor_tensor(result[:].indirect(offsets[:, q0 * w : q1 * w]), y_sb[:, cols], gate_sb[:, cols], MULT)
 
         c = CHUNKS - 1
-        gated(c, 0)
-        gated(c, 1)
-        nc.vector.quantize_mx(out=w2_codes[:].bitcast(FP8X4), scales=w2_scales[:], in_=w2_grouped[:].rearrange("p g n j -> p (g n j)"))
-        quant_h(c, 0, 2)
-        down(0, 2)
-        gated(c, 2)
-        gated(c, 3)
-        quant_h(c, 2, 3)
-        down(2, 3)
-        quant_h(c, 3, 4)
-        down(3, 4)
-        scatter(0)
-        scatter(1)
+        for it in TAIL.split():
+            if it[0] == "g":
+                gated(c, int(it[1]))
+            elif it == "w":
+                nc.vector.quantize_mx(out=w2_codes[:].bitcast(FP8X4), scales=w2_scales[:], in_=w2_grouped[:].rearrange("p g n j -> p (g n j)"))
+            elif it[0] == "q":
+                quant_h(c, int(it[1]), int(it[2]))
+            elif it[0] == "d":
+                down(int(it[1]), int(it[2]))
+            else:
+                scatter(int(it[1]), int(it[2]))
         nc.sync.dma_start(out=out, in_=result[:])

@@ -23,12 +23,13 @@ CHUNKS = H // KP
 QUART = 4
 NQ = S // QUART
 HALF = S // 2
-SHARES = (32, 32, 32, 32, 48, 32, 64, 40, 64, 32, 40, 16)
-LOADS = "x0 00 x1 s 01 x2 10 020 110 120 021 111 121"
-GLAG = 3
-SLAG = (0, 2)
-TAIL = "g0 g1 w q02 d02 g2 g3 q23 d23 q34 d34 s02 s24"
-LAST = (256, 128, 128)
+SHARES = (32, 32, 32, 32, 64, 0, 64, 64, 40, 0, 24, 44)
+LOADS = "x0 00 x1 s 01 x2 02 100 110 120 101 111 121"
+GLAG = 0
+PLAIN = 0
+SLAG = (2, 2)
+TAIL = "g0 g1 g2 w q02 d02 g3 q24 d24 s02 s24"
+LAST = (256, 256)
 
 
 def tile_picked_depth_glu_silu_sub_p_kernel(tc, x_words, x_scales, w1, w3, w2, gate, offs, out):
@@ -61,7 +62,7 @@ def tile_picked_depth_glu_silu_sub_p_kernel(tc, x_words, x_scales, w1, w3, w2, g
             raw[key] = []
             col = 0
             for width in widths:
-                tl = keep.tile([P, PACK, width], F32, name="raw%d%d%d_%d" % (mat, g, c, col), align_bytes=64)
+                tl = keep.tile([P, PACK, width], F32, name="raw%d%d%d_%d" % (mat, g, c, col), tag="raw%d%d%d_%d" % (mat, g, c, len(raw[key])), align_bytes=64)
                 nc.sync.dma_start(out=tl[:], in_=rows[:, :, c * KP + col : c * KP + col + width])
                 raw[key].append((tl[:], col // PACK, (col + width) // PACK))
                 col += width
@@ -89,10 +90,13 @@ def tile_picked_depth_glu_silu_sub_p_kernel(tc, x_words, x_scales, w1, w3, w2, g
                 pieces.append(key)
         last = pieces[-1]
         w2_raw = keep.tile([P, CHUNKS, PACK, N], F32, name="w2_raw", align_bytes=64)
-        w2_rows = w2.rearrange("(g a t e) n -> g e a t n", g=CHUNKS, t=PACK, e=2)
-        for g in range(CHUNKS):
-            for e in range(2):
-                nc.sync.dma_start(out=w2_raw[e:P:2, g], in_=w2_rows[g, e])
+        if PLAIN:
+            nc.sync.dma_start(out=w2_raw[:], in_=w2.rearrange("(g p t) n -> p g t n", g=CHUNKS, t=PACK))
+        else:
+            w2_rows = w2.rearrange("(g a t e) n -> g e a t n", g=CHUNKS, t=PACK, e=2)
+            for g in range(CHUNKS):
+                for e in range(2):
+                    nc.sync.dma_start(out=w2_raw[e:P:2, g], in_=w2_rows[g, e])
         gate_sb = keep.tile([P, S], F32, name="gate_sb", align_bytes=64)
         nc.sync.dma_start(out=gate_sb[:], in_=gate)
 
@@ -111,6 +115,9 @@ def tile_picked_depth_glu_silu_sub_p_kernel(tc, x_words, x_scales, w1, w3, w2, g
             for tl, m0, m1 in raw[key]:
                 src = tl.rearrange("p j (a t e) -> p a t j e", t=PACK, e=2)
                 dst = grouped[key][:].rearrange("p t (a e) j -> p a t j e", e=2)[:, m0 // 2 : m1 // 2]
+                if PLAIN:
+                    src = tl.rearrange("p j (a e t) -> p a e j t", t=PACK, e=2)
+                    dst = grouped[key][:].rearrange("p t (a e) j -> p a e j t", e=2)[:, m0 // 2 : m1 // 2]
                 n = (m1 - m0) // 2
                 cut = 2 * ((share * n + 64) // 128)
                 if cut > 0:
@@ -151,7 +158,8 @@ def tile_picked_depth_glu_silu_sub_p_kernel(tc, x_words, x_scales, w1, w3, w2, g
 
         act = [keep.tile([P, QUART, NQ, PACK], F32, name="act%d" % c, align_bytes=64) for c in range(CHUNKS)]
         hb = [keep.tile([P, QUART, NQ, PACK], BF16, name="hb%d" % c, align_bytes=64) for c in range(CHUNKS)]
-        hc = [keep.tile([P, S], U32, name="hc%d" % c, align_bytes=64) for c in range(CHUNKS)]
+        hc1 = keep.tile([P, S], U32, name="hc1", align_bytes=64)
+        hc = {(1, 0): hc1[:, 0:HALF], (1, 1): hc1[:, HALF:S]}
         hs = [keep.tile([P, S], U8, name="hs%d" % c, align_bytes=64) for c in range(CHUNKS)]
 
         def silu(c):
@@ -163,7 +171,7 @@ def tile_picked_depth_glu_silu_sub_p_kernel(tc, x_words, x_scales, w1, w3, w2, g
 
         def quant_h(c, q0, q1):
             cols = slice(q0 * NQ, q1 * NQ)
-            nc.vector.quantize_mx(out=hc[c][:, cols].bitcast(FP8X4), scales=hs[c][:, cols], in_=hb[c][:, q0:q1].rearrange("p q n t -> p (q n t)"))
+            nc.vector.quantize_mx(out=hc[(c, q0 // 2)][:, q0 % 2 * NQ : (q1 - q0 // 2 * 2) * NQ].bitcast(FP8X4), scales=hs[c][:, cols], in_=hb[c][:, q0:q1].rearrange("p q n t -> p (q n t)"))
 
         def gather_words(g):
             nc.vector.tensor_copy(xg[g][:], xw[g][:].bitcast(U32).indirect(offsets[:]))
@@ -221,7 +229,9 @@ def tile_picked_depth_glu_silu_sub_p_kernel(tc, x_words, x_scales, w1, w3, w2, g
             pend.append(key)
             pump()
         assert not pend and not later
-        quant_h(0, 0, QUART)
+        for u in range(2):
+            hc[(0, u)] = keep.tile([P, HALF], U32, name="hc0%d" % u, tag="raw%d%d%d_%d" % (last + (len(LAST) - 2 + u,)), align_bytes=64)[:]
+            quant_h(0, 2 * u, 2 * u + 2)
 
         w2_grouped = keep.tile([P, CHUNKS, N, PACK], BF16, name="w2_grouped", align_bytes=64)
         for g in range(CHUNKS):
@@ -241,7 +251,7 @@ def tile_picked_depth_glu_silu_sub_p_kernel(tc, x_words, x_scales, w1, w3, w2, g
                     out=y[:],
                     lhsT=w2_codes[:, g * N : (g + 1) * N].bitcast(FP8X4),
                     lhsT_scale=w2_scales[:, g * N : (g + 1) * N],
-                    rhs=hc[g][:, cols].bitcast(FP8X4),
+                    rhs=hc[(g, q0 // 2)][:, q0 % 2 * NQ : (q1 - q0 // 2 * 2) * NQ].bitcast(FP8X4),
                     rhs_scale=hs[g][:, cols],
                     start=(g == 0),
                     stop=(g == CHUNKS - 1),

@@ -156,7 +156,7 @@ def tile_picked_depth_glu_silu_sub_p_kernel(tc, x_words, x_scales, w1, w3, w2, g
                         stop=(closes and t == ts[-1]),
                     )
 
-        act = [keep.tile([P, QUART, NQ, PACK], F32, name="act%d" % c, align_bytes=64) for c in range(CHUNKS)]
+        act = [keep.tile([P, QUART, NQ // 2, PACK, 2], F32, name="act%d" % c, align_bytes=64) for c in range(CHUNKS)]
         hb = [keep.tile([P, QUART, NQ, PACK], BF16, name="hb%d" % c, align_bytes=64) for c in range(CHUNKS)]
         hc1 = keep.tile([P, S], U32, name="hc1", align_bytes=64)
         hc = {(1, 0): hc1[:, 0:HALF], (1, 1): hc1[:, HALF:S]}
@@ -164,10 +164,10 @@ def tile_picked_depth_glu_silu_sub_p_kernel(tc, x_words, x_scales, w1, w3, w2, g
 
         def silu(c):
             for q in range(QUART):
-                nc.scalar.activation(act[c][:, q], banks[(0, c, q)][:].rearrange("p t n -> p n t"), SILU)
+                nc.scalar.activation(act[c][:, q], banks[(0, c, q)][:].rearrange("p t (a i) -> p a t i", i=2), SILU)
 
         def gated(c, q):
-            nc.vector.tensor_tensor(hb[c][:, q], banks[(1, c, q)][:].rearrange("p t n -> p n t"), act[c][:, q], MULT)
+            nc.vector.tensor_tensor(hb[c][:, q].rearrange("p (a i) t -> p a t i", i=2), banks[(1, c, q)][:].rearrange("p t (a i) -> p a t i", i=2), act[c][:, q], MULT)
 
         def quant_h(c, q0, q1):
             cols = slice(q0 * NQ, q1 * NQ)

@@ -139,6 +139,21 @@ def tile_picked_depth_glu_silu_sub_p_kernel(tc, x_words, x_scales, w1, w3, w2, g
 
         def multiply(key, ts, opens, closes, half):
             mat, g, c = key
+            if mat == 0:
+                for t in ts:
+                    if opens:
+                        banks[(mat, c, t)] = psum.tile([P, S], F32, name="acc", tag="bank%d" % (half * QUART + t))
+                    mc = slice(t * P, (t + 1) * P)
+                    nc.tensor.matmul_mx(
+                        out=banks[(mat, c, t)][:],
+                        lhsT=codes[key][:, mc].bitcast(FP8X4),
+                        lhsT_scale=scales[key][:, mc],
+                        rhs=xg[g][:].bitcast(FP8X4),
+                        rhs_scale=xsg[4 * g : P, :],
+                        start=opens,
+                        stop=closes,
+                    )
+                return
             if opens:
                 for q in range(QUART):
                     banks[(mat, c, q)] = psum.tile([P, PACK, NQ], F32, name="acc", tag="bank%d" % (half * QUART + q))
@@ -156,7 +171,7 @@ def tile_picked_depth_glu_silu_sub_p_kernel(tc, x_words, x_scales, w1, w3, w2, g
                         stop=(closes and t == ts[-1]),
                     )
 
-        act = [keep.tile([P, QUART, NQ // 2, PACK, 2], F32, name="act%d" % c, align_bytes=64) for c in range(CHUNKS)]
+        act = [keep.tile([P, PACK, S], F32, name="act%d" % c, align_bytes=64) for c in range(CHUNKS)]
         hb = [keep.tile([P, QUART, NQ, PACK], BF16, name="hb%d" % c, align_bytes=64) for c in range(CHUNKS)]
         hc1 = keep.tile([P, S], U32, name="hc1", align_bytes=64)
         hc = {(1, 0): hc1[:, 0:HALF], (1, 1): hc1[:, HALF:S]}
@@ -164,10 +179,10 @@ def tile_picked_depth_glu_silu_sub_p_kernel(tc, x_words, x_scales, w1, w3, w2, g
 
         def silu(c):
             for q in range(QUART):
-                nc.scalar.activation(act[c][:, q], banks[(0, c, q)][:].rearrange("p t (a i) -> p a t i", i=2), SILU)
+                nc.scalar.activation(act[c][:, q], banks[(0, c, q)][:], SILU)
 
         def gated(c, q):
-            nc.vector.tensor_tensor(hb[c][:, q].rearrange("p (a i) t -> p a t i", i=2), banks[(1, c, q)][:].rearrange("p t (a i) -> p a t i", i=2), act[c][:, q], MULT)
+            nc.vector.tensor_tensor(hb[c][:, q].rearrange("p (a i) t -> p a t i", i=2), banks[(1, c, q)][:].rearrange("p t (a i) -> p a t i", i=2), act[c][:, :, q * NQ : (q + 1) * NQ].rearrange("p t (a i) -> p a t i", i=2), MULT)
 
         def quant_h(c, q0, q1):
             cols = slice(q0 * NQ, q1 * NQ)

@@ -20,16 +20,17 @@ PACK = 4
 KP = P * PACK
 PASSES = K // KP
 CHUNKS = H // KP
-QUART = 4
-NQ = S // QUART
+QUARTERS = 4
+NQ = S // QUARTERS
 HALF = S // 2
-SHARES = (32, 32, 32, 32, 64, 0, 64, 64, 40, 0, 24, 44)
-LOADS = "x0 00 x1 s 01 x2 02 100 110 120 101 111 121"
-GLAG = 0
-PLAIN = 0
-SLAG = (2, 2)
-TAIL = "g0 g1 g2 w q02 d02 g3 q24 d24 s02 s24"
-LAST = (256, 256)
+W1, W3 = 0, 1
+
+EVEN = 32
+BALANCED = 44
+ALL_VECTOR = 64
+AFTER_SILU = 24
+BESIDE_GATING = 16
+LAST_PARTS = ((0, 384, BESIDE_GATING), (384, 512, BALANCED))
 
 
 def tile_picked_depth_glu_silu_sub_p_kernel(tc, x_words, x_scales, w1, w3, w2, gate, offs, out):
@@ -42,83 +43,67 @@ def tile_picked_depth_glu_silu_sub_p_kernel(tc, x_words, x_scales, w1, w3, w2, g
         offsets = keep.tile([P, S // 16], U16, name="offsets")
         nc.sync.dma_start(offsets[:], offs)
 
-        warm = keep.tile([P, 8], F32, name="warm")
+        warm_in = keep.tile([P, 8], F32, name="warm_in")
         warm_out = keep.tile([P, 8], F32, name="warm_out")
-        xs = keep.tile([P, T], U8, name="xs", align_bytes=64)
-        nc.gpsimd.memset(xs[:].bitcast(I32), 0)
-        nc.vector.memset(warm[:], 0.0)
-        nc.scalar.activation(warm_out[:], warm[:], SILU)
+        x_scale_rows = keep.tile([P, T], U8, name="x_scale_rows", align_bytes=64)
+        nc.gpsimd.memset(x_scale_rows[:].bitcast(I32), 0)
+        nc.vector.memset(warm_in[:], 0.0)
+        nc.scalar.activation(warm_out[:], warm_in[:], SILU)
 
-        weights = (w1, w3)
-        xw = [keep.tile([P, T], I32, name="xw%d" % g, align_bytes=64) for g in range(PASSES)]
+        x_all = [keep.tile([P, T], I32, name="x_all%d" % g, align_bytes=64) for g in range(PASSES)]
         raw = {}
 
-        def load_x(g):
-            nc.sync.dma_start(out=xw[g][:], in_=x_words[g].rearrange("p n t -> p (n t)").bitcast(I32))
+        def k_rows(w, g):
+            return w[g * KP : (g + 1) * KP, :].rearrange("(p j) h -> p j h", j=PACK)
 
-        def load_w(key, widths):
-            mat, g, c = key
-            rows = weights[mat][g * KP : (g + 1) * KP, :].rearrange("(p j) h -> p j h", j=PACK)
-            raw[key] = []
-            col = 0
-            for width in widths:
-                tl = keep.tile([P, PACK, width], F32, name="raw%d%d%d_%d" % (mat, g, c, col), tag="raw%d%d%d_%d" % (mat, g, c, len(raw[key])), align_bytes=64)
-                nc.sync.dma_start(out=tl[:], in_=rows[:, :, c * KP + col : c * KP + col + width])
-                raw[key].append((tl[:], col // PACK, (col + width) // PACK))
-                col += width
-
-        def load_full(mat, g):
-            rows = weights[mat][g * KP : (g + 1) * KP, :].rearrange("(p j) h -> p j h", j=PACK)
-            tl = keep.tile([P, PACK, H], F32, name="full%d%d" % (mat, g), align_bytes=64)
-            nc.sync.dma_start(out=tl[:], in_=rows)
-            for c in range(CHUNKS):
-                raw[(mat, g, c)] = [(tl[:, :, c * KP : (c + 1) * KP], 0, P)]
-
-        pieces = []
-        for it in LOADS.split():
-            if it[0] == "x":
-                load_x(int(it[1]))
-            elif it == "s":
+        for g in range(PASSES):
+            nc.sync.dma_start(out=x_all[g][:], in_=x_words[g].rearrange("p n t -> p (n t)").bitcast(I32))
+            if g == 1:
                 for q in range(4):
-                    nc.sync.dma_start(out=xs[:].bitcast(I32)[32 * q : 32 * q + 4 * PASSES, :], in_=x_scales[:, 4 * q : 4 * q + 4, :].bitcast(I32))
-            elif len(it) == 2:
-                load_full(int(it[0]), int(it[1]))
-                pieces += [(int(it[0]), int(it[1]), c) for c in range(2)]
-            else:
-                key = tuple(int(v) for v in it)
-                load_w(key, LAST if it == LOADS.split()[-1] else (KP,))
-                pieces.append(key)
-        last = pieces[-1]
+                    nc.sync.dma_start(
+                        out=x_scale_rows[:].bitcast(I32)[32 * q : 32 * q + 4 * PASSES, :],
+                        in_=x_scales[:, 4 * q : 4 * q + 4, :].bitcast(I32),
+                    )
+            wide = keep.tile([P, PACK, H], F32, name="w1_pass%d" % g, align_bytes=64)
+            nc.sync.dma_start(out=wide[:], in_=k_rows(w1, g))
+            for c in range(CHUNKS):
+                raw[(W1, g, c)] = [(wide[:, :, c * KP : (c + 1) * KP], 0, KP)]
+        wide = keep.tile([P, PACK, H], F32, name="w3_pass0", align_bytes=64)
+        nc.sync.dma_start(out=wide[:], in_=k_rows(w3, 0))
+        for c in range(CHUNKS):
+            raw[(W3, 0, c)] = [(wide[:, :, c * KP : (c + 1) * KP], 0, KP)]
+        last = (W3, PASSES - 1, CHUNKS - 1)
+        for c in range(CHUNKS):
+            for g in range(1, PASSES):
+                key = (W3, g, c)
+                raw[key] = []
+                for col0, col1 in [part[:2] for part in LAST_PARTS] if key == last else [(0, KP)]:
+                    tag = "w3_%d%d_%d" % (g, c, col0)
+                    part = keep.tile([P, PACK, col1 - col0], F32, name=tag, tag=tag, align_bytes=64)
+                    nc.sync.dma_start(out=part[:], in_=k_rows(w3, g)[:, :, c * KP + col0 : c * KP + col1])
+                    raw[key].append((part[:], col0, col1))
         w2_raw = keep.tile([P, CHUNKS, PACK, N], F32, name="w2_raw", align_bytes=64)
-        if PLAIN:
-            nc.sync.dma_start(out=w2_raw[:], in_=w2.rearrange("(g p t) n -> p g t n", g=CHUNKS, t=PACK))
-        else:
-            w2_rows = w2.rearrange("(g a t e) n -> g e a t n", g=CHUNKS, t=PACK, e=2)
-            for g in range(CHUNKS):
-                for e in range(2):
-                    nc.sync.dma_start(out=w2_raw[e:P:2, g], in_=w2_rows[g, e])
+        w2_rows = w2.rearrange("(c a t e) n -> c e a t n", c=CHUNKS, t=PACK, e=2)
+        for c in range(CHUNKS):
+            for e in range(2):
+                nc.sync.dma_start(out=w2_raw[e:P:2, c], in_=w2_rows[c, e])
         gate_sb = keep.tile([P, S], F32, name="gate_sb", align_bytes=64)
         nc.sync.dma_start(out=gate_sb[:], in_=gate)
 
         result = keep.tile([P, T], F32, name="result", align_bytes=64)
         nc.vector.memset(result[:], 0.0)
 
-        xg = [keep.tile([P, S], U32, name="xg%d" % g, align_bytes=64) for g in range(PASSES)]
-        xsg = keep.tile([P, S], U8, name="xsg", align_bytes=64)
+        x_picked = [keep.tile([P, S], U32, name="x_picked%d" % g, align_bytes=64) for g in range(PASSES)]
+        x_picked_scales = keep.tile([P, S], U8, name="x_picked_scales", align_bytes=64)
 
-        grouped = {}
-        codes = {}
-        scales = {}
+        rounded, codes, scales, banks = {}, {}, {}, {}
 
-        def cast(key, share):
-            grouped[key] = stage.tile([P, PACK, P, PACK], BF16, name="grouped", align_bytes=64)
-            for tl, m0, m1 in raw[key]:
-                src = tl.rearrange("p j (a t e) -> p a t j e", t=PACK, e=2)
-                dst = grouped[key][:].rearrange("p t (a e) j -> p a t j e", e=2)[:, m0 // 2 : m1 // 2]
-                if PLAIN:
-                    src = tl.rearrange("p j (a e t) -> p a e j t", t=PACK, e=2)
-                    dst = grouped[key][:].rearrange("p t (a e) j -> p a e j t", e=2)[:, m0 // 2 : m1 // 2]
-                n = (m1 - m0) // 2
+        def round_piece(key, *shares):
+            rounded[key] = stage.tile([P, PACK, P, PACK], BF16, name="rounded", align_bytes=64)
+            for (view, col0, col1), share in zip(raw[key], shares):
+                src = view.rearrange("p j (a t e) -> p a t j e", t=PACK, e=2)
+                dst = rounded[key][:].rearrange("p t (a e) j -> p a t j e", e=2)[:, col0 // 8 : col1 // 8]
+                n = (col1 - col0) // 8
                 cut = 2 * ((share * n + 64) // 128)
                 if cut > 0:
                     nc.vector.tensor_copy(dst[:, 0:cut], src[:, 0:cut])
@@ -127,167 +112,135 @@ def tile_picked_depth_glu_silu_sub_p_kernel(tc, x_words, x_scales, w1, w3, w2, g
             codes[key] = keep.tile([P, KP], U32, name="codes%d%d%d" % key, align_bytes=64)
             scales[key] = keep.tile([P, KP], U8, name="scales%d%d%d" % key, align_bytes=64)
 
-        def quant(key, t0, t1):
+        def quantise(key, t0, t1):
             cols = slice(t0 * P, t1 * P)
             nc.vector.quantize_mx(
                 out=codes[key][:, cols].bitcast(FP8X4),
                 scales=scales[key][:, cols],
-                in_=grouped[key][:, t0:t1].rearrange("p t m j -> p (t m j)"),
+                in_=rounded[key][:, t0:t1].rearrange("p t m j -> p (t m j)"),
             )
 
-        banks = {}
+        def prepare(key, share):
+            round_piece(key, share)
+            quantise(key, 0, PACK)
 
-        def multiply(key, ts, opens, closes, half):
-            mat, g, c = key
-            if mat == 0:
+        def matmul(acc, key, t, cols, start, stop):
+            g = key[1]
+            mc = slice(t * P, (t + 1) * P)
+            nc.tensor.matmul_mx(
+                out=acc,
+                lhsT=codes[key][:, mc].bitcast(FP8X4),
+                lhsT_scale=scales[key][:, mc],
+                rhs=x_picked[g][:, cols].bitcast(FP8X4),
+                rhs_scale=x_picked_scales[4 * g : P, cols],
+                start=start,
+                stop=stop,
+            )
+
+        def multiply_w1(g, c):
+            for t in range(PACK):
+                if g == 0:
+                    banks[(W1, c, t)] = psum.tile([P, S], F32, name="acc", tag="bank%d" % (c * PACK + t))
+                matmul(banks[(W1, c, t)][:], (W1, g, c), t, slice(0, S), g == 0, g == PASSES - 1)
+
+        def multiply_w3(g, c, ts=range(PACK)):
+            if g == 0:
+                for q in range(QUARTERS):
+                    banks[(W3, c, q)] = psum.tile([P, PACK, NQ], F32, name="acc", tag="bank%d" % (c * QUARTERS + q))
+            for q in range(QUARTERS):
                 for t in ts:
-                    if opens:
-                        banks[(mat, c, t)] = psum.tile([P, S], F32, name="acc", tag="bank%d" % (half * QUART + t))
-                    mc = slice(t * P, (t + 1) * P)
-                    nc.tensor.matmul_mx(
-                        out=banks[(mat, c, t)][:],
-                        lhsT=codes[key][:, mc].bitcast(FP8X4),
-                        lhsT_scale=scales[key][:, mc],
-                        rhs=xg[g][:].bitcast(FP8X4),
-                        rhs_scale=xsg[4 * g : P, :],
-                        start=opens,
-                        stop=closes,
-                    )
-                return
-            if opens:
-                for q in range(QUART):
-                    banks[(mat, c, q)] = psum.tile([P, PACK, NQ], F32, name="acc", tag="bank%d" % (half * QUART + q))
-            for q in range(QUART):
-                cols = slice(q * NQ, (q + 1) * NQ)
-                for t in ts:
-                    mc = slice(t * P, (t + 1) * P)
-                    nc.tensor.matmul_mx(
-                        out=banks[(mat, c, q)][:, t, :],
-                        lhsT=codes[key][:, mc].bitcast(FP8X4),
-                        lhsT_scale=scales[key][:, mc],
-                        rhs=xg[g][:, cols].bitcast(FP8X4),
-                        rhs_scale=xsg[4 * g : P, cols],
-                        start=(opens and t == ts[0]),
-                        stop=(closes and t == ts[-1]),
-                    )
+                    first, final = g == 0 and t == ts[0], g == PASSES - 1 and t == ts[-1]
+                    matmul(banks[(W3, c, q)][:, t, :], (W3, g, c), t, slice(q * NQ, (q + 1) * NQ), first, final)
 
         act = [keep.tile([P, PACK, S], F32, name="act%d" % c, align_bytes=64) for c in range(CHUNKS)]
-        hb = [keep.tile([P, QUART, NQ, PACK], BF16, name="hb%d" % c, align_bytes=64) for c in range(CHUNKS)]
-        hc1 = keep.tile([P, S], U32, name="hc1", align_bytes=64)
-        hc = {(1, 0): hc1[:, 0:HALF], (1, 1): hc1[:, HALF:S]}
-        hs = [keep.tile([P, S], U8, name="hs%d" % c, align_bytes=64) for c in range(CHUNKS)]
+        h = [keep.tile([P, QUARTERS, NQ, PACK], BF16, name="h%d" % c, align_bytes=64) for c in range(CHUNKS)]
+        h_codes1 = keep.tile([P, S], U32, name="h_codes1", align_bytes=64)
+        h_codes = {(1, u): h_codes1[:, u * HALF : (u + 1) * HALF] for u in range(2)}
+        h_scales = [keep.tile([P, S], U8, name="h_scales%d" % c, align_bytes=64) for c in range(CHUNKS)]
 
         def silu(c):
-            for q in range(QUART):
-                nc.scalar.activation(act[c][:, q], banks[(0, c, q)][:], SILU)
+            for t in range(PACK):
+                nc.scalar.activation(act[c][:, t], banks[(W1, c, t)][:], SILU)
 
         def gated(c, q):
-            nc.vector.tensor_tensor(hb[c][:, q].rearrange("p (a i) t -> p a t i", i=2), banks[(1, c, q)][:].rearrange("p t (a i) -> p a t i", i=2), act[c][:, :, q * NQ : (q + 1) * NQ].rearrange("p t (a i) -> p a t i", i=2), MULT)
+            nc.vector.tensor_tensor(
+                h[c][:, q].rearrange("p (a i) t -> p a t i", i=2),
+                banks[(W3, c, q)][:].rearrange("p t (a i) -> p a t i", i=2),
+                act[c][:, :, q * NQ : (q + 1) * NQ].rearrange("p t (a i) -> p a t i", i=2),
+                MULT,
+            )
 
-        def quant_h(c, q0, q1):
-            cols = slice(q0 * NQ, q1 * NQ)
-            nc.vector.quantize_mx(out=hc[(c, q0 // 2)][:, q0 % 2 * NQ : (q1 - q0 // 2 * 2) * NQ].bitcast(FP8X4), scales=hs[c][:, cols], in_=hb[c][:, q0:q1].rearrange("p q n t -> p (q n t)"))
-
-        def gather_words(g):
-            nc.vector.tensor_copy(xg[g][:], xw[g][:].bitcast(U32).indirect(offsets[:]))
+        def quantise_h(c, u):
+            nc.vector.quantize_mx(
+                out=h_codes[(c, u)].bitcast(FP8X4),
+                scales=h_scales[c][:, u * HALF : (u + 1) * HALF],
+                in_=h[c][:, 2 * u : 2 * u + 2].rearrange("p q n t -> p (q n t)"),
+            )
 
         for g in range(PASSES):
-            gather_words(g)
-        nc.vector.tensor_copy(xsg[:], xs[:].indirect(offsets[:]))
-        TAGS = {}
-        free = [0, 1]
-        pend = []
-        ndone = {}
-        later = []
+            nc.vector.tensor_copy(x_picked[g][:], x_all[g][:].bitcast(U32).indirect(offsets[:]))
+        nc.vector.tensor_copy(x_picked_scales[:], x_scale_rows[:].indirect(offsets[:]))
 
-        def pump():
-            again = True
-            while again:
-                again = False
-                for key in list(pend):
-                    mat, g, c = key
-                    if (mat, c) not in TAGS:
-                        if not free or (mat == 1 and (0, c) not in TAGS) or (c == 1 and (mat, 0) not in TAGS):
-                            continue
-                        TAGS[(mat, c)] = free.pop(0)
-                    n = ndone.get((mat, c), 0)
-                    pend.remove(key)
-                    multiply(key, range(PACK) if key != last else (2, 3, 0, 1), n == 0, n == PASSES - 1, TAGS[(mat, c)])
-                    ndone[(mat, c)] = n + 1
-                    if n == PASSES - 1 and key != last:
-                        later.append([SLAG[c] if mat == 0 else GLAG, mat, c])
-                for ent in list(later):
-                    if ent[0] <= 0 and (ent[1] == 0 or ent[2] in silued):
-                        later.remove(ent)
-                        if ent[1] == 0:
-                            silu(ent[2])
-                            silued.append(ent[2])
-                        else:
-                            for q in range(QUART):
-                                gated(ent[2], q)
-                        free.append(TAGS[(ent[1], ent[2])])
-                        again = True
-
-        silued = []
-        for i, key in enumerate(pieces):
-            cast(key, SHARES[i])
-            if key == last:
-                for ent in later:
-                    ent[0] = 0
-                pump()
-                quant(key, 2, 4)
-                quant(key, 0, 2)
-            else:
-                quant(key, 0, PACK)
-            for ent in later:
-                ent[0] -= 1
-            pend.append(key)
-            pump()
-        assert not pend and not later
+        for g in range(PASSES):
+            for c in range(CHUNKS):
+                prepare((W1, g, c), EVEN if g < PASSES - 1 else BALANCED)
+                multiply_w1(g, c)
+                if (g, c) == (PASSES - 1, 0):
+                    silu(0)
+        prepare((W3, 0, 0), ALL_VECTOR)
+        multiply_w3(0, 0)
+        prepare((W3, 0, 1), BALANCED)
+        silu(1)
+        multiply_w3(0, 1)
+        for g, c, share in ((1, 0, ALL_VECTOR), (2, 0, AFTER_SILU), (1, 1, EVEN)):
+            prepare((W3, g, c), share)
+            multiply_w3(g, c)
+        round_piece(last, *[part[2] for part in LAST_PARTS])
+        for q in range(QUARTERS):
+            gated(0, q)
+        quantise(last, 2, 4)
+        quantise(last, 0, 2)
+        multiply_w3(last[1], last[2], (2, 3, 0, 1))
         for u in range(2):
-            hc[(0, u)] = keep.tile([P, HALF], U32, name="hc0%d" % u, tag="raw%d%d%d_%d" % (last + (len(LAST) - 2 + u,)), align_bytes=64)[:]
-            quant_h(0, 2 * u, 2 * u + 2)
+            tag = "w3_%d%d_%d" % (last[1], last[2], LAST_PARTS[u][0])
+            h_codes[(0, u)] = keep.tile([P, HALF], U32, name="h_codes0%d" % u, tag=tag, align_bytes=64)[:]
+            quantise_h(0, u)
 
-        w2_grouped = keep.tile([P, CHUNKS, N, PACK], BF16, name="w2_grouped", align_bytes=64)
-        for g in range(CHUNKS):
+        w2_rounded = keep.tile([P, CHUNKS, N, PACK], BF16, name="w2_rounded", align_bytes=64)
+        for c in range(CHUNKS):
             nc.scalar.copy(
-                w2_grouped[:, g].rearrange("p (c i) j -> p c j i", i=4),
-                w2_raw[:, g].rearrange("p j (c i) -> p c j i", i=4),
+                w2_rounded[:, c].rearrange("p (b i) t -> p b t i", i=4),
+                w2_raw[:, c].rearrange("p t (b i) -> p b t i", i=4),
             )
         w2_codes = keep.tile([P, CHUNKS * N], U32, name="w2_codes", align_bytes=64)
         w2_scales = keep.tile([P, CHUNKS * N], U8, name="w2_scales", align_bytes=64)
         y_sb = keep.tile([P, S], F32, name="y_sb", align_bytes=64)
 
-        def down(q0, q1):
-            cols = slice(q0 * NQ, q1 * NQ)
-            y = psum.tile([P, (q1 - q0) * NQ], F32, name="y", tag="bank%d" % (4 * (1 - TAGS[(1, 1)]) + q0))
-            for g in range(CHUNKS):
+        def down(u):
+            cols = slice(u * HALF, (u + 1) * HALF)
+            y = psum.tile([P, HALF], F32, name="y", tag="bank%d" % (2 * u))
+            for c in range(CHUNKS):
                 nc.tensor.matmul_mx(
                     out=y[:],
-                    lhsT=w2_codes[:, g * N : (g + 1) * N].bitcast(FP8X4),
-                    lhsT_scale=w2_scales[:, g * N : (g + 1) * N],
-                    rhs=hc[(g, q0 // 2)][:, q0 % 2 * NQ : (q1 - q0 // 2 * 2) * NQ].bitcast(FP8X4),
-                    rhs_scale=hs[g][:, cols],
-                    start=(g == 0),
-                    stop=(g == CHUNKS - 1),
+                    lhsT=w2_codes[:, c * N : (c + 1) * N].bitcast(FP8X4),
+                    lhsT_scale=w2_scales[:, c * N : (c + 1) * N],
+                    rhs=h_codes[(c, u)].bitcast(FP8X4),
+                    rhs_scale=h_scales[c][:, cols],
+                    start=(c == 0),
+                    stop=(c == CHUNKS - 1),
                 )
             nc.scalar.copy(y_sb[:, cols], y[:])
 
-        def scatter(q0, q1):
-            cols = slice(q0 * NQ, q1 * NQ)
-            w = NQ // 16
-            nc.vector.tensor_tensor(result[:].indirect(offsets[:, q0 * w : q1 * w]), y_sb[:, cols], gate_sb[:, cols], MULT)
-
-        c = CHUNKS - 1
-        for it in TAIL.split():
-            if it[0] == "g":
-                gated(c, int(it[1]))
-            elif it == "w":
-                nc.vector.quantize_mx(out=w2_codes[:].bitcast(FP8X4), scales=w2_scales[:], in_=w2_grouped[:].rearrange("p g n j -> p (g n j)"))
-            elif it[0] == "q":
-                quant_h(c, int(it[1]), int(it[2]))
-            elif it[0] == "d":
-                down(int(it[1]), int(it[2]))
-            else:
-                scatter(int(it[1]), int(it[2]))
+        for q in range(QUARTERS - 1):
+            gated(1, q)
+        nc.vector.quantize_mx(out=w2_codes[:].bitcast(FP8X4), scales=w2_scales[:], in_=w2_rounded[:].rearrange("p c n t -> p (c n t)"))
+        quantise_h(1, 0)
+        down(0)
+        gated(1, QUARTERS - 1)
+        quantise_h(1, 1)
+        down(1)
+        for u in range(2):
+            cols = slice(u * HALF, (u + 1) * HALF)
+            picked = offsets[:, u * HALF // 16 : (u + 1) * HALF // 16]
+            nc.vector.tensor_tensor(result[:].indirect(picked), y_sb[:, cols], gate_sb[:, cols], MULT)
         nc.sync.dma_start(out=out, in_=result[:])

@@ -28,9 +28,10 @@ W1, W3 = 0, 1
 EVEN = 32
 BALANCED = 44
 ALL_VECTOR = 64
-AFTER_SILU = 24
+BEFORE_SILU = 24
+AFTER_SILU = 36
 BESIDE_GATING = 16
-LAST_PARTS = ((0, 384, BESIDE_GATING), (384, 512, BALANCED))
+LAST_PARTS = ((0, 384, BESIDE_GATING), (384, 512, 40))
 
 
 def tile_picked_depth_glu_silu_sub_p_kernel(tc, x_words, x_scales, w1, w3, w2, gate, offs, out):
@@ -98,18 +99,20 @@ def tile_picked_depth_glu_silu_sub_p_kernel(tc, x_words, x_scales, w1, w3, w2, g
 
         rounded, codes, scales, banks = {}, {}, {}, {}
 
-        def round_piece(key, *shares):
+        def round_piece(key, *shares, first=0, codes_tag=None):
             rounded[key] = stage.tile([P, PACK, P, PACK], BF16, name="rounded", align_bytes=64)
             for (view, col0, col1), share in zip(raw[key], shares):
                 src = view.rearrange("p j (a t e) -> p a t j e", t=PACK, e=2)
                 dst = rounded[key][:].rearrange("p t (a e) j -> p a t j e", e=2)[:, col0 // 8 : col1 // 8]
                 n = (col1 - col0) // 8
                 cut = 2 * ((share * n + 64) // 128)
-                if cut > 0:
-                    nc.vector.tensor_copy(dst[:, 0:cut], src[:, 0:cut])
+                if first > 0:
+                    nc.vector.tensor_copy(dst[:, 0:first], src[:, 0:first])
+                if cut > first:
+                    nc.vector.tensor_copy(dst[:, first:cut], src[:, first:cut])
                 if cut < n:
                     nc.scalar.copy(dst[:, cut:n], src[:, cut:n])
-            codes[key] = keep.tile([P, KP], U32, name="codes%d%d%d" % key, align_bytes=64)
+            codes[key] = keep.tile([P, KP], U32, name="codes%d%d%d" % key, tag=codes_tag or "codes%d%d%d" % key, align_bytes=64)
             scales[key] = keep.tile([P, KP], U8, name="scales%d%d%d" % key, align_bytes=64)
 
         def quantise(key, t0, t1):
@@ -183,27 +186,30 @@ def tile_picked_depth_glu_silu_sub_p_kernel(tc, x_words, x_scales, w1, w3, w2, g
 
         for g in range(PASSES):
             for c in range(CHUNKS):
-                prepare((W1, g, c), EVEN if g < PASSES - 1 else BALANCED)
+                prepare((W1, g, c), EVEN if g < PASSES - 1 else (BALANCED, BEFORE_SILU)[c])
                 multiply_w1(g, c)
-                if (g, c) == (PASSES - 1, 0):
-                    silu(0)
+                if g == PASSES - 1:
+                    silu(c)
         prepare((W3, 0, 0), ALL_VECTOR)
         multiply_w3(0, 0)
-        prepare((W3, 0, 1), BALANCED)
-        silu(1)
+        round_piece((W3, 0, 1), ALL_VECTOR, first=16, codes_tag="w3_20_0")
+        for g in range(1, PASSES):
+            prepare((W3, g, 0), AFTER_SILU)
+            multiply_w3(g, 0)
+        quantise((W3, 0, 1), 0, PACK)
         multiply_w3(0, 1)
-        for g, c, share in ((1, 0, ALL_VECTOR), (2, 0, AFTER_SILU), (1, 1, EVEN)):
-            prepare((W3, g, c), share)
-            multiply_w3(g, c)
+        prepare((W3, 1, 1), BESIDE_GATING)
+        multiply_w3(1, 1)
         round_piece(last, *[part[2] for part in LAST_PARTS])
         for q in range(QUARTERS):
             gated(0, q)
         quantise(last, 2, 4)
         quantise(last, 0, 2)
         multiply_w3(last[1], last[2], (2, 3, 0, 1))
+        tag = "w3_%d%d_%d" % (last[1], last[2], LAST_PARTS[-1][0])
+        h_codes0 = keep.tile([P, S], U32, name="h_codes0", tag=tag, align_bytes=64)
         for u in range(2):
-            tag = "w3_%d%d_%d" % (last[1], last[2], LAST_PARTS[u][0])
-            h_codes[(0, u)] = keep.tile([P, HALF], U32, name="h_codes0%d" % u, tag=tag, align_bytes=64)[:]
+            h_codes[(0, u)] = h_codes0[:, u * HALF : (u + 1) * HALF]
             quantise_h(0, u)
 
         w2_rounded = keep.tile([P, CHUNKS, N, PACK], BF16, name="w2_rounded", align_bytes=64)

@@ -42,7 +42,6 @@ def tile_picked_depth_glu_silu_sub_p_kernel(tc, x_words, x_scales, w1, w3, w2, g
         psum = ctx.enter_context(tc.psum_pool(name="psum", bufs=1))
 
         offsets = keep.tile([P, S // 16], U16, name="offsets")
-        nc.sync.dma_start(offsets[:], offs)
 
         warm_in = keep.tile([P, 8], F32, name="warm_in")
         warm_out = keep.tile([P, 8], F32, name="warm_out")
@@ -59,6 +58,8 @@ def tile_picked_depth_glu_silu_sub_p_kernel(tc, x_words, x_scales, w1, w3, w2, g
 
         for g in range(PASSES):
             nc.sync.dma_start(out=x_all[g][:], in_=x_words[g].rearrange("p n t -> p (n t)").bitcast(I32))
+            if g == 0:
+                nc.sync.dma_start(offsets[:], offs)
             if g == 1:
                 for q in range(4):
                     nc.sync.dma_start(
@@ -157,8 +158,7 @@ def tile_picked_depth_glu_silu_sub_p_kernel(tc, x_words, x_scales, w1, w3, w2, g
 
         act = [keep.tile([P, PACK, S], F32, name="act%d" % c, align_bytes=64) for c in range(CHUNKS)]
         h = [keep.tile([P, QUARTERS, NQ, PACK], BF16, name="h%d" % c, align_bytes=64) for c in range(CHUNKS)]
-        h_codes1 = keep.tile([P, S], U32, name="h_codes1", align_bytes=64)
-        h_codes = {(1, u): h_codes1[:, u * HALF : (u + 1) * HALF] for u in range(2)}
+        h_codes = {1: keep.tile([P, S], U32, name="h_codes1", align_bytes=64)}
         h_scales = [keep.tile([P, S], U8, name="h_scales%d" % c, align_bytes=64) for c in range(CHUNKS)]
 
         def silu(c):
@@ -173,11 +173,12 @@ def tile_picked_depth_glu_silu_sub_p_kernel(tc, x_words, x_scales, w1, w3, w2, g
                 MULT,
             )
 
-        def quantise_h(c, u):
+        def quantise_h(c, q0, q1):
+            cols = slice(q0 * NQ, q1 * NQ)
             nc.vector.quantize_mx(
-                out=h_codes[(c, u)].bitcast(FP8X4),
-                scales=h_scales[c][:, u * HALF : (u + 1) * HALF],
-                in_=h[c][:, 2 * u : 2 * u + 2].rearrange("p q n t -> p (q n t)"),
+                out=h_codes[c][:, cols].bitcast(FP8X4),
+                scales=h_scales[c][:, cols],
+                in_=h[c][:, q0:q1].rearrange("p q n t -> p (q n t)"),
             )
 
         for g in range(PASSES):
@@ -207,10 +208,9 @@ def tile_picked_depth_glu_silu_sub_p_kernel(tc, x_words, x_scales, w1, w3, w2, g
         quantise(last, 0, 2)
         multiply_w3(last[1], last[2], (2, 3, 0, 1))
         tag = "w3_%d%d_%d" % (last[1], last[2], LAST_PARTS[-1][0])
-        h_codes0 = keep.tile([P, S], U32, name="h_codes0", tag=tag, align_bytes=64)
+        h_codes[0] = keep.tile([P, S], U32, name="h_codes0", tag=tag, align_bytes=64)
         for u in range(2):
-            h_codes[(0, u)] = h_codes0[:, u * HALF : (u + 1) * HALF]
-            quantise_h(0, u)
+            quantise_h(0, 2 * u, 2 * u + 2)
 
         w2_rounded = keep.tile([P, CHUNKS, N, PACK], BF16, name="w2_rounded", align_bytes=64)
         for c in range(CHUNKS):
@@ -222,31 +222,34 @@ def tile_picked_depth_glu_silu_sub_p_kernel(tc, x_words, x_scales, w1, w3, w2, g
         w2_scales = keep.tile([P, CHUNKS * N], U8, name="w2_scales", align_bytes=64)
         y_sb = keep.tile([P, S], F32, name="y_sb", align_bytes=64)
 
-        def down(u):
-            cols = slice(u * HALF, (u + 1) * HALF)
-            y = psum.tile([P, HALF], F32, name="y", tag="bank%d" % (2 * u))
+        def down(q0, q1):
+            cols = slice(q0 * NQ, q1 * NQ)
+            y = psum.tile([P, (q1 - q0) * NQ], F32, name="y", tag="bank%d" % q0)
             for c in range(CHUNKS):
                 nc.tensor.matmul_mx(
                     out=y[:],
                     lhsT=w2_codes[:, c * N : (c + 1) * N].bitcast(FP8X4),
                     lhsT_scale=w2_scales[:, c * N : (c + 1) * N],
-                    rhs=h_codes[(c, u)].bitcast(FP8X4),
+                    rhs=h_codes[c][:, cols].bitcast(FP8X4),
                     rhs_scale=h_scales[c][:, cols],
                     start=(c == 0),
                     stop=(c == CHUNKS - 1),
                 )
             nc.scalar.copy(y_sb[:, cols], y[:])
 
-        for q in range(QUARTERS - 1):
-            gated(1, q)
+        def scatter(j0, j1):
+            nc.vector.tensor_tensor(result[:].indirect(offsets[:, j0 // 16 : j1 // 16]), y_sb[:, j0:j1], gate_sb[:, j0:j1], MULT)
+
+        gated(1, 0)
+        gated(1, 1)
         nc.vector.quantize_mx(out=w2_codes[:].bitcast(FP8X4), scales=w2_scales[:], in_=w2_rounded[:].rearrange("p c n t -> p (c n t)"))
-        quantise_h(1, 0)
-        down(0)
-        gated(1, QUARTERS - 1)
-        quantise_h(1, 1)
-        down(1)
+        quantise_h(1, 0, 2)
+        down(0, 2)
+        gated(1, 2)
+        gated(1, 3)
+        quantise_h(1, 2, 3)
+        quantise_h(1, 3, 4)
+        down(2, 4)
         for u in range(2):
-            cols = slice(u * HALF, (u + 1) * HALF)
-            picked = offsets[:, u * HALF // 16 : (u + 1) * HALF // 16]
-            nc.vector.tensor_tensor(result[:].indirect(picked), y_sb[:, cols], gate_sb[:, cols], MULT)
+            scatter(u * HALF, (u + 1) * HALF)
         nc.sync.dma_start(out=out, in_=result[:])

@@ -29,7 +29,8 @@ EVEN = 32
 BALANCED = 44
 ALL_VECTOR = 64
 BEFORE_SILU = 24
-AFTER_SILU = 36
+AFTER_SILU = 40
+CHUNK_END = 36
 BESIDE_GATING = 16
 LAST_PARTS = ((0, 384, BESIDE_GATING), (384, 512, 40))
 
@@ -100,17 +101,15 @@ def tile_picked_depth_glu_silu_sub_p_kernel(tc, x_words, x_scales, w1, w3, w2, g
 
         rounded, codes, scales, banks = {}, {}, {}, {}
 
-        def round_piece(key, *shares, first=0, codes_tag=None):
+        def round_piece(key, *shares, codes_tag=None):
             rounded[key] = stage.tile([P, PACK, P, PACK], BF16, name="rounded", align_bytes=64)
             for (view, col0, col1), share in zip(raw[key], shares):
                 src = view.rearrange("p j (a t e) -> p a t j e", t=PACK, e=2)
                 dst = rounded[key][:].rearrange("p t (a e) j -> p a t j e", e=2)[:, col0 // 8 : col1 // 8]
                 n = (col1 - col0) // 8
                 cut = 2 * ((share * n + 64) // 128)
-                if first > 0:
-                    nc.vector.tensor_copy(dst[:, 0:first], src[:, 0:first])
-                if cut > first:
-                    nc.vector.tensor_copy(dst[:, first:cut], src[:, first:cut])
+                if cut > 0:
+                    nc.vector.tensor_copy(dst[:, 0:cut], src[:, 0:cut])
                 if cut < n:
                     nc.scalar.copy(dst[:, cut:n], src[:, cut:n])
             codes[key] = keep.tile([P, KP], U32, name="codes%d%d%d" % key, tag=codes_tag or "codes%d%d%d" % key, align_bytes=64)
@@ -193,9 +192,9 @@ def tile_picked_depth_glu_silu_sub_p_kernel(tc, x_words, x_scales, w1, w3, w2, g
                     silu(c)
         prepare((W3, 0, 0), ALL_VECTOR)
         multiply_w3(0, 0)
-        round_piece((W3, 0, 1), ALL_VECTOR, first=16, codes_tag="w3_20_0")
+        round_piece((W3, 0, 1), AFTER_SILU, codes_tag="w3_20_0")
         for g in range(1, PASSES):
-            prepare((W3, g, 0), AFTER_SILU)
+            prepare((W3, g, 0), ALL_VECTOR if g == 1 else CHUNK_END)
             multiply_w3(g, 0)
         quantise((W3, 0, 1), 0, PACK)
         multiply_w3(0, 1)

@@ -86,10 +86,7 @@ def tile_picked_depth_glu_silu_sub_p_kernel(tc, x_words, x_scales, w1, w3, w2, g
                     nc.sync.dma_start(out=part[:], in_=k_rows(w3, g)[:, :, c * KP + col0 : c * KP + col1])
                     raw[key].append((part[:], col0, col1))
         w2_raw = keep.tile([P, CHUNKS, PACK, N], F32, name="w2_raw", align_bytes=64)
-        w2_rows = w2.rearrange("(c a t e) n -> c e a t n", c=CHUNKS, t=PACK, e=2)
-        for c in range(CHUNKS):
-            for e in range(2):
-                nc.sync.dma_start(out=w2_raw[e:P:2, c], in_=w2_rows[c, e])
+        nc.sync.dma_start(out=w2_raw[:], in_=w2.rearrange("(c p t) n -> p c t n", c=CHUNKS, t=PACK))
         gate_sb = keep.tile([P, S], F32, name="gate_sb", align_bytes=64)
         nc.sync.dma_start(out=gate_sb[:], in_=gate)
 
@@ -104,10 +101,10 @@ def tile_picked_depth_glu_silu_sub_p_kernel(tc, x_words, x_scales, w1, w3, w2, g
         def round_piece(key, *shares, codes_tag=None):
             rounded[key] = stage.tile([P, PACK, P, PACK], BF16, name="rounded", align_bytes=64)
             for (view, col0, col1), share in zip(raw[key], shares):
-                src = view.rearrange("p j (a t e) -> p a t j e", t=PACK, e=2)
-                dst = rounded[key][:].rearrange("p t (a e) j -> p a t j e", e=2)[:, col0 // 8 : col1 // 8]
-                n = (col1 - col0) // 8
-                cut = 2 * ((share * n + 64) // 128)
+                src = view.rearrange("p j (m u v) -> p m u j v", u=2, v=2)
+                dst = rounded[key][:].rearrange("p (u v) m j -> p m u j v", v=2)[:, col0 // 4 : col1 // 4]
+                n = (col1 - col0) // 4
+                cut = 4 * ((share * n + 128) // 256)
                 if cut > 0:
                     nc.vector.tensor_copy(dst[:, 0:cut], src[:, 0:cut])
                 if cut < n:
@@ -157,7 +154,7 @@ def tile_picked_depth_glu_silu_sub_p_kernel(tc, x_words, x_scales, w1, w3, w2, g
 
         act = [keep.tile([P, PACK, S], F32, name="act%d" % c, align_bytes=64) for c in range(CHUNKS)]
         h = [keep.tile([P, QUARTERS, NQ, PACK], BF16, name="h%d" % c, align_bytes=64) for c in range(CHUNKS)]
-        h_codes = {1: keep.tile([P, S], U32, name="h_codes1", align_bytes=64)}
+        h_codes = {(1, u): keep.tile([P, HALF], U32, name="h_codes1%d" % u, align_bytes=64) for u in range(2)}
         h_scales = [keep.tile([P, S], U8, name="h_scales%d" % c, align_bytes=64) for c in range(CHUNKS)]
 
         def silu(c):
@@ -172,12 +169,11 @@ def tile_picked_depth_glu_silu_sub_p_kernel(tc, x_words, x_scales, w1, w3, w2, g
                 MULT,
             )
 
-        def quantise_h(c, q0, q1):
-            cols = slice(q0 * NQ, q1 * NQ)
+        def quantise_h(c, u):
             nc.vector.quantize_mx(
-                out=h_codes[c][:, cols].bitcast(FP8X4),
-                scales=h_scales[c][:, cols],
-                in_=h[c][:, q0:q1].rearrange("p q n t -> p (q n t)"),
+                out=h_codes[(c, u)][:].bitcast(FP8X4),
+                scales=h_scales[c][:, u * HALF : (u + 1) * HALF],
+                in_=h[c][:, 2 * u : 2 * u + 2].rearrange("p q n t -> p (q n t)"),
             )
 
         for g in range(PASSES):
@@ -207,9 +203,8 @@ def tile_picked_depth_glu_silu_sub_p_kernel(tc, x_words, x_scales, w1, w3, w2, g
         quantise(last, 0, 2)
         multiply_w3(last[1], last[2], (2, 3, 0, 1))
         tag = "w3_%d%d_%d" % (last[1], last[2], LAST_PARTS[-1][0])
-        h_codes[0] = keep.tile([P, S], U32, name="h_codes0", tag=tag, align_bytes=64)
-        for u in range(2):
-            quantise_h(0, 2 * u, 2 * u + 2)
+        h_codes[(0, 0)] = keep.tile([P, HALF], U32, name="h_codes00", tag=tag, align_bytes=64)
+        quantise_h(0, 0)
 
         w2_rounded = keep.tile([P, CHUNKS, N, PACK], BF16, name="w2_rounded", align_bytes=64)
         for c in range(CHUNKS):
@@ -229,7 +224,7 @@ def tile_picked_depth_glu_silu_sub_p_kernel(tc, x_words, x_scales, w1, w3, w2, g
                     out=y[:],
                     lhsT=w2_codes[:, c * N : (c + 1) * N].bitcast(FP8X4),
                     lhsT_scale=w2_scales[:, c * N : (c + 1) * N],
-                    rhs=h_codes[c][:, cols].bitcast(FP8X4),
+                    rhs=h_codes[(c, q0 // 2)][:].bitcast(FP8X4),
                     rhs_scale=h_scales[c][:, cols],
                     start=(c == 0),
                     stop=(c == CHUNKS - 1),
@@ -242,12 +237,13 @@ def tile_picked_depth_glu_silu_sub_p_kernel(tc, x_words, x_scales, w1, w3, w2, g
         gated(1, 0)
         gated(1, 1)
         nc.vector.quantize_mx(out=w2_codes[:].bitcast(FP8X4), scales=w2_scales[:], in_=w2_rounded[:].rearrange("p c n t -> p (c n t)"))
-        quantise_h(1, 0, 2)
+        quantise_h(1, 0)
         down(0, 2)
         gated(1, 2)
         gated(1, 3)
-        quantise_h(1, 2, 3)
-        quantise_h(1, 3, 4)
+        h_codes[(0, 1)] = keep.tile([P, HALF], U32, name="h_codes01", tag="w2_rounded", align_bytes=64)
+        quantise_h(0, 1)
+        quantise_h(1, 1)
         down(2, 4)
         for u in range(2):
             scatter(u * HALF, (u + 1) * HALF)

@@ -32,7 +32,7 @@ BEFORE_SILU = 24
 AFTER_SILU = 40
 CHUNK_END = 36
 BESIDE_GATING = 16
-LAST_PARTS = ((0, 384, BESIDE_GATING), (384, 512, 40))
+LAST_PARTS = ((0, 384, BEFORE_SILU), (384, 512, 40))
 
 
 def tile_picked_depth_glu_silu_sub_p_kernel(tc, x_words, x_scales, w1, w3, w2, gate, offs, out):
@@ -154,6 +154,7 @@ def tile_picked_depth_glu_silu_sub_p_kernel(tc, x_words, x_scales, w1, w3, w2, g
 
         act = [keep.tile([P, PACK, S], F32, name="act%d" % c, align_bytes=64) for c in range(CHUNKS)]
         h = [keep.tile([P, QUARTERS, NQ, PACK], BF16, name="h%d" % c, align_bytes=64) for c in range(CHUNKS)]
+        h_late = {}
         h_codes = {(1, u): keep.tile([P, HALF], U32, name="h_codes1%d" % u, align_bytes=64) for u in range(2)}
         h_scales = [keep.tile([P, S], U8, name="h_scales%d" % c, align_bytes=64) for c in range(CHUNKS)]
 
@@ -163,7 +164,7 @@ def tile_picked_depth_glu_silu_sub_p_kernel(tc, x_words, x_scales, w1, w3, w2, g
 
         def gated(c, q):
             nc.vector.tensor_tensor(
-                h[c][:, q].rearrange("p (a i) t -> p a t i", i=2),
+                h_late.get((c, q), h[c][:, q]).rearrange("p (a i) t -> p a t i", i=2),
                 banks[(W3, c, q)][:].rearrange("p t (a i) -> p a t i", i=2),
                 act[c][:, :, q * NQ : (q + 1) * NQ].rearrange("p t (a i) -> p a t i", i=2),
                 MULT,
@@ -197,13 +198,15 @@ def tile_picked_depth_glu_silu_sub_p_kernel(tc, x_words, x_scales, w1, w3, w2, g
         prepare((W3, 1, 1), BESIDE_GATING)
         multiply_w3(1, 1)
         round_piece(last, *[part[2] for part in LAST_PARTS])
-        for q in range(QUARTERS):
+        for q in range(QUARTERS - 1):
             gated(0, q)
         quantise(last, 2, 4)
         quantise(last, 0, 2)
         multiply_w3(last[1], last[2], (2, 3, 0, 1))
-        tag = "w3_%d%d_%d" % (last[1], last[2], LAST_PARTS[-1][0])
-        h_codes[(0, 0)] = keep.tile([P, HALF], U32, name="h_codes00", tag=tag, align_bytes=64)
+        tags = ["w3_%d%d_%d" % (last[1], last[2], part[0]) for part in LAST_PARTS]
+        h_late[(0, 3)] = keep.tile([P, NQ, PACK], BF16, name="h03", tag=tags[1], align_bytes=64)[:]
+        gated(0, 3)
+        h_codes[(0, 0)] = keep.tile([P, HALF], U32, name="h_codes00", tag=tags[0], align_bytes=64)
         quantise_h(0, 0)
 
         w2_rounded = keep.tile([P, CHUNKS, N, PACK], BF16, name="w2_rounded", align_bytes=64)
@@ -242,7 +245,12 @@ def tile_picked_depth_glu_silu_sub_p_kernel(tc, x_words, x_scales, w1, w3, w2, g
         gated(1, 2)
         gated(1, 3)
         h_codes[(0, 1)] = keep.tile([P, HALF], U32, name="h_codes01", tag="w2_rounded", align_bytes=64)
-        quantise_h(0, 1)
+        for q, src in ((2, h[0][:, 2]), (3, h_late[(0, 3)])):
+            nc.vector.quantize_mx(
+                out=h_codes[(0, 1)][:, (q - 2) * NQ : (q - 1) * NQ].bitcast(FP8X4),
+                scales=h_scales[0][:, q * NQ : (q + 1) * NQ],
+                in_=src.rearrange("p n t -> p (n t)"),
+            )
         quantise_h(1, 1)
         down(2, 4)
         for u in range(2):

@@ -30,9 +30,9 @@ BALANCED = 44
 ALL_VECTOR = 64
 BEFORE_SILU = 24
 AFTER_SILU = 40
-CHUNK_END = 36
+CHUNK_END = 32
 BESIDE_GATING = 16
-LAST_PARTS = ((0, 384, BEFORE_SILU), (384, 512, 40))
+LAST_PARTS = ((0, 384, EVEN), (384, 512, 40))
 
 
 def tile_picked_depth_glu_silu_sub_p_kernel(tc, x_words, x_scales, w1, w3, w2, gate, offs, out):
@@ -110,6 +110,16 @@ def tile_picked_depth_glu_silu_sub_p_kernel(tc, x_words, x_scales, w1, w3, w2, g
                 if cut < n:
                     nc.scalar.copy(dst[:, cut:n], src[:, cut:n])
             codes[key] = keep.tile([P, KP], U32, name="codes%d%d%d" % key, tag=codes_tag or "codes%d%d%d" % key, align_bytes=64)
+            scales[key] = keep.tile([P, KP], U8, name="scales%d%d%d" % key, align_bytes=64)
+
+        def round_by_pairs(key, cut):
+            rounded[key] = stage.tile([P, PACK, P, PACK], BF16, name="rounded", align_bytes=64)
+            src = raw[key][0][0].rearrange("p j (m u v) -> p u m j v", u=2, v=2)
+            dst = rounded[key][:].rearrange("p (u v) m j -> p u m j v", v=2)
+            nc.scalar.copy(dst[:, 1, cut:P], src[:, 1, cut:P])
+            nc.vector.tensor_copy(dst[:, 0], src[:, 0])
+            nc.vector.tensor_copy(dst[:, 1, 0:cut], src[:, 1, 0:cut])
+            codes[key] = keep.tile([P, KP], U32, name="codes%d%d%d" % key, align_bytes=64)
             scales[key] = keep.tile([P, KP], U8, name="scales%d%d%d" % key, align_bytes=64)
 
         def quantise(key, t0, t1):
@@ -190,23 +200,34 @@ def tile_picked_depth_glu_silu_sub_p_kernel(tc, x_words, x_scales, w1, w3, w2, g
         prepare((W3, 0, 0), ALL_VECTOR)
         multiply_w3(0, 0)
         round_piece((W3, 0, 1), AFTER_SILU, codes_tag="w3_20_0")
-        for g in range(1, PASSES):
-            prepare((W3, g, 0), ALL_VECTOR if g == 1 else CHUNK_END)
-            multiply_w3(g, 0)
+        prepare((W3, 1, 0), ALL_VECTOR)
+        multiply_w3(1, 0)
+        round_by_pairs((W3, 2, 0), CHUNK_END)
+        quantise((W3, 2, 0), 0, 2)
+        quantise((W3, 2, 0), 2, 4)
+        multiply_w3(2, 0)
         quantise((W3, 0, 1), 0, PACK)
         multiply_w3(0, 1)
         prepare((W3, 1, 1), BESIDE_GATING)
         multiply_w3(1, 1)
-        round_piece(last, *[part[2] for part in LAST_PARTS])
+        pair = [keep.tile([P, 2, P, PACK], BF16, name="pair%d" % u, align_bytes=64) for u in range(2)]
+        for view, col0, col1 in raw[last]:
+            src = view.rearrange("p j (m u v) -> p u m j v", u=2, v=2)
+            for u, copy in enumerate((nc.vector.tensor_copy, nc.scalar.copy)):
+                copy(pair[u][:].rearrange("p v m j -> p m j v")[:, col0 // 4 : col1 // 4], src[:, u])
+        codes[last] = keep.tile([P, KP], U32, name="codes_last", align_bytes=64)
+        scales[last] = keep.tile([P, KP], U8, name="scales_last", align_bytes=64)
         for q in range(QUARTERS - 1):
             gated(0, q)
-        quantise(last, 2, 4)
-        quantise(last, 0, 2)
+        for u in (1, 0):
+            cols = slice(u * HALF, (u + 1) * HALF)
+            nc.vector.quantize_mx(
+                out=codes[last][:, cols].bitcast(FP8X4), scales=scales[last][:, cols], in_=pair[u][:].rearrange("p v m j -> p (v m j)")
+            )
         multiply_w3(last[1], last[2], (2, 3, 0, 1))
-        tags = ["w3_%d%d_%d" % (last[1], last[2], part[0]) for part in LAST_PARTS]
-        h_late[(0, 3)] = keep.tile([P, NQ, PACK], BF16, name="h03", tag=tags[1], align_bytes=64)[:]
+        h_late[(0, 3)] = keep.tile([P, NQ, PACK], BF16, name="h03", tag="pair1", align_bytes=64)[:]
         gated(0, 3)
-        h_codes[(0, 0)] = keep.tile([P, HALF], U32, name="h_codes00", tag=tags[0], align_bytes=64)
+        h_codes[(0, 0)] = keep.tile([P, HALF], U32, name="h_codes00", tag="pair0", align_bytes=64)
         quantise_h(0, 0)
 
         w2_rounded = keep.tile([P, CHUNKS, N, PACK], BF16, name="w2_rounded", align_bytes=64)

@@ -30,7 +30,9 @@ BALANCED = 44
 ALL_VECTOR = 64
 BEFORE_SILU = 24
 AFTER_SILU = 40
-CHUNK_END = 32
+CHUNK_END = 160
+MID = 256
+GATING = 32
 BESIDE_GATING = 16
 LAST_PARTS = ((0, 384, EVEN), (384, 512, 40))
 
@@ -116,9 +118,12 @@ def tile_picked_depth_glu_silu_sub_p_kernel(tc, x_words, x_scales, w1, w3, w2, g
             rounded[key] = stage.tile([P, PACK, P, PACK], BF16, name="rounded", align_bytes=64)
             src = raw[key][0][0].rearrange("p j (m u v) -> p u m j v", u=2, v=2)
             dst = rounded[key][:].rearrange("p (u v) m j -> p u m j v", v=2)
-            nc.scalar.copy(dst[:, 1, cut:P], src[:, 1, cut:P])
-            nc.vector.tensor_copy(dst[:, 0], src[:, 0])
-            nc.vector.tensor_copy(dst[:, 1, 0:cut], src[:, 1, 0:cut])
+            for u in range(2):
+                n = min(P, max(0, cut - u * P))
+                if n > 0:
+                    nc.vector.tensor_copy(dst[:, u, 0:n], src[:, u, 0:n])
+                if n < P:
+                    nc.scalar.copy(dst[:, u, n:P], src[:, u, n:P])
             codes[key] = keep.tile([P, KP], U32, name="codes%d%d%d" % key, align_bytes=64)
             scales[key] = keep.tile([P, KP], U8, name="scales%d%d%d" % key, align_bytes=64)
 
@@ -200,7 +205,9 @@ def tile_picked_depth_glu_silu_sub_p_kernel(tc, x_words, x_scales, w1, w3, w2, g
         prepare((W3, 0, 0), ALL_VECTOR)
         multiply_w3(0, 0)
         round_piece((W3, 0, 1), AFTER_SILU, codes_tag="w3_20_0")
-        prepare((W3, 1, 0), ALL_VECTOR)
+        round_by_pairs((W3, 1, 0), MID)
+        quantise((W3, 1, 0), 0, 2)
+        quantise((W3, 1, 0), 2, 4)
         multiply_w3(1, 0)
         round_by_pairs((W3, 2, 0), CHUNK_END)
         quantise((W3, 2, 0), 0, 2)
@@ -208,7 +215,9 @@ def tile_picked_depth_glu_silu_sub_p_kernel(tc, x_words, x_scales, w1, w3, w2, g
         multiply_w3(2, 0)
         quantise((W3, 0, 1), 0, PACK)
         multiply_w3(0, 1)
-        prepare((W3, 1, 1), BESIDE_GATING)
+        round_by_pairs((W3, 1, 1), GATING)
+        quantise((W3, 1, 1), 0, 2)
+        quantise((W3, 1, 1), 2, 4)
         multiply_w3(1, 1)
         pair = [keep.tile([P, 2, P, PACK], BF16, name="pair%d" % u, align_bytes=64) for u in range(2)]
         for view, col0, col1 in raw[last]:

@@ -87,8 +87,9 @@ def tile_picked_depth_glu_silu_sub_p_kernel(tc, x_words, x_scales, w1, w3, w2, g
                     part = keep.tile([P, PACK, col1 - col0], F32, name=tag, tag=tag, align_bytes=64)
                     nc.sync.dma_start(out=part[:], in_=k_rows(w3, g)[:, :, c * KP + col0 : c * KP + col1])
                     raw[key].append((part[:], col0, col1))
-        w2_raw = keep.tile([P, CHUNKS, PACK, N], F32, name="w2_raw", align_bytes=64)
-        nc.sync.dma_start(out=w2_raw[:], in_=w2.rearrange("(c p t) n -> p c t n", c=CHUNKS, t=PACK))
+        w2_raw = [keep.tile([P, PACK, N], F32, name="w2_raw%d" % c, align_bytes=64) for c in range(CHUNKS)]
+        for c in range(CHUNKS):
+            nc.sync.dma_start(out=w2_raw[c][:], in_=w2[c * KP : (c + 1) * KP, :].rearrange("(p t) n -> p t n", t=PACK))
         gate_sb = keep.tile([P, S], F32, name="gate_sb", align_bytes=64)
         nc.sync.dma_start(out=gate_sb[:], in_=gate)
 
@@ -220,9 +221,9 @@ def tile_picked_depth_glu_silu_sub_p_kernel(tc, x_words, x_scales, w1, w3, w2, g
         quantise((W3, 1, 1), 2, 4)
         multiply_w3(1, 1)
         pair = [keep.tile([P, 2, P, PACK], BF16, name="pair%d" % u, align_bytes=64) for u in range(2)]
-        for view, col0, col1 in raw[last]:
+        for (view, col0, col1), second in zip(raw[last], (nc.scalar.copy, nc.vector.tensor_copy)):
             src = view.rearrange("p j (m u v) -> p u m j v", u=2, v=2)
-            for u, copy in enumerate((nc.vector.tensor_copy, nc.scalar.copy)):
+            for u, copy in ((1, second), (0, nc.vector.tensor_copy)):
                 copy(pair[u][:].rearrange("p v m j -> p m j v")[:, col0 // 4 : col1 // 4], src[:, u])
         codes[last] = keep.tile([P, KP], U32, name="codes_last", align_bytes=64)
         scales[last] = keep.tile([P, KP], U8, name="scales_last", align_bytes=64)
@@ -243,7 +244,7 @@ def tile_picked_depth_glu_silu_sub_p_kernel(tc, x_words, x_scales, w1, w3, w2, g
         for c in range(CHUNKS):
             nc.scalar.copy(
                 w2_rounded[:, c].rearrange("p (b i) t -> p b t i", i=4),
-                w2_raw[:, c].rearrange("p t (b i) -> p b t i", i=4),
+                w2_raw[c][:].rearrange("p t (b i) -> p b t i", i=4),
             )
         w2_codes = keep.tile([P, CHUNKS * N], U32, name="w2_codes", align_bytes=64)
         w2_scales = keep.tile([P, CHUNKS * N], U8, name="w2_scales", align_bytes=64)

@@ -180,9 +180,9 @@ def tile_picked_depth_glu_silu_sub_p_kernel(tc, x_words, x_scales, w1, w3, w2, g
 
         def gated(c, q):
             nc.vector.tensor_tensor(
-                h_late.get((c, q), h[c][:, q]).rearrange("p (a i) t -> p a t i", i=2),
-                banks[(W3, c, q)][:].rearrange("p t (a i) -> p a t i", i=2),
-                act[c][:, :, q * NQ : (q + 1) * NQ].rearrange("p t (a i) -> p a t i", i=2),
+                h_late.get((c, q), h[c][:, q]).rearrange("p (a i) t -> p a t i", i=4),
+                banks[(W3, c, q)][:].rearrange("p t (a i) -> p a t i", i=4),
+                act[c][:, :, q * NQ : (q + 1) * NQ].rearrange("p t (a i) -> p a t i", i=4),
                 MULT,
             )
 

@@ -14,6 +14,7 @@ U8 = mybir.dt.uint8
 FP8X4 = mybir.dt.float8_e4m3fn_x4
 MULT = mybir.AluOpType.mult
 SILU = mybir.ActivationFunctionType.Silu
+COPY = mybir.ActivationFunctionType.Copy
 
 P = 128
 PACK = 4
@@ -90,8 +91,9 @@ def tile_picked_depth_glu_silu_sub_p_kernel(tc, x_words, x_scales, w1, w3, w2, g
         w2_raw = [keep.tile([P, PACK, N], F32, name="w2_raw%d" % c, align_bytes=64) for c in range(CHUNKS)]
         for c in range(CHUNKS):
             nc.sync.dma_start(out=w2_raw[c][:], in_=w2[c * KP : (c + 1) * KP, :].rearrange("(p t) n -> p t n", t=PACK))
-        gate_sb = keep.tile([P, S], F32, name="gate_sb", align_bytes=64)
-        nc.sync.dma_start(out=gate_sb[:], in_=gate)
+        gates = [keep.tile([P, HALF], F32, name="gate%d" % u, align_bytes=64) for u in range(2)]
+        for u in range(2):
+            nc.sync.dma_start(out=gates[u][:], in_=gate[:, u * HALF : (u + 1) * HALF])
 
         result = keep.tile([P, T], F32, name="result", align_bytes=64)
         nc.vector.memset(result[:], 0.0)
@@ -171,7 +173,7 @@ def tile_picked_depth_glu_silu_sub_p_kernel(tc, x_words, x_scales, w1, w3, w2, g
         act = [keep.tile([P, PACK, S], F32, name="act%d" % c, align_bytes=64) for c in range(CHUNKS)]
         h = [keep.tile([P, QUARTERS, NQ, PACK], BF16, name="h%d" % c, align_bytes=64) for c in range(CHUNKS)]
         h_late = {}
-        h_codes = {(1, u): keep.tile([P, HALF], U32, name="h_codes1%d" % u, align_bytes=64) for u in range(2)}
+        h_codes = {(1, 0): keep.tile([P, HALF], U32, name="h_codes10", align_bytes=64)}
         h_scales = [keep.tile([P, S], U8, name="h_scales%d" % c, align_bytes=64) for c in range(CHUNKS)]
 
         def silu(c):
@@ -258,32 +260,37 @@ def tile_picked_depth_glu_silu_sub_p_kernel(tc, x_words, x_scales, w1, w3, w2, g
                     out=y[:],
                     lhsT=w2_codes[:, c * N : (c + 1) * N].bitcast(FP8X4),
                     lhsT_scale=w2_scales[:, c * N : (c + 1) * N],
-                    rhs=h_codes[(c, q0 // 2)][:].bitcast(FP8X4),
+                    rhs=h_codes[(c, q0)][:].bitcast(FP8X4),
                     rhs_scale=h_scales[c][:, cols],
                     start=(c == 0),
                     stop=(c == CHUNKS - 1),
                 )
-            nc.scalar.copy(y_sb[:, cols], y[:])
+            nc.vector.tensor_tensor(y_sb[:, cols], y[:], gates[q0 // 2][:, q0 % 2 * NQ : (q1 - 1) % 2 * NQ + NQ], MULT)
 
-        def scatter(j0, j1):
-            nc.vector.tensor_tensor(result[:].indirect(offsets[:, j0 // 16 : j1 // 16]), y_sb[:, j0:j1], gate_sb[:, j0:j1], MULT)
+        def quantise_quarter(c, q, src, tag=None):
+            name = "h_quarter%d%d" % (c, q)
+            h_codes[(c, q)] = keep.tile([P, NQ], U32, name=name, tag=tag or name, align_bytes=64)
+            nc.vector.quantize_mx(
+                out=h_codes[(c, q)][:].bitcast(FP8X4), scales=h_scales[c][:, q * NQ : (q + 1) * NQ], in_=src.rearrange("p n t -> p (n t)")
+            )
+
+        def window(u):
+            return result[:].indirect(offsets[:, u * HALF // 16 : (u + 1) * HALF // 16])
 
         gated(1, 0)
         gated(1, 1)
         nc.vector.quantize_mx(out=w2_codes[:].bitcast(FP8X4), scales=w2_scales[:], in_=w2_rounded[:].rearrange("p c n t -> p (c n t)"))
         quantise_h(1, 0)
         down(0, 2)
+        nc.scalar.activation(window(0), y_sb[:, 0:HALF], COPY)
         gated(1, 2)
+        quantise_quarter(0, 2, h[0][:, 2], "w2_rounded")
+        quantise_quarter(1, 2, h[1][:, 2])
+        h_late[(1, 3)] = keep.tile([P, NQ, PACK], BF16, name="h13", tag="h_codes10", align_bytes=64)[:]
         gated(1, 3)
-        h_codes[(0, 1)] = keep.tile([P, HALF], U32, name="h_codes01", tag="w2_rounded", align_bytes=64)
-        for q, src in ((2, h[0][:, 2]), (3, h_late[(0, 3)])):
-            nc.vector.quantize_mx(
-                out=h_codes[(0, 1)][:, (q - 2) * NQ : (q - 1) * NQ].bitcast(FP8X4),
-                scales=h_scales[0][:, q * NQ : (q + 1) * NQ],
-                in_=src.rearrange("p n t -> p (n t)"),
-            )
-        quantise_h(1, 1)
-        down(2, 4)
-        for u in range(2):
-            scatter(u * HALF, (u + 1) * HALF)
+        quantise_quarter(0, 3, h_late[(0, 3)], "gate0")
+        down(2, 3)
+        quantise_quarter(1, 3, h_late[(1, 3)])
+        down(3, 4)
+        nc.vector.tensor_copy(window(1), y_sb[:, HALF:S])
         nc.sync.dma_start(out=out, in_=result[:])

@@ -285,12 +285,12 @@ def tile_picked_depth_glu_silu_sub_p_kernel(tc, x_words, x_scales, w1, w3, w2, g
         nc.scalar.activation(window(0), y_sb[:, 0:HALF], COPY)
         gated(1, 2)
         quantise_quarter(0, 2, h[0][:, 2], "w2_rounded")
-        quantise_quarter(1, 2, h[1][:, 2])
         h_late[(1, 3)] = keep.tile([P, NQ, PACK], BF16, name="h13", tag="h_codes10", align_bytes=64)[:]
         gated(1, 3)
         quantise_quarter(0, 3, h_late[(0, 3)], "gate0")
-        down(2, 3)
+        quantise_quarter(1, 2, h[1][:, 2])
         quantise_quarter(1, 3, h_late[(1, 3)])
+        down(2, 3)
         down(3, 4)
         nc.vector.tensor_copy(window(1), y_sb[:, HALF:S])
         nc.sync.dma_start(out=out, in_=result[:])

@@ -173,24 +173,24 @@ def tile_picked_depth_glu_silu_sub_p_kernel(tc, x_words, x_scales, w1, w3, w2, g
         act = [keep.tile([P, PACK, S], F32, name="act%d" % c, align_bytes=64) for c in range(CHUNKS)]
         h = [keep.tile([P, QUARTERS, NQ, PACK], BF16, name="h%d" % c, align_bytes=64) for c in range(CHUNKS)]
         h_late = {}
-        h_codes = {(1, 0): keep.tile([P, HALF], U32, name="h_codes10", align_bytes=64)}
+        h_codes = {(1, 0): keep.tile([P, HALF], U32, name="h_codes10", align_bytes=64)[:]}
         h_scales = [keep.tile([P, S], U8, name="h_scales%d" % c, align_bytes=64) for c in range(CHUNKS)]
 
         def silu(c):
             for t in range(PACK):
                 nc.scalar.activation(act[c][:, t], banks[(W1, c, t)][:], SILU)
 
-        def gated(c, q):
+        def gated(c, q, part=slice(0, NQ // 4)):
             nc.vector.tensor_tensor(
-                h_late.get((c, q), h[c][:, q]).rearrange("p (a i) t -> p a t i", i=4),
-                banks[(W3, c, q)][:].rearrange("p t (a i) -> p a t i", i=4),
-                act[c][:, :, q * NQ : (q + 1) * NQ].rearrange("p t (a i) -> p a t i", i=4),
+                h_late.get((c, q), h[c][:, q]).rearrange("p (a i) t -> p a t i", i=4)[:, part],
+                banks[(W3, c, q)][:].rearrange("p t (a i) -> p a t i", i=4)[:, part],
+                act[c][:, :, q * NQ : (q + 1) * NQ].rearrange("p t (a i) -> p a t i", i=4)[:, part],
                 MULT,
             )
 
         def quantise_h(c, u):
             nc.vector.quantize_mx(
-                out=h_codes[(c, u)][:].bitcast(FP8X4),
+                out=h_codes[(c, u)].bitcast(FP8X4),
                 scales=h_scales[c][:, u * HALF : (u + 1) * HALF],
                 in_=h[c][:, 2 * u : 2 * u + 2].rearrange("p q n t -> p (q n t)"),
             )
@@ -237,10 +237,12 @@ def tile_picked_depth_glu_silu_sub_p_kernel(tc, x_words, x_scales, w1, w3, w2, g
                 out=codes[last][:, cols].bitcast(FP8X4), scales=scales[last][:, cols], in_=pair[u][:].rearrange("p v m j -> p (v m j)")
             )
         multiply_w3(last[1], last[2], (2, 3, 0, 1))
-        h_late[(0, 3)] = keep.tile([P, NQ, PACK], BF16, name="h03", tag="pair1", align_bytes=64)[:]
-        gated(0, 3)
-        h_codes[(0, 0)] = keep.tile([P, HALF], U32, name="h_codes00", tag="pair0", align_bytes=64)
+        early_codes = keep.tile([P, 3 * NQ], U32, name="early_codes", tag="pair0", align_bytes=64)
+        h_codes[(0, 0)], h_codes[(0, 2)] = early_codes[:, 0:HALF], early_codes[:, HALF : 3 * NQ]
         quantise_h(0, 0)
+        nc.vector.quantize_mx(
+            out=h_codes[(0, 2)].bitcast(FP8X4), scales=h_scales[0][:, HALF : 3 * NQ], in_=h[0][:, 2].rearrange("p n t -> p (n t)")
+        )
 
         w2_rounded = keep.tile([P, CHUNKS, N, PACK], BF16, name="w2_rounded", align_bytes=64)
         for c in range(CHUNKS):
@@ -260,7 +262,7 @@ def tile_picked_depth_glu_silu_sub_p_kernel(tc, x_words, x_scales, w1, w3, w2, g
                     out=y[:],
                     lhsT=w2_codes[:, c * N : (c + 1) * N].bitcast(FP8X4),
                     lhsT_scale=w2_scales[:, c * N : (c + 1) * N],
-                    rhs=h_codes[(c, q0)][:].bitcast(FP8X4),
+                    rhs=h_codes[(c, q0)].bitcast(FP8X4),
                     rhs_scale=h_scales[c][:, cols],
                     start=(c == 0),
                     stop=(c == CHUNKS - 1),
@@ -269,28 +271,33 @@ def tile_picked_depth_glu_silu_sub_p_kernel(tc, x_words, x_scales, w1, w3, w2, g
 
         def quantise_quarter(c, q, src, tag=None):
             name = "h_quarter%d%d" % (c, q)
-            h_codes[(c, q)] = keep.tile([P, NQ], U32, name=name, tag=tag or name, align_bytes=64)
+            h_codes[(c, q)] = keep.tile([P, NQ], U32, name=name, tag=tag or name, align_bytes=64)[:]
             nc.vector.quantize_mx(
-                out=h_codes[(c, q)][:].bitcast(FP8X4), scales=h_scales[c][:, q * NQ : (q + 1) * NQ], in_=src.rearrange("p n t -> p (n t)")
+                out=h_codes[(c, q)].bitcast(FP8X4), scales=h_scales[c][:, q * NQ : (q + 1) * NQ], in_=src.rearrange("p n t -> p (n t)")
             )
 
-        def window(u):
-            return result[:].indirect(offsets[:, u * HALF // 16 : (u + 1) * HALF // 16])
+        def window(q0, q1):
+            return result[:].indirect(offsets[:, q0 * NQ // 16 : q1 * NQ // 16])
 
+        first = keep.tile([P, 2, NQ, PACK], BF16, name="h1_first", align_bytes=64)
+        h_late[(1, 0)], h_late[(1, 1)] = first[:, 0], first[:, 1]
         gated(1, 0)
         gated(1, 1)
         nc.vector.quantize_mx(out=w2_codes[:].bitcast(FP8X4), scales=w2_scales[:], in_=w2_rounded[:].rearrange("p c n t -> p (c n t)"))
-        quantise_h(1, 0)
+        nc.vector.quantize_mx(out=h_codes[(1, 0)].bitcast(FP8X4), scales=h_scales[1][:, 0:HALF], in_=first[:].rearrange("p q n t -> p (q n t)"))
         down(0, 2)
-        nc.scalar.activation(window(0), y_sb[:, 0:HALF], COPY)
+        nc.scalar.activation(window(0, 2), y_sb[:, 0:HALF], COPY)
         gated(1, 2)
-        quantise_quarter(0, 2, h[0][:, 2], "w2_rounded")
+        h_late[(0, 3)] = keep.tile([P, NQ, PACK], BF16, name="h03", tag="h1_first", align_bytes=64)[:]
+        gated(0, 3, slice(0, NQ // 8))
+        quantise_quarter(1, 2, h[1][:, 2], "gate0")
+        gated(0, 3, slice(NQ // 8, NQ // 4))
         h_late[(1, 3)] = keep.tile([P, NQ, PACK], BF16, name="h13", tag="h_codes10", align_bytes=64)[:]
         gated(1, 3)
-        quantise_quarter(0, 3, h_late[(0, 3)], "gate0")
-        quantise_quarter(1, 2, h[1][:, 2])
-        quantise_quarter(1, 3, h_late[(1, 3)])
         down(2, 3)
+        nc.scalar.activation(window(2, 3), y_sb[:, HALF : 3 * NQ], COPY)
+        quantise_quarter(0, 3, h_late[(0, 3)])
+        quantise_quarter(1, 3, h_late[(1, 3)])
         down(3, 4)
-        nc.vector.tensor_copy(window(1), y_sb[:, HALF:S])
+        nc.vector.tensor_copy(window(3, 4), y_sb[:, 3 * NQ : S])
         nc.sync.dma_start(out=out, in_=result[:])

@@ -161,11 +161,18 @@ def tile_picked_depth_glu_silu_sub_p_kernel(tc, x_words, x_scales, w1, w3, w2, g
                     banks[(W1, c, t)] = psum.tile([P, S], F32, name="acc", tag="bank%d" % (c * PACK + t))
                 matmul(banks[(W1, c, t)][:], (W1, g, c), t, slice(0, S), g == 0, g == PASSES - 1)
 
+        def multiply_late(q):
+            banks[(W3, 1, q)] = psum.tile([P, PACK, NQ], F32, name="acc", tag="bank%d" % (QUARTERS + q))
+            order = [(g, t) for g in (2, 0, 1) for t in range(PACK)]
+            for g, t in order:
+                matmul(banks[(W3, 1, q)][:, t, :], (W3, g, 1), t, slice(q * NQ, (q + 1) * NQ), (g, t) == order[0], (g, t) == order[-1])
+
         def multiply_w3(g, c, ts=range(PACK)):
+            quarters = range(QUARTERS if c == 0 else 2)
             if g == 0:
-                for q in range(QUARTERS):
+                for q in quarters:
                     banks[(W3, c, q)] = psum.tile([P, PACK, NQ], F32, name="acc", tag="bank%d" % (c * QUARTERS + q))
-            for q in range(QUARTERS):
+            for q in quarters:
                 for t in ts:
                     first, final = g == 0 and t == ts[0], g == PASSES - 1 and t == ts[-1]
                     matmul(banks[(W3, c, q)][:, t, :], (W3, g, c), t, slice(q * NQ, (q + 1) * NQ), first, final)
@@ -237,6 +244,7 @@ def tile_picked_depth_glu_silu_sub_p_kernel(tc, x_words, x_scales, w1, w3, w2, g
                 out=codes[last][:, cols].bitcast(FP8X4), scales=scales[last][:, cols], in_=pair[u][:].rearrange("p v m j -> p (v m j)")
             )
         multiply_w3(last[1], last[2], (2, 3, 0, 1))
+        multiply_late(2)
         early_codes = keep.tile([P, 3 * NQ], U32, name="early_codes", tag="pair0", align_bytes=64)
         h_codes[(0, 0)], h_codes[(0, 2)] = early_codes[:, 0:HALF], early_codes[:, HALF : 3 * NQ]
         quantise_h(0, 0)
@@ -287,6 +295,7 @@ def tile_picked_depth_glu_silu_sub_p_kernel(tc, x_words, x_scales, w1, w3, w2, g
         nc.vector.quantize_mx(out=h_codes[(1, 0)].bitcast(FP8X4), scales=h_scales[1][:, 0:HALF], in_=first[:].rearrange("p q n t -> p (q n t)"))
         down(0, 2)
         nc.scalar.activation(window(0, 2), y_sb[:, 0:HALF], COPY)
+        multiply_late(3)
         gated(1, 2)
         h_late[(0, 3)] = keep.tile([P, NQ, PACK], BF16, name="h03", tag="h1_first", align_bytes=64)[:]
         gated(0, 3, slice(0, NQ // 8))

@@ -31,11 +31,11 @@ BALANCED = 44
 ALL_VECTOR = 64
 BEFORE_SILU = 24
 AFTER_SILU = 40
+ALL_STEPS = 256
 CHUNK_END = 160
-MID = 256
-GATING = 32
-BESIDE_GATING = 16
-LAST_PARTS = ((0, 384, EVEN), (384, 512, 40))
+BESIDE_GATING = 32
+LAST_CUT = 384
+EARLY_QUARTERS = 2
 
 
 def tile_picked_depth_glu_silu_sub_p_kernel(tc, x_words, x_scales, w1, w3, w2, gate, offs, out):
@@ -54,21 +54,22 @@ def tile_picked_depth_glu_silu_sub_p_kernel(tc, x_words, x_scales, w1, w3, w2, g
         nc.vector.memset(warm_in[:], 0.0)
         nc.scalar.activation(warm_out[:], warm_in[:], SILU)
 
-        x_all = [keep.tile([P, T], I32, name="x_all%d" % g, align_bytes=64) for g in range(PASSES)]
+        x_all = keep.tile([P, PASSES * T], I32, name="x_all", align_bytes=64)
+        nc.sync.dma_start(
+            out=x_all[:].rearrange("p (g n) -> p g n", g=PASSES), in_=x_words.rearrange("g p n t -> p g (n t)").bitcast(I32)
+        )
+        nc.sync.dma_start(offsets[:], offs)
         raw = {}
 
         def k_rows(w, g):
             return w[g * KP : (g + 1) * KP, :].rearrange("(p j) h -> p j h", j=PACK)
 
         for g in range(PASSES):
-            nc.sync.dma_start(out=x_all[g][:], in_=x_words[g].rearrange("p n t -> p (n t)").bitcast(I32))
-            if g == 0:
-                nc.sync.dma_start(offsets[:], offs)
             if g == 1:
-                for q in range(4):
+                for d in range(P // 32):
                     nc.sync.dma_start(
-                        out=x_scale_rows[:].bitcast(I32)[32 * q : 32 * q + 4 * PASSES, :],
-                        in_=x_scales[:, 4 * q : 4 * q + 4, :].bitcast(I32),
+                        out=x_scale_rows[:].bitcast(I32)[32 * d : 32 * d + 4 * PASSES, :],
+                        in_=x_scales[:, 4 * d : 4 * d + 4, :].bitcast(I32),
                     )
             wide = keep.tile([P, PACK, H], F32, name="w1_pass%d" % g, align_bytes=64)
             nc.sync.dma_start(out=wide[:], in_=k_rows(w1, g))
@@ -83,7 +84,7 @@ def tile_picked_depth_glu_silu_sub_p_kernel(tc, x_words, x_scales, w1, w3, w2, g
             for g in range(1, PASSES):
                 key = (W3, g, c)
                 raw[key] = []
-                for col0, col1 in [part[:2] for part in LAST_PARTS] if key == last else [(0, KP)]:
+                for col0, col1 in [(0, LAST_CUT), (LAST_CUT, KP)] if key == last else [(0, KP)]:
                     tag = "w3_%d%d_%d" % (g, c, col0)
                     part = keep.tile([P, PACK, col1 - col0], F32, name=tag, tag=tag, align_bytes=64)
                     nc.sync.dma_start(out=part[:], in_=k_rows(w3, g)[:, :, c * KP + col0 : c * KP + col1])
@@ -103,17 +104,14 @@ def tile_picked_depth_glu_silu_sub_p_kernel(tc, x_words, x_scales, w1, w3, w2, g
 
         rounded, codes, scales, banks = {}, {}, {}, {}
 
-        def round_piece(key, *shares, codes_tag=None):
+        def round_piece(key, share, codes_tag=None):
             rounded[key] = stage.tile([P, PACK, P, PACK], BF16, name="rounded", align_bytes=64)
-            for (view, col0, col1), share in zip(raw[key], shares):
-                src = view.rearrange("p j (m u v) -> p m u j v", u=2, v=2)
-                dst = rounded[key][:].rearrange("p (u v) m j -> p m u j v", v=2)[:, col0 // 4 : col1 // 4]
-                n = (col1 - col0) // 4
-                cut = 4 * ((share * n + 128) // 256)
-                if cut > 0:
-                    nc.vector.tensor_copy(dst[:, 0:cut], src[:, 0:cut])
-                if cut < n:
-                    nc.scalar.copy(dst[:, cut:n], src[:, cut:n])
+            src = raw[key][0][0].rearrange("p j (m u v) -> p m u j v", u=2, v=2)
+            dst = rounded[key][:].rearrange("p (u v) m j -> p m u j v", v=2)
+            cut = share * P // ALL_VECTOR
+            nc.vector.tensor_copy(dst[:, 0:cut], src[:, 0:cut])
+            if cut < P:
+                nc.scalar.copy(dst[:, cut:P], src[:, cut:P])
             codes[key] = keep.tile([P, KP], U32, name="codes%d%d%d" % key, tag=codes_tag or "codes%d%d%d" % key, align_bytes=64)
             scales[key] = keep.tile([P, KP], U8, name="scales%d%d%d" % key, align_bytes=64)
 
@@ -163,12 +161,12 @@ def tile_picked_depth_glu_silu_sub_p_kernel(tc, x_words, x_scales, w1, w3, w2, g
 
         def multiply_late(q):
             banks[(W3, 1, q)] = psum.tile([P, PACK, NQ], F32, name="acc", tag="bank%d" % (QUARTERS + q))
-            order = [(g, t) for g in (2, 0, 1) for t in range(PACK)]
+            order = [(g, t) for g in (PASSES - 1, 0, 1) for t in range(PACK)]
             for g, t in order:
                 matmul(banks[(W3, 1, q)][:, t, :], (W3, g, 1), t, slice(q * NQ, (q + 1) * NQ), (g, t) == order[0], (g, t) == order[-1])
 
         def multiply_w3(g, c, ts=range(PACK)):
-            quarters = range(QUARTERS if c == 0 else 2)
+            quarters = range(QUARTERS if c == 0 else EARLY_QUARTERS)
             if g == 0:
                 for q in quarters:
                     banks[(W3, c, q)] = psum.tile([P, PACK, NQ], F32, name="acc", tag="bank%d" % (c * QUARTERS + q))
@@ -179,7 +177,7 @@ def tile_picked_depth_glu_silu_sub_p_kernel(tc, x_words, x_scales, w1, w3, w2, g
 
         act = [keep.tile([P, PACK, S], F32, name="act%d" % c, align_bytes=64) for c in range(CHUNKS)]
         h = [keep.tile([P, QUARTERS, NQ, PACK], BF16, name="h%d" % c, align_bytes=64) for c in range(CHUNKS)]
-        h_late = {}
+        h_apart = {}
         h_codes = {(1, 0): keep.tile([P, HALF], U32, name="h_codes10", align_bytes=64)[:]}
         h_scales = [keep.tile([P, S], U8, name="h_scales%d" % c, align_bytes=64) for c in range(CHUNKS)]
 
@@ -189,21 +187,17 @@ def tile_picked_depth_glu_silu_sub_p_kernel(tc, x_words, x_scales, w1, w3, w2, g
 
         def gated(c, q, part=slice(0, NQ // 4)):
             nc.vector.tensor_tensor(
-                h_late.get((c, q), h[c][:, q]).rearrange("p (a i) t -> p a t i", i=4)[:, part],
+                h_apart.get((c, q), h[c][:, q]).rearrange("p (a i) t -> p a t i", i=4)[:, part],
                 banks[(W3, c, q)][:].rearrange("p t (a i) -> p a t i", i=4)[:, part],
                 act[c][:, :, q * NQ : (q + 1) * NQ].rearrange("p t (a i) -> p a t i", i=4)[:, part],
                 MULT,
             )
 
-        def quantise_h(c, u):
-            nc.vector.quantize_mx(
-                out=h_codes[(c, u)].bitcast(FP8X4),
-                scales=h_scales[c][:, u * HALF : (u + 1) * HALF],
-                in_=h[c][:, 2 * u : 2 * u + 2].rearrange("p q n t -> p (q n t)"),
-            )
+        def quantise_h(c, q0, q1, src):
+            nc.vector.quantize_mx(out=h_codes[(c, q0)].bitcast(FP8X4), scales=h_scales[c][:, q0 * NQ : q1 * NQ], in_=src)
 
         for g in range(PASSES):
-            nc.vector.tensor_copy(x_picked[g][:], x_all[g][:].bitcast(U32).indirect(offsets[:]))
+            nc.vector.tensor_copy(x_picked[g][:], x_all[:, g * T : (g + 1) * T].bitcast(U32).indirect(offsets[:]))
         nc.vector.tensor_copy(x_picked_scales[:], x_scale_rows[:].indirect(offsets[:]))
 
         for g in range(PASSES):
@@ -215,7 +209,7 @@ def tile_picked_depth_glu_silu_sub_p_kernel(tc, x_words, x_scales, w1, w3, w2, g
         prepare((W3, 0, 0), ALL_VECTOR)
         multiply_w3(0, 0)
         round_piece((W3, 0, 1), AFTER_SILU, codes_tag="w3_20_0")
-        round_by_pairs((W3, 1, 0), MID)
+        round_by_pairs((W3, 1, 0), ALL_STEPS)
         quantise((W3, 1, 0), 0, 2)
         quantise((W3, 1, 0), 2, 4)
         multiply_w3(1, 0)
@@ -225,7 +219,7 @@ def tile_picked_depth_glu_silu_sub_p_kernel(tc, x_words, x_scales, w1, w3, w2, g
         multiply_w3(2, 0)
         quantise((W3, 0, 1), 0, PACK)
         multiply_w3(0, 1)
-        round_by_pairs((W3, 1, 1), GATING)
+        round_by_pairs((W3, 1, 1), BESIDE_GATING)
         quantise((W3, 1, 1), 0, 2)
         quantise((W3, 1, 1), 2, 4)
         multiply_w3(1, 1)
@@ -247,10 +241,8 @@ def tile_picked_depth_glu_silu_sub_p_kernel(tc, x_words, x_scales, w1, w3, w2, g
         multiply_late(2)
         early_codes = keep.tile([P, 3 * NQ], U32, name="early_codes", tag="pair0", align_bytes=64)
         h_codes[(0, 0)], h_codes[(0, 2)] = early_codes[:, 0:HALF], early_codes[:, HALF : 3 * NQ]
-        quantise_h(0, 0)
-        nc.vector.quantize_mx(
-            out=h_codes[(0, 2)].bitcast(FP8X4), scales=h_scales[0][:, HALF : 3 * NQ], in_=h[0][:, 2].rearrange("p n t -> p (n t)")
-        )
+        quantise_h(0, 0, 2, h[0][:, 0:2].rearrange("p q n t -> p (q n t)"))
+        quantise_h(0, 2, 3, h[0][:, 2].rearrange("p n t -> p (n t)"))
 
         w2_rounded = keep.tile([P, CHUNKS, N, PACK], BF16, name="w2_rounded", align_bytes=64)
         for c in range(CHUNKS):
@@ -280,33 +272,31 @@ def tile_picked_depth_glu_silu_sub_p_kernel(tc, x_words, x_scales, w1, w3, w2, g
         def quantise_quarter(c, q, src, tag=None):
             name = "h_quarter%d%d" % (c, q)
             h_codes[(c, q)] = keep.tile([P, NQ], U32, name=name, tag=tag or name, align_bytes=64)[:]
-            nc.vector.quantize_mx(
-                out=h_codes[(c, q)].bitcast(FP8X4), scales=h_scales[c][:, q * NQ : (q + 1) * NQ], in_=src.rearrange("p n t -> p (n t)")
-            )
+            quantise_h(c, q, q + 1, src.rearrange("p n t -> p (n t)"))
 
         def window(q0, q1):
             return result[:].indirect(offsets[:, q0 * NQ // 16 : q1 * NQ // 16])
 
-        first = keep.tile([P, 2, NQ, PACK], BF16, name="h1_first", align_bytes=64)
-        h_late[(1, 0)], h_late[(1, 1)] = first[:, 0], first[:, 1]
+        first_half = keep.tile([P, 2, NQ, PACK], BF16, name="h1_first", align_bytes=64)
+        h_apart[(1, 0)], h_apart[(1, 1)] = first_half[:, 0], first_half[:, 1]
         gated(1, 0)
         gated(1, 1)
         nc.vector.quantize_mx(out=w2_codes[:].bitcast(FP8X4), scales=w2_scales[:], in_=w2_rounded[:].rearrange("p c n t -> p (c n t)"))
-        nc.vector.quantize_mx(out=h_codes[(1, 0)].bitcast(FP8X4), scales=h_scales[1][:, 0:HALF], in_=first[:].rearrange("p q n t -> p (q n t)"))
+        quantise_h(1, 0, 2, first_half[:].rearrange("p q n t -> p (q n t)"))
         down(0, 2)
         nc.scalar.activation(window(0, 2), y_sb[:, 0:HALF], COPY)
         multiply_late(3)
         gated(1, 2)
-        h_late[(0, 3)] = keep.tile([P, NQ, PACK], BF16, name="h03", tag="h1_first", align_bytes=64)[:]
+        h_apart[(0, 3)] = keep.tile([P, NQ, PACK], BF16, name="h03", tag="h1_first", align_bytes=64)[:]
         gated(0, 3, slice(0, NQ // 8))
         quantise_quarter(1, 2, h[1][:, 2], "gate0")
         gated(0, 3, slice(NQ // 8, NQ // 4))
-        h_late[(1, 3)] = keep.tile([P, NQ, PACK], BF16, name="h13", tag="h_codes10", align_bytes=64)[:]
+        h_apart[(1, 3)] = keep.tile([P, NQ, PACK], BF16, name="h13", tag="h_codes10", align_bytes=64)[:]
         gated(1, 3)
         down(2, 3)
         nc.scalar.activation(window(2, 3), y_sb[:, HALF : 3 * NQ], COPY)
-        quantise_quarter(0, 3, h_late[(0, 3)])
-        quantise_quarter(1, 3, h_late[(1, 3)])
+        quantise_quarter(0, 3, h_apart[(0, 3)])
+        quantise_quarter(1, 3, h_apart[(1, 3)])
         down(3, 4)
         nc.vector.tensor_copy(window(3, 4), y_sb[:, 3 * NQ : S])
         nc.sync.dma_start(out=out, in_=result[:])

@@ -33,7 +33,8 @@ BEFORE_SILU = 24
 AFTER_SILU = 40
 ALL_STEPS = 256
 CHUNK_END = 160
-BESIDE_GATING = 32
+NO_STEPS = 0
+LAST_SHARE = 32
 LAST_CUT = 384
 EARLY_QUARTERS = 2
 
@@ -176,9 +177,9 @@ def tile_picked_depth_glu_silu_sub_p_kernel(tc, x_words, x_scales, w1, w3, w2, g
                     matmul(banks[(W3, c, q)][:, t, :], (W3, g, c), t, slice(q * NQ, (q + 1) * NQ), first, final)
 
         act = [keep.tile([P, PACK, S], F32, name="act%d" % c, align_bytes=64) for c in range(CHUNKS)]
-        h = [keep.tile([P, QUARTERS, NQ, PACK], BF16, name="h%d" % c, align_bytes=64) for c in range(CHUNKS)]
+        h = [keep.tile([P, QUARTERS, NQ, PACK], BF16, name="h0", align_bytes=64)]
         h_apart = {}
-        h_codes = {(1, 0): keep.tile([P, HALF], U32, name="h_codes10", align_bytes=64)[:]}
+        h_codes = {}
         h_scales = [keep.tile([P, S], U8, name="h_scales%d" % c, align_bytes=64) for c in range(CHUNKS)]
 
         def silu(c):
@@ -187,7 +188,7 @@ def tile_picked_depth_glu_silu_sub_p_kernel(tc, x_words, x_scales, w1, w3, w2, g
 
         def gated(c, q, part=slice(0, NQ // 4)):
             nc.vector.tensor_tensor(
-                h_apart.get((c, q), h[c][:, q]).rearrange("p (a i) t -> p a t i", i=4)[:, part],
+                (h_apart[(c, q)] if c else h[0][:, q]).rearrange("p (a i) t -> p a t i", i=4)[:, part],
                 banks[(W3, c, q)][:].rearrange("p t (a i) -> p a t i", i=4)[:, part],
                 act[c][:, :, q * NQ : (q + 1) * NQ].rearrange("p t (a i) -> p a t i", i=4)[:, part],
                 MULT,
@@ -219,30 +220,34 @@ def tile_picked_depth_glu_silu_sub_p_kernel(tc, x_words, x_scales, w1, w3, w2, g
         multiply_w3(2, 0)
         quantise((W3, 0, 1), 0, PACK)
         multiply_w3(0, 1)
-        round_by_pairs((W3, 1, 1), BESIDE_GATING)
+        round_by_pairs((W3, 1, 1), NO_STEPS)
         quantise((W3, 1, 1), 0, 2)
         quantise((W3, 1, 1), 2, 4)
         multiply_w3(1, 1)
+        for q in range(QUARTERS):
+            gated(0, q)
         pair = [keep.tile([P, 2, P, PACK], BF16, name="pair%d" % u, align_bytes=64) for u in range(2)]
-        for (view, col0, col1), second in zip(raw[last], (nc.scalar.copy, nc.vector.tensor_copy)):
-            src = view.rearrange("p j (m u v) -> p u m j v", u=2, v=2)
-            for u, copy in ((1, second), (0, nc.vector.tensor_copy)):
-                copy(pair[u][:].rearrange("p v m j -> p m j v")[:, col0 // 4 : col1 // 4], src[:, u])
+        dst = [pair[u][:].rearrange("p v m j -> p m j v") for u in range(2)]
+        first, second = [view.rearrange("p j (m u v) -> p u m j v", u=2, v=2) for view, col0, col1 in raw[last]]
+        cut = LAST_CUT // PACK
+        nc.vector.tensor_copy(dst[0][:, 0:LAST_SHARE], first[:, 0, 0:LAST_SHARE])
+        nc.scalar.copy(dst[0][:, LAST_SHARE:cut], first[:, 0, LAST_SHARE:cut])
+        nc.scalar.copy(dst[1][:, 0:cut], first[:, 1])
+        for u in range(2):
+            nc.vector.tensor_copy(dst[u][:, cut:P], second[:, u])
         codes[last] = keep.tile([P, KP], U32, name="codes_last", align_bytes=64)
         scales[last] = keep.tile([P, KP], U8, name="scales_last", align_bytes=64)
-        for q in range(QUARTERS - 1):
-            gated(0, q)
-        for u in (1, 0):
+        for u in range(2):
             cols = slice(u * HALF, (u + 1) * HALF)
             nc.vector.quantize_mx(
                 out=codes[last][:, cols].bitcast(FP8X4), scales=scales[last][:, cols], in_=pair[u][:].rearrange("p v m j -> p (v m j)")
             )
-        multiply_w3(last[1], last[2], (2, 3, 0, 1))
+        multiply_w3(last[1], last[2])
         multiply_late(2)
-        early_codes = keep.tile([P, 3 * NQ], U32, name="early_codes", tag="pair0", align_bytes=64)
-        h_codes[(0, 0)], h_codes[(0, 2)] = early_codes[:, 0:HALF], early_codes[:, HALF : 3 * NQ]
-        quantise_h(0, 0, 2, h[0][:, 0:2].rearrange("p q n t -> p (q n t)"))
-        quantise_h(0, 2, 3, h[0][:, 2].rearrange("p n t -> p (n t)"))
+        early_codes = keep.tile([P, S], U32, name="early_codes", tag="pair1", align_bytes=64)
+        nc.vector.quantize_mx(out=early_codes[:].bitcast(FP8X4), scales=h_scales[0][:], in_=h[0][:].rearrange("p q n t -> p (q n t)"))
+        for q in range(QUARTERS):
+            h_codes[(0, q)] = early_codes[:, q * NQ : (q + 1) * NQ]
 
         w2_rounded = keep.tile([P, CHUNKS, N, PACK], BF16, name="w2_rounded", align_bytes=64)
         for c in range(CHUNKS):
@@ -252,51 +257,55 @@ def tile_picked_depth_glu_silu_sub_p_kernel(tc, x_words, x_scales, w1, w3, w2, g
             )
         w2_codes = keep.tile([P, CHUNKS * N], U32, name="w2_codes", align_bytes=64)
         w2_scales = keep.tile([P, CHUNKS * N], U8, name="w2_scales", align_bytes=64)
-        y_sb = keep.tile([P, S], F32, name="y_sb", align_bytes=64)
 
-        def down(q0, q1):
-            cols = slice(q0 * NQ, q1 * NQ)
-            y = psum.tile([P, (q1 - q0) * NQ], F32, name="y", tag="bank%d" % q0)
+        def down(q):
+            y = psum.tile([P, NQ], F32, name="y", tag="bank%d" % q)
             for c in range(CHUNKS):
                 nc.tensor.matmul_mx(
                     out=y[:],
                     lhsT=w2_codes[:, c * N : (c + 1) * N].bitcast(FP8X4),
                     lhsT_scale=w2_scales[:, c * N : (c + 1) * N],
-                    rhs=h_codes[(c, q0)].bitcast(FP8X4),
-                    rhs_scale=h_scales[c][:, cols],
+                    rhs=h_codes[(c, q)].bitcast(FP8X4),
+                    rhs_scale=h_scales[c][:, q * NQ : (q + 1) * NQ],
                     start=(c == 0),
                     stop=(c == CHUNKS - 1),
                 )
-            nc.vector.tensor_tensor(y_sb[:, cols], y[:], gates[q0 // 2][:, q0 % 2 * NQ : (q1 - 1) % 2 * NQ + NQ], MULT)
+            return y
 
-        def quantise_quarter(c, q, src, tag=None):
-            name = "h_quarter%d%d" % (c, q)
-            h_codes[(c, q)] = keep.tile([P, NQ], U32, name=name, tag=tag or name, align_bytes=64)[:]
-            quantise_h(c, q, q + 1, src.rearrange("p n t -> p (n t)"))
+        def gate_of(q):
+            return gates[q // 2][:, q % 2 * NQ : (q % 2 + 1) * NQ]
 
-        def window(q0, q1):
-            return result[:].indirect(offsets[:, q0 * NQ // 16 : q1 * NQ // 16])
+        def window(q):
+            return result[:].indirect(offsets[:, q * NQ // 16 : (q + 1) * NQ // 16])
 
-        first_half = keep.tile([P, 2, NQ, PACK], BF16, name="h1_first", align_bytes=64)
-        h_apart[(1, 0)], h_apart[(1, 1)] = first_half[:, 0], first_half[:, 1]
-        gated(1, 0)
-        gated(1, 1)
+        def product(q, tag):
+            h_apart[(1, q)] = keep.tile([P, NQ, PACK], BF16, name="h1%d" % q, tag=tag, align_bytes=64)[:]
+            gated(1, q)
+
+        def quantise_quarter(q):
+            h_codes[(1, q)] = keep.tile([P, NQ], U32, name="h_codes1%d" % q, align_bytes=64)[:]
+            quantise_h(1, q, q + 1, h_apart[(1, q)].rearrange("p n t -> p (n t)"))
+
+        def weigh(q, tag):
+            weighted = keep.tile([P, NQ], F32, name="weighted%d" % q, tag=tag, align_bytes=64)
+            nc.vector.tensor_tensor(weighted[:], down(q)[:], gate_of(q), MULT)
+            return weighted[:]
+
+        product(0, "h10")
         nc.vector.quantize_mx(out=w2_codes[:].bitcast(FP8X4), scales=w2_scales[:], in_=w2_rounded[:].rearrange("p c n t -> p (c n t)"))
-        quantise_h(1, 0, 2, first_half[:].rearrange("p q n t -> p (q n t)"))
-        down(0, 2)
-        nc.scalar.activation(window(0, 2), y_sb[:, 0:HALF], COPY)
+        quantise_quarter(0)
+        product(1, "h11")
+        quantise_quarter(1)
+        nc.scalar.activation(window(0), weigh(0, "weighted0"), COPY)
         multiply_late(3)
-        gated(1, 2)
-        h_apart[(0, 3)] = keep.tile([P, NQ, PACK], BF16, name="h03", tag="h1_first", align_bytes=64)[:]
-        gated(0, 3, slice(0, NQ // 8))
-        quantise_quarter(1, 2, h[1][:, 2], "gate0")
-        gated(0, 3, slice(NQ // 8, NQ // 4))
-        h_apart[(1, 3)] = keep.tile([P, NQ, PACK], BF16, name="h13", tag="h_codes10", align_bytes=64)[:]
-        gated(1, 3)
-        down(2, 3)
-        nc.scalar.activation(window(2, 3), y_sb[:, HALF : 3 * NQ], COPY)
-        quantise_quarter(0, 3, h_apart[(0, 3)])
-        quantise_quarter(1, 3, h_apart[(1, 3)])
-        down(3, 4)
-        nc.vector.tensor_copy(window(3, 4), y_sb[:, 3 * NQ : S])
+        product(2, "h11")
+        nc.scalar.activation(window(1), weigh(1, "weighted1"), COPY)
+        quantise_quarter(2)
+        product(3, "gate0")
+        weighted = weigh(2, "weighted2")
+        quantise_quarter(3)
+        nc.vector.tensor_copy(window(2), weighted)
+        y_last = keep.tile([P, NQ], F32, name="y_last", align_bytes=64)
+        nc.scalar.copy(y_last[:], down(3)[:])
+        nc.vector.tensor_tensor(window(3), y_last[:], gate_of(3), MULT)
         nc.sync.dma_start(out=out, in_=result[:])

@@ -36,7 +36,7 @@ CHUNK_END = 160
 NO_STEPS = 0
 LAST_SHARE = 32
 LAST_CUT = 384
-EARLY_QUARTERS = 2
+EARLY_QUARTERS = 3
 
 
 def tile_picked_depth_glu_silu_sub_p_kernel(tc, x_words, x_scales, w1, w3, w2, gate, offs, out):
@@ -160,9 +160,9 @@ def tile_picked_depth_glu_silu_sub_p_kernel(tc, x_words, x_scales, w1, w3, w2, g
                     banks[(W1, c, t)] = psum.tile([P, S], F32, name="acc", tag="bank%d" % (c * PACK + t))
                 matmul(banks[(W1, c, t)][:], (W1, g, c), t, slice(0, S), g == 0, g == PASSES - 1)
 
-        def multiply_late(q):
-            banks[(W3, 1, q)] = psum.tile([P, PACK, NQ], F32, name="acc", tag="bank%d" % (QUARTERS + q))
-            order = [(g, t) for g in (PASSES - 1, 0, 1) for t in range(PACK)]
+        def multiply_late(q, tag):
+            banks[(W3, 1, q)] = psum.tile([P, PACK, NQ], F32, name="acc", tag=tag)
+            order = [(g, t) for g in range(PASSES) for t in range(PACK)]
             for g, t in order:
                 matmul(banks[(W3, 1, q)][:, t, :], (W3, g, 1), t, slice(q * NQ, (q + 1) * NQ), (g, t) == order[0], (g, t) == order[-1])
 
@@ -243,7 +243,6 @@ def tile_picked_depth_glu_silu_sub_p_kernel(tc, x_words, x_scales, w1, w3, w2, g
                 out=codes[last][:, cols].bitcast(FP8X4), scales=scales[last][:, cols], in_=pair[u][:].rearrange("p v m j -> p (v m j)")
             )
         multiply_w3(last[1], last[2])
-        multiply_late(2)
         early_codes = keep.tile([P, S], U32, name="early_codes", tag="pair1", align_bytes=64)
         nc.vector.quantize_mx(out=early_codes[:].bitcast(FP8X4), scales=h_scales[0][:], in_=h[0][:].rearrange("p q n t -> p (q n t)"))
         for q in range(QUARTERS):
@@ -297,10 +296,10 @@ def tile_picked_depth_glu_silu_sub_p_kernel(tc, x_words, x_scales, w1, w3, w2, g
         product(1, "h11")
         quantise_quarter(1)
         nc.scalar.activation(window(0), weigh(0, "weighted0"), COPY)
-        multiply_late(3)
         product(2, "h11")
         nc.scalar.activation(window(1), weigh(1, "weighted1"), COPY)
         quantise_quarter(2)
+        multiply_late(3, "bank5")
         product(3, "gate0")
         weighted = weigh(2, "weighted2")
         quantise_quarter(3)

@@ -13,6 +13,7 @@ U16 = mybir.dt.uint16
 U8 = mybir.dt.uint8
 FP8X4 = mybir.dt.float8_e4m3fn_x4
 MULT = mybir.AluOpType.mult
+ADD = mybir.AluOpType.add
 SILU = mybir.ActivationFunctionType.Silu
 COPY = mybir.ActivationFunctionType.Copy
 
@@ -33,7 +34,7 @@ BEFORE_SILU = 24
 AFTER_SILU = 40
 ALL_STEPS = 256
 CHUNK_END = 160
-NO_STEPS = 0
+GPSIMD_FROM = 48
 LAST_SHARE = 32
 LAST_CUT = 384
 EARLY_QUARTERS = 3
@@ -105,8 +106,9 @@ def tile_picked_depth_glu_silu_sub_p_kernel(tc, x_words, x_scales, w1, w3, w2, g
 
         rounded, codes, scales, banks = {}, {}, {}, {}
 
-        def round_piece(key, share, codes_tag=None):
-            rounded[key] = stage.tile([P, PACK, P, PACK], BF16, name="rounded", align_bytes=64)
+        def round_piece(key, share, codes_tag=None, tag="rounded"):
+            pool = stage if tag == "rounded" else keep
+            rounded[key] = pool.tile([P, PACK, P, PACK], BF16, name="rounded", tag=tag, align_bytes=64)
             src = raw[key][0][0].rearrange("p j (m u v) -> p m u j v", u=2, v=2)
             dst = rounded[key][:].rearrange("p (u v) m j -> p m u j v", v=2)
             cut = share * P // ALL_VECTOR
@@ -209,7 +211,7 @@ def tile_picked_depth_glu_silu_sub_p_kernel(tc, x_words, x_scales, w1, w3, w2, g
                     silu(c)
         prepare((W3, 0, 0), ALL_VECTOR)
         multiply_w3(0, 0)
-        round_piece((W3, 0, 1), AFTER_SILU, codes_tag="w3_20_0")
+        round_piece((W3, 0, 1), AFTER_SILU, codes_tag="w3_20_0", tag="rounded_late")
         round_by_pairs((W3, 1, 0), ALL_STEPS)
         quantise((W3, 1, 0), 0, 2)
         quantise((W3, 1, 0), 2, 4)
@@ -220,12 +222,27 @@ def tile_picked_depth_glu_silu_sub_p_kernel(tc, x_words, x_scales, w1, w3, w2, g
         multiply_w3(2, 0)
         quantise((W3, 0, 1), 0, PACK)
         multiply_w3(0, 1)
-        round_by_pairs((W3, 1, 1), NO_STEPS)
-        quantise((W3, 1, 1), 0, 2)
-        quantise((W3, 1, 1), 2, 4)
-        multiply_w3(1, 1)
+        middle = (W3, 1, 1)
+        rounded[middle] = keep.tile([P, PACK, P, PACK], BF16, name="rounded_middle", tag="rounded_late", align_bytes=64)
+        src = raw[middle][0][0].rearrange("p j (m u v) -> p u m j v", u=2, v=2)
+        dst = rounded[middle][:].rearrange("p (u v) m j -> p u m j v", v=2)
+        nc.scalar.copy(dst[:, 0], src[:, 0])
+        nc.scalar.copy(dst[:, 1, 0:GPSIMD_FROM], src[:, 1, 0:GPSIMD_FROM])
+        nc.gpsimd.tensor_scalar(
+            dst[:, 1, GPSIMD_FROM:P].rearrange("p m j v -> p v m j"),
+            src[:, 1, GPSIMD_FROM:P].rearrange("p m j v -> p v m j"),
+            1.0,
+            0.0,
+            MULT,
+            ADD,
+        )
+        codes[middle] = keep.tile([P, KP], U32, name="codes_middle", align_bytes=64)
+        scales[middle] = keep.tile([P, KP], U8, name="scales_middle", align_bytes=64)
         for q in range(QUARTERS):
             gated(0, q)
+        quantise(middle, 0, 2)
+        quantise(middle, 2, 4)
+        multiply_w3(1, 1)
         pair = [keep.tile([P, 2, P, PACK], BF16, name="pair%d" % u, align_bytes=64) for u in range(2)]
         dst = [pair[u][:].rearrange("p v m j -> p m j v") for u in range(2)]
         first, second = [view.rearrange("p j (m u v) -> p u m j v", u=2, v=2) for view, col0, col1 in raw[last]]

@@ -172,7 +172,7 @@ def tile_picked_depth_glu_silu_sub_p_kernel(tc, x_words, x_scales, w1, w3, w2, g
             quarters = range(QUARTERS if c == 0 else EARLY_QUARTERS)
             if g == 0:
                 for q in quarters:
-                    banks[(W3, c, q)] = psum.tile([P, PACK, NQ], F32, name="acc", tag="bank%d" % (c * QUARTERS + q))
+                    banks[(W3, c, q)] = psum.tile([P, PACK, NQ], F32, name="acc", tag="bank%d" % q)
             for q in quarters:
                 for t in ts:
                     first, final = g == 0 and t == ts[0], g == PASSES - 1 and t == ts[-1]
@@ -275,7 +275,7 @@ def tile_picked_depth_glu_silu_sub_p_kernel(tc, x_words, x_scales, w1, w3, w2, g
         w2_scales = keep.tile([P, CHUNKS * N], U8, name="w2_scales", align_bytes=64)
 
         def down(q):
-            y = psum.tile([P, NQ], F32, name="y", tag="bank%d" % q)
+            y = psum.tile([P, NQ], F32, name="y", tag="bank%d" % (QUARTERS + q))
             for c in range(CHUNKS):
                 nc.tensor.matmul_mx(
                     out=y[:],
@@ -316,7 +316,7 @@ def tile_picked_depth_glu_silu_sub_p_kernel(tc, x_words, x_scales, w1, w3, w2, g
         product(2, "h11")
         nc.scalar.activation(window(1), weigh(1, "weighted1"), COPY)
         quantise_quarter(2)
-        multiply_late(3, "bank5")
+        multiply_late(3, "bank1")
         product(3, "gate0")
         weighted = weigh(2, "weighted2")
         quantise_quarter(3)

@@ -37,7 +37,6 @@ CHUNK_END = 160
 GPSIMD_FROM = 48
 LAST_SHARE = 32
 LAST_CUT = 384
-EARLY_QUARTERS = 3
 
 
 def tile_picked_depth_glu_silu_sub_p_kernel(tc, x_words, x_scales, w1, w3, w2, gate, offs, out):
@@ -162,14 +161,8 @@ def tile_picked_depth_glu_silu_sub_p_kernel(tc, x_words, x_scales, w1, w3, w2, g
                     banks[(W1, c, t)] = psum.tile([P, S], F32, name="acc", tag="bank%d" % (c * PACK + t))
                 matmul(banks[(W1, c, t)][:], (W1, g, c), t, slice(0, S), g == 0, g == PASSES - 1)
 
-        def multiply_late(q, tag):
-            banks[(W3, 1, q)] = psum.tile([P, PACK, NQ], F32, name="acc", tag=tag)
-            order = [(g, t) for g in range(PASSES) for t in range(PACK)]
-            for g, t in order:
-                matmul(banks[(W3, 1, q)][:, t, :], (W3, g, 1), t, slice(q * NQ, (q + 1) * NQ), (g, t) == order[0], (g, t) == order[-1])
-
         def multiply_w3(g, c, ts=range(PACK)):
-            quarters = range(QUARTERS if c == 0 else EARLY_QUARTERS)
+            quarters = range(QUARTERS)
             if g == 0:
                 for q in quarters:
                     banks[(W3, c, q)] = psum.tile([P, PACK, NQ], F32, name="acc", tag="bank%d" % q)
@@ -316,7 +309,6 @@ def tile_picked_depth_glu_silu_sub_p_kernel(tc, x_words, x_scales, w1, w3, w2, g
         product(2, "h11")
         nc.scalar.activation(window(1), weigh(1, "weighted1"), COPY)
         quantise_quarter(2)
-        multiply_late(3, "bank1")
         product(3, "gate0")
         weighted = weigh(2, "weighted2")
         quantise_quarter(3)

@@ -35,8 +35,7 @@ AFTER_SILU = 40
 ALL_STEPS = 256
 CHUNK_END = 160
 GPSIMD_FROM = 48
-LAST_SHARE = 32
-LAST_CUT = 384
+LAST_CUT = 256
 
 
 def tile_picked_depth_glu_silu_sub_p_kernel(tc, x_words, x_scales, w1, w3, w2, gate, offs, out):
@@ -240,11 +239,10 @@ def tile_picked_depth_glu_silu_sub_p_kernel(tc, x_words, x_scales, w1, w3, w2, g
         dst = [pair[u][:].rearrange("p v m j -> p m j v") for u in range(2)]
         first, second = [view.rearrange("p j (m u v) -> p u m j v", u=2, v=2) for view, col0, col1 in raw[last]]
         cut = LAST_CUT // PACK
-        nc.vector.tensor_copy(dst[0][:, 0:LAST_SHARE], first[:, 0, 0:LAST_SHARE])
-        nc.scalar.copy(dst[0][:, LAST_SHARE:cut], first[:, 0, LAST_SHARE:cut])
-        nc.scalar.copy(dst[1][:, 0:cut], first[:, 1])
         for u in range(2):
-            nc.vector.tensor_copy(dst[u][:, cut:P], second[:, u])
+            nc.scalar.copy(dst[u][:, 0:cut], first[:, u])
+        nc.vector.tensor_copy(dst[0][:, cut:P], second[:, 0])
+        nc.scalar.copy(dst[1][:, cut:P], second[:, 1])
         codes[last] = keep.tile([P, KP], U32, name="codes_last", align_bytes=64)
         scales[last] = keep.tile([P, KP], U8, name="scales_last", align_bytes=64)
         for u in range(2):

@@ -241,8 +241,10 @@ def tile_picked_depth_glu_silu_sub_p_kernel(tc, x_words, x_scales, w1, w3, w2, g
         cut = LAST_CUT // PACK
         for u in range(2):
             nc.scalar.copy(dst[u][:, 0:cut], first[:, u])
-        nc.vector.tensor_copy(dst[0][:, cut:P], second[:, 0])
-        nc.scalar.copy(dst[1][:, cut:P], second[:, 1])
+        half = (P - cut) // 2
+        for u in range(2):
+            nc.vector.tensor_copy(dst[u][:, cut : cut + half], second[:, u, 0:half])
+            nc.scalar.copy(dst[u][:, cut + half : P], second[:, u, half : 2 * half])
         codes[last] = keep.tile([P, KP], U32, name="codes_last", align_bytes=64)
         scales[last] = keep.tile([P, KP], U8, name="scales_last", align_bytes=64)
         for u in range(2):

@@ -36,6 +36,7 @@ ALL_STEPS = 256
 CHUNK_END = 160
 GPSIMD_FROM = 48
 LAST_CUT = 256
+EARLY_QUARTERS = 3
 
 
 def tile_picked_depth_glu_silu_sub_p_kernel(tc, x_words, x_scales, w1, w3, w2, gate, offs, out):
@@ -160,8 +161,14 @@ def tile_picked_depth_glu_silu_sub_p_kernel(tc, x_words, x_scales, w1, w3, w2, g
                     banks[(W1, c, t)] = psum.tile([P, S], F32, name="acc", tag="bank%d" % (c * PACK + t))
                 matmul(banks[(W1, c, t)][:], (W1, g, c), t, slice(0, S), g == 0, g == PASSES - 1)
 
+        def multiply_late(q, tag):
+            banks[(W3, 1, q)] = psum.tile([P, PACK, NQ], F32, name="acc", tag=tag)
+            order = [(g, t) for g in range(PASSES) for t in range(PACK)]
+            for g, t in order:
+                matmul(banks[(W3, 1, q)][:, t, :], (W3, g, 1), t, slice(q * NQ, (q + 1) * NQ), (g, t) == order[0], (g, t) == order[-1])
+
         def multiply_w3(g, c, ts=range(PACK)):
-            quarters = range(QUARTERS)
+            quarters = range(QUARTERS if c == 0 else EARLY_QUARTERS)
             if g == 0:
                 for q in quarters:
                     banks[(W3, c, q)] = psum.tile([P, PACK, NQ], F32, name="acc", tag="bank%d" % q)
@@ -309,6 +316,7 @@ def tile_picked_depth_glu_silu_sub_p_kernel(tc, x_words, x_scales, w1, w3, w2, g
         product(2, "h11")
         nc.scalar.activation(window(1), weigh(1, "weighted1"), COPY)
         quantise_quarter(2)
+        multiply_late(3, "bank1")
         product(3, "gate0")
         weighted = weigh(2, "weighted2")
         quantise_quarter(3)

@@ -34,7 +34,8 @@ BEFORE_SILU = 24
 AFTER_SILU = 40
 ALL_STEPS = 256
 CHUNK_END = 160
-GPSIMD_FROM = 48
+GPSIMD_FROM = 32
+LAST_SHARE = 32
 LAST_CUT = 256
 EARLY_QUARTERS = 3
 
@@ -246,8 +247,9 @@ def tile_picked_depth_glu_silu_sub_p_kernel(tc, x_words, x_scales, w1, w3, w2, g
         dst = [pair[u][:].rearrange("p v m j -> p m j v") for u in range(2)]
         first, second = [view.rearrange("p j (m u v) -> p u m j v", u=2, v=2) for view, col0, col1 in raw[last]]
         cut = LAST_CUT // PACK
-        for u in range(2):
-            nc.scalar.copy(dst[u][:, 0:cut], first[:, u])
+        nc.vector.tensor_copy(dst[0][:, 0:LAST_SHARE], first[:, 0, 0:LAST_SHARE])
+        nc.scalar.copy(dst[0][:, LAST_SHARE:cut], first[:, 0, LAST_SHARE:cut])
+        nc.scalar.copy(dst[1][:, 0:cut], first[:, 1])
         half = (P - cut) // 2
         for u in range(2):
             nc.vector.tensor_copy(dst[u][:, cut : cut + half], second[:, u, 0:half])

from contextlib import ExitStack

import concourse.mybir as mybir

K, T, S, H, N = 1536, 1024, 512, 1024, 128
FLOPS = 2 * K * H * S * 2 + 2 * H * N * S

F32 = mybir.dt.float32
BF16 = mybir.dt.bfloat16
I32 = mybir.dt.int32
U32 = mybir.dt.uint32
U16 = mybir.dt.uint16
U8 = mybir.dt.uint8
FP8X4 = mybir.dt.float8_e4m3fn_x4
MULT = mybir.AluOpType.mult
ADD = mybir.AluOpType.add
SILU = mybir.ActivationFunctionType.Silu
COPY = mybir.ActivationFunctionType.Copy

P = 128
PACK = 4
KP = P * PACK
PASSES = K // KP
CHUNKS = H // KP
QUARTERS = 4
NQ = S // QUARTERS
HALF = S // 2
W1, W3 = 0, 1

EVEN = 32
BALANCED = 44
ALL_VECTOR = 64
BEFORE_SILU = 24
AFTER_SILU = 40
ALL_STEPS = 256
CHUNK_END = 160
GPSIMD_FROM = 32
LAST_SHARE = 32
LAST_CUT = 256
EARLY_QUARTERS = 3


def tile_picked_depth_glu_silu_sub_p_kernel(tc, x_words, x_scales, w1, w3, w2, gate, offs, out):
    nc = tc.nc
    with ExitStack() as ctx:
        keep = ctx.enter_context(tc.tile_pool(name="keep", bufs=1))
        stage = ctx.enter_context(tc.tile_pool(name="stage", bufs=8))
        psum = ctx.enter_context(tc.psum_pool(name="psum", bufs=1))

        offsets = keep.tile([P, S // 16], U16, name="offsets")

        warm_in = keep.tile([P, 8], F32, name="warm_in")
        warm_out = keep.tile([P, 8], F32, name="warm_out")
        x_scale_rows = keep.tile([P, T], U8, name="x_scale_rows", align_bytes=64)
        nc.gpsimd.memset(x_scale_rows[:].bitcast(I32), 0)
        nc.vector.memset(warm_in[:], 0.0)
        nc.scalar.activation(warm_out[:], warm_in[:], SILU)

        x_all = keep.tile([P, PASSES * T], I32, name="x_all", align_bytes=64)
        nc.sync.dma_start(
            out=x_all[:].rearrange("p (g n) -> p g n", g=PASSES), in_=x_words.rearrange("g p n t -> p g (n t)").bitcast(I32)
        )
        nc.sync.dma_start(offsets[:], offs)
        raw = {}

        def k_rows(w, g):
            return w[g * KP : (g + 1) * KP, :].rearrange("(p j) h -> p j h", j=PACK)

        for g in range(PASSES):
            if g == 1:
                for d in range(P // 32):
                    nc.sync.dma_start(
                        out=x_scale_rows[:].bitcast(I32)[32 * d : 32 * d + 4 * PASSES, :],
                        in_=x_scales[:, 4 * d : 4 * d + 4, :].bitcast(I32),
                    )
            wide = keep.tile([P, PACK, H], F32, name="w1_pass%d" % g, align_bytes=64)
            nc.sync.dma_start(out=wide[:], in_=k_rows(w1, g))
            for c in range(CHUNKS):
                raw[(W1, g, c)] = [(wide[:, :, c * KP : (c + 1) * KP], 0, KP)]
        wide = keep.tile([P, PACK, H], F32, name="w3_pass0", align_bytes=64)
        nc.sync.dma_start(out=wide[:], in_=k_rows(w3, 0))
        for c in range(CHUNKS):
            raw[(W3, 0, c)] = [(wide[:, :, c * KP : (c + 1) * KP], 0, KP)]
        last = (W3, PASSES - 1, CHUNKS - 1)
        for c in range(CHUNKS):
            for g in range(1, PASSES):
                key = (W3, g, c)
                raw[key] = []
                for col0, col1 in [(0, LAST_CUT), (LAST_CUT, KP)] if key == last else [(0, KP)]:
                    tag = "w3_%d%d_%d" % (g, c, col0)
                    part = keep.tile([P, PACK, col1 - col0], F32, name=tag, tag=tag, align_bytes=64)
                    nc.sync.dma_start(out=part[:], in_=k_rows(w3, g)[:, :, c * KP + col0 : c * KP + col1])
                    raw[key].append((part[:], col0, col1))
        w2_raw = [keep.tile([P, PACK, N], F32, name="w2_raw%d" % c, align_bytes=64) for c in range(CHUNKS)]
        for c in range(CHUNKS):
            nc.sync.dma_start(out=w2_raw[c][:], in_=w2[c * KP : (c + 1) * KP, :].rearrange("(p t) n -> p t n", t=PACK))
        gates = [keep.tile([P, HALF], F32, name="gate%d" % u, align_bytes=64) for u in range(2)]
        for u in range(2):
            nc.sync.dma_start(out=gates[u][:], in_=gate[:, u * HALF : (u + 1) * HALF])

        result = keep.tile([P, T], F32, name="result", align_bytes=64)
        nc.vector.memset(result[:], 0.0)

        x_picked = [keep.tile([P, S], U32, name="x_picked%d" % g, align_bytes=64) for g in range(PASSES)]
        x_picked_scales = keep.tile([P, S], U8, name="x_picked_scales", align_bytes=64)

        rounded, codes, scales, banks = {}, {}, {}, {}

        def round_piece(key, share, codes_tag=None, tag="rounded"):
            pool = stage if tag == "rounded" else keep
            rounded[key] = pool.tile([P, PACK, P, PACK], BF16, name="rounded", tag=tag, align_bytes=64)
            src = raw[key][0][0].rearrange("p j (m u v) -> p m u j v", u=2, v=2)
            dst = rounded[key][:].rearrange("p (u v) m j -> p m u j v", v=2)
            cut = share * P // ALL_VECTOR
            nc.vector.tensor_copy(dst[:, 0:cut], src[:, 0:cut])
            if cut < P:
                nc.scalar.copy(dst[:, cut:P], src[:, cut:P])
            codes[key] = keep.tile([P, KP], U32, name="codes%d%d%d" % key, tag=codes_tag or "codes%d%d%d" % key, align_bytes=64)
            scales[key] = keep.tile([P, KP], U8, name="scales%d%d%d" % key, align_bytes=64)

        def round_by_pairs(key, cut):
            rounded[key] = stage.tile([P, PACK, P, PACK], BF16, name="rounded", align_bytes=64)
            src = raw[key][0][0].rearrange("p j (m u v) -> p u m j v", u=2, v=2)
            dst = rounded[key][:].rearrange("p (u v) m j -> p u m j v", v=2)
            for u in range(2):
                n = min(P, max(0, cut - u * P))
                if n > 0:
                    nc.vector.tensor_copy(dst[:, u, 0:n], src[:, u, 0:n])
                if n < P:
                    nc.scalar.copy(dst[:, u, n:P], src[:, u, n:P])
            codes[key] = keep.tile([P, KP], U32, name="codes%d%d%d" % key, align_bytes=64)
            scales[key] = keep.tile([P, KP], U8, name="scales%d%d%d" % key, align_bytes=64)

        def quantise(key, t0, t1):
            cols = slice(t0 * P, t1 * P)
            nc.vector.quantize_mx(
                out=codes[key][:, cols].bitcast(FP8X4),
                scales=scales[key][:, cols],
                in_=rounded[key][:, t0:t1].rearrange("p t m j -> p (t m j)"),
            )

        def prepare(key, share):
            round_piece(key, share)
            quantise(key, 0, PACK)

        def matmul(acc, key, t, cols, start, stop):
            g = key[1]
            mc = slice(t * P, (t + 1) * P)
            nc.tensor.matmul_mx(
                out=acc,
                lhsT=codes[key][:, mc].bitcast(FP8X4),
                lhsT_scale=scales[key][:, mc],
                rhs=x_picked[g][:, cols].bitcast(FP8X4),
                rhs_scale=x_picked_scales[4 * g : P, cols],
                start=start,
                stop=stop,
            )

        def multiply_w1(g, c):
            for t in range(PACK):
                if g == 0:
                    banks[(W1, c, t)] = psum.tile([P, S], F32, name="acc", tag="bank%d" % (c * PACK + t))
                matmul(banks[(W1, c, t)][:], (W1, g, c), t, slice(0, S), g == 0, g == PASSES - 1)

        def multiply_late(q, tag):
            banks[(W3, 1, q)] = psum.tile([P, PACK, NQ], F32, name="acc", tag=tag)
            order = [(g, t) for g in range(PASSES) for t in range(PACK)]
            for g, t in order:
                matmul(banks[(W3, 1, q)][:, t, :], (W3, g, 1), t, slice(q * NQ, (q + 1) * NQ), (g, t) == order[0], (g, t) == order[-1])

        def multiply_w3(g, c, ts=range(PACK)):
            quarters = range(QUARTERS if c == 0 else EARLY_QUARTERS)
            if g == 0:
                for q in quarters:
                    banks[(W3, c, q)] = psum.tile([P, PACK, NQ], F32, name="acc", tag="bank%d" % q)
            for q in quarters:
                for t in ts:
                    first, final = g == 0 and t == ts[0], g == PASSES - 1 and t == ts[-1]
                    matmul(banks[(W3, c, q)][:, t, :], (W3, g, c), t, slice(q * NQ, (q + 1) * NQ), first, final)

        act = [keep.tile([P, PACK, S], F32, name="act%d" % c, align_bytes=64) for c in range(CHUNKS)]
        h = [keep.tile([P, QUARTERS, NQ, PACK], BF16, name="h0", align_bytes=64)]
        h_apart = {}
        h_codes = {}
        h_scales = [keep.tile([P, S], U8, name="h_scales%d" % c, align_bytes=64) for c in range(CHUNKS)]

        def silu(c):
            for t in range(PACK):
                nc.scalar.activation(act[c][:, t], banks[(W1, c, t)][:], SILU)

        def gated(c, q, part=slice(0, NQ // 4)):
            nc.vector.tensor_tensor(
                (h_apart[(c, q)] if c else h[0][:, q]).rearrange("p (a i) t -> p a t i", i=4)[:, part],
                banks[(W3, c, q)][:].rearrange("p t (a i) -> p a t i", i=4)[:, part],
                act[c][:, :, q * NQ : (q + 1) * NQ].rearrange("p t (a i) -> p a t i", i=4)[:, part],
                MULT,
            )

        def quantise_h(c, q0, q1, src):
            nc.vector.quantize_mx(out=h_codes[(c, q0)].bitcast(FP8X4), scales=h_scales[c][:, q0 * NQ : q1 * NQ], in_=src)

        for g in range(PASSES):
            nc.vector.tensor_copy(x_picked[g][:], x_all[:, g * T : (g + 1) * T].bitcast(U32).indirect(offsets[:]))
        nc.vector.tensor_copy(x_picked_scales[:], x_scale_rows[:].indirect(offsets[:]))

        for g in range(PASSES):
            for c in range(CHUNKS):
                prepare((W1, g, c), EVEN if g < PASSES - 1 else (BALANCED, BEFORE_SILU)[c])
                multiply_w1(g, c)
                if g == PASSES - 1:
                    silu(c)
        prepare((W3, 0, 0), ALL_VECTOR)
        multiply_w3(0, 0)
        round_piece((W3, 0, 1), AFTER_SILU, codes_tag="w3_20_0", tag="rounded_late")
        round_by_pairs((W3, 1, 0), ALL_STEPS)
        quantise((W3, 1, 0), 0, 2)
        quantise((W3, 1, 0), 2, 4)
        multiply_w3(1, 0)
        round_by_pairs((W3, 2, 0), CHUNK_END)
        quantise((W3, 2, 0), 0, 2)
        quantise((W3, 2, 0), 2, 4)
        multiply_w3(2, 0)
        quantise((W3, 0, 1), 0, PACK)
        multiply_w3(0, 1)
        middle = (W3, 1, 1)
        rounded[middle] = keep.tile([P, PACK, P, PACK], BF16, name="rounded_middle", tag="rounded_late", align_bytes=64)
        src = raw[middle][0][0].rearrange("p j (m u v) -> p u m j v", u=2, v=2)
        dst = rounded[middle][:].rearrange("p (u v) m j -> p u m j v", v=2)
        nc.scalar.copy(dst[:, 0], src[:, 0])
        nc.scalar.copy(dst[:, 1, 0:GPSIMD_FROM], src[:, 1, 0:GPSIMD_FROM])
        nc.gpsimd.tensor_scalar(
            dst[:, 1, GPSIMD_FROM:P].rearrange("p m j v -> p v m j"),
            src[:, 1, GPSIMD_FROM:P].rearrange("p m j v -> p v m j"),
            1.0,
            0.0,
            MULT,
            ADD,
        )
        codes[middle] = keep.tile([P, KP], U32, name="codes_middle", align_bytes=64)
        scales[middle] = keep.tile([P, KP], U8, name="scales_middle", align_bytes=64)
        for q in range(QUARTERS):
            gated(0, q)
        quantise(middle, 0, 2)
        quantise(middle, 2, 4)
        multiply_w3(1, 1)
        pair = [keep.tile([P, 2, P, PACK], BF16, name="pair%d" % u, align_bytes=64) for u in range(2)]
        dst = [pair[u][:].rearrange("p v m j -> p m j v") for u in range(2)]
        first, second = [view.rearrange("p j (m u v) -> p u m j v", u=2, v=2) for view, col0, col1 in raw[last]]
        cut = LAST_CUT // PACK
        nc.vector.tensor_copy(dst[0][:, 0:LAST_SHARE], first[:, 0, 0:LAST_SHARE])
        nc.scalar.copy(dst[0][:, LAST_SHARE:cut], first[:, 0, LAST_SHARE:cut])
        nc.scalar.copy(dst[1][:, 0:cut], first[:, 1])
        half = (P - cut) // 2
        for u in range(2):
            nc.vector.tensor_copy(dst[u][:, cut : cut + half], second[:, u, 0:half])
            nc.scalar.copy(dst[u][:, cut + half : P], second[:, u, half : 2 * half])
        codes[last] = keep.tile([P, KP], U32, name="codes_last", align_bytes=64)
        scales[last] = keep.tile([P, KP], U8, name="scales_last", align_bytes=64)
        for u in range(2):
            cols = slice(u * HALF, (u + 1) * HALF)
            nc.vector.quantize_mx(
                out=codes[last][:, cols].bitcast(FP8X4), scales=scales[last][:, cols], in_=pair[u][:].rearrange("p v m j -> p (v m j)")
            )
        multiply_w3(last[1], last[2])
        early_codes = keep.tile([P, S], U32, name="early_codes", tag="pair1", align_bytes=64)
        nc.vector.quantize_mx(out=early_codes[:].bitcast(FP8X4), scales=h_scales[0][:], in_=h[0][:].rearrange("p q n t -> p (q n t)"))
        for q in range(QUARTERS):
            h_codes[(0, q)] = early_codes[:, q * NQ : (q + 1) * NQ]

        w2_rounded = keep.tile([P, CHUNKS, N, PACK], BF16, name="w2_rounded", align_bytes=64)
        for c in range(CHUNKS):
            nc.scalar.copy(
                w2_rounded[:, c].rearrange("p (b i) t -> p b t i", i=4),
                w2_raw[c][:].rearrange("p t (b i) -> p b t i", i=4),
            )
        w2_codes = keep.tile([P, CHUNKS * N], U32, name="w2_codes", align_bytes=64)
        w2_scales = keep.tile([P, CHUNKS * N], U8, name="w2_scales", align_bytes=64)

        def down(q):
            y = psum.tile([P, NQ], F32, name="y", tag="bank%d" % (QUARTERS + q))
            for c in range(CHUNKS):
                nc.tensor.matmul_mx(
                    out=y[:],
                    lhsT=w2_codes[:, c * N : (c + 1) * N].bitcast(FP8X4),
                    lhsT_scale=w2_scales[:, c * N : (c + 1) * N],
                    rhs=h_codes[(c, q)].bitcast(FP8X4),
                    rhs_scale=h_scales[c][:, q * NQ : (q + 1) * NQ],
                    start=(c == 0),
                    stop=(c == CHUNKS - 1),
                )
            return y

        def gate_of(q):
            return gates[q // 2][:, q % 2 * NQ : (q % 2 + 1) * NQ]

        def window(q):
            return result[:].indirect(offsets[:, q * NQ // 16 : (q + 1) * NQ // 16])

        def product(q, tag):
            h_apart[(1, q)] = keep.tile([P, NQ, PACK], BF16, name="h1%d" % q, tag=tag, align_bytes=64)[:]
            gated(1, q)

        def quantise_quarter(q):
            h_codes[(1, q)] = keep.tile([P, NQ], U32, name="h_codes1%d" % q, align_bytes=64)[:]
            quantise_h(1, q, q + 1, h_apart[(1, q)].rearrange("p n t -> p (n t)"))

        def weigh(q, tag):
            weighted = keep.tile([P, NQ], F32, name="weighted%d" % q, tag=tag, align_bytes=64)
            nc.vector.tensor_tensor(weighted[:], down(q)[:], gate_of(q), MULT)
            return weighted[:]

        product(0, "h10")
        nc.vector.quantize_mx(out=w2_codes[:].bitcast(FP8X4), scales=w2_scales[:], in_=w2_rounded[:].rearrange("p c n t -> p (c n t)"))
        quantise_quarter(0)
        product(1, "h11")
        quantise_quarter(1)
        nc.scalar.activation(window(0), weigh(0, "weighted0"), COPY)
        product(2, "h11")
        nc.scalar.activation(window(1), weigh(1, "weighted1"), COPY)
        quantise_quarter(2)
        multiply_late(3, "bank1")
        product(3, "gate0")
        weighted = weigh(2, "weighted2")
        quantise_quarter(3)
        nc.vector.tensor_copy(window(2), weighted)
        y_last = keep.tile([P, NQ], F32, name="y_last", align_bytes=64)
        nc.scalar.copy(y_last[:], down(3)[:])
        nc.vector.tensor_tensor(window(3), y_last[:], gate_of(3), MULT)
        nc.sync.dma_start(out=out, in_=result[:])
